import numpy as np, ml_dtypes
CORES = [242,247,114,119]
N = 4
BF = ml_dtypes.bfloat16
W, VI, CR, S, EV = 1024, 256, 4, 4, 2
V = W - VI
R, NEED, DT, DL = 0.75, 9, 0.0625, 0.1875
def invol(rng, lone):
    o = np.argsort(rng.random((N, 8, CR, W)), axis=-1); x, y = o[..., 0::2], o[..., 1::2]; m = rng.random(x.shape) < lone
    c = np.empty((N, 8, CR, W), np.int64)
    np.put_along_axis(c, x, np.where(m, x, y), -1); np.put_along_axis(c, y, np.where(m, y, x), -1)
    return c
def join(row, x, y):
    p, s = int(row[x]), int(row[y])
    if p == y: return
    row[x] = y; row[y] = x
    if p != x and s != y: row[p] = s; row[s] = p
    elif p != x: row[p] = p
    elif s != y: row[s] = s
def signs(rng, shape): return np.where(rng.random(shape) < 0.5, -1.0, 1.0)
def parts(rng):
    sh = (N, 8, 16, W)
    q = 2.0 * rng.random(sh) - 1.0; v = signs(rng, sh) * (0.5 + 1.5 * rng.random(sh)); k = 0.125 + 0.375 * rng.random(sh)
    a = 2.0 * rng.random((N, 8, W)) - 1.0; con = invol(rng, 0.02)
    u = rng.random((N, 8, W)); far = rng.integers(0, CR, (N, 8, W))
    cur = (rng.integers(0, CR, (N, 8, 1)) + np.where(u < 0.7, 0, np.where(u < 0.8, 1, np.where(u < 0.9, 2, far)))) & (CR - 1)
    return q, v, k, a, con, cur
def small(x, least):
    return np.where(np.abs(x) < least, 0.0, x).astype(np.float32).astype(BF)
def camps(rng, near):
    o = rng.permutation(W); h = W // 2; side = np.empty(W); side[o[:h]] = 1.0; side[o[h:]] = -1.0
    rows = np.empty((CR, W), np.int64)
    for m in range(CR):
        x, y = rng.permutation(o[:h]), rng.permutation(o[h:])
        if near[m]: x, y = np.concatenate([x[0::2], y[0::2]]), np.concatenate([x[1::2], y[1::2]])
        rows[m, x] = y; rows[m, y] = x
    return side, rows
def brink(rng):
    F = np.float32; n = 2 ** 18
    ki = (rng.integers(160, 256, n) * 2.0 ** -9).astype(F); kj = (rng.integers(160, 256, n) * 2.0 ** -9).astype(F)
    vi = (rng.integers(128, 256, n) * 2.0 ** -7).astype(F); vj = (rng.integers(-255, -127, n) * 2.0 ** -21).astype(F)
    dv = vi - vj; kk = ki * kj; p = kk * dv; x = kk.astype(np.float64) * dv.astype(np.float64)
    t = DT * ((vi - p).astype(np.float64) - (vj + p).astype(np.float64))
    hi = small(t, 2.0 ** -20).astype(F); lo = small(t - hi, 2.0 ** -20).astype(F)
    def behind(a, b): return (F(DT) * a - hi) - (lo + F(DT) * b) < 0
    right = behind(vi - p, vj + p)
    wrong = (behind(vi - ki * (kj * dv), vj + kj * (ki * dv)), behind(vi - x, vj + x), behind((vi - x).astype(F), (vj + x).astype(F)))
    best = np.stack([np.argsort(right == w, kind="stable")[:96] for w in wrong])
    return np.stack([-hi, lo, vi, vj, ki, kj])[:, best]
def pack(q, v, k, a, con, cur):
    return {"q0": small(q, 2.0 ** -20).reshape(N, 128, W), "v0": small(v, 2.0 ** -16).reshape(N, 128, W), "kap": k.astype(np.float32).astype(BF).reshape(N, 128, W), "aim": small(a, 2.0 ** -20),
            "con": np.ascontiguousarray(con.reshape(N, 8 * CR, W)).astype(np.int32), "cur": np.ascontiguousarray(cur).astype(np.int32)}
def setup_inputs(rng):
    return pack(*parts(rng))
def setup_inputs_calm(rng):
    q, v, k, a, con, cur = parts(rng); v = v * 0.5
    g = np.arange(8)[None, :, None]; r = np.arange(N)[:, None, None]
    cur = (np.where(r % 2 == 0, g - 2, CR - 3 - g) & (CR - 1)) + np.zeros((N, 8, W), np.int64)
    return pack(q, v, k, a, con, cur)
def setup_inputs_corners(rng):
    q, v, k, a, con, cur = parts(rng); s = int(rng.integers(0, 8)); here = np.arange(W)
    for r in range(N):
        for g in range(8):
            z = (g + 3 * r + s) % 8
            if z == 0: con[r, g] = here
            elif z == 1:
                join(con[r, g, 0], 0, W - 1); con[r, g] = con[r, g, 0].copy(); q[r, g] = q[r, g] * 0.25
            elif z == 2: k[r, g] = np.where(rng.random((16, W)) < 0.5, 0.0625, 0.5)
            elif z == 3: q[r, g] = q[r, g, :, :1].copy()
            elif z == 4:
                side, rows = camps(rng, [m % 2 == 1 for m in range(CR)])
                con[r, g] = rows; q[r, g] = side[None, :] * (0.75 + 0.25 * rng.random((16, W))); cur[r, g] = 2 * int(rng.integers(0, CR // 2))
            elif z == 5:
                for m in range(CR):
                    x, y = 1 + m, W - 2 - m
                    join(con[r, g, m], 0, x); join(con[r, g, m], W - 1, y)
                    q[r, g, :, x] = q[r, g, :, 0]; q[r, g, :, y] = q[r, g, :, W - 1]; cur[r, g, x] = m; cur[r, g, y] = m
            elif z == 6:
                for m in range(CR):
                    o = rng.permutation(V); row = con[r, g, m]; h = (V - VI) // 2
                    row[V:] = o[:VI]; row[o[:VI]] = V + np.arange(VI)
                    x, y = o[VI:VI + h], o[VI + h:]
                    row[x] = y; row[y] = x
            else:
                side, rows = camps(rng, [1 <= m <= CR - 3 for m in range(CR)])
                con[r, g] = rows; q[r, g] = side[None, :] * (0.75 + 0.25 * rng.random((16, W))); cur[r, g] = CR - 1 - rng.integers(0, 2, W)
    return pack(q, v, k, a, con, cur)
def setup_inputs_ends(rng):
    q, v, k, a, con, cur = parts(rng); q = signs(rng, q.shape)
    for r in range(N):
        for g in range(8):
            for m in (0, CR - 1):
                join(con[r, g, m], 0, W - 1); join(con[r, g, m], 1, W - 2)
            e = 1.0 if (r + g) % 2 == 0 else -1.0
            q[r, g, :, W - 1] = e * q[r, g, :, 0]; q[r, g, :, W - 2] = -e * q[r, g, :, 1]
    v = np.where(rng.random(q.shape) < 0.875, -2.0, 2.0) * q
    k = np.where(rng.random(q.shape) < 0.8, 0.5, 0.0625); a = signs(rng, a.shape)
    cur = np.where(rng.random(cur.shape) < 0.75, 0, CR - 1)
    return pack(q, v, k, a, con, cur)
def setup_inputs_spread(rng):
    q, v, k, a, con, cur = parts(rng); sh = (N, 8, 16, W); one = (N, 8, 1, W)
    q = q * np.exp2(-rng.random(one)); v = signs(rng, sh) * (0.5 + 0.5 * rng.random(sh)) * np.exp2(2.0 * rng.random(one) - 1.0)
    k = (0.25 + 0.25 * rng.random(sh)) * np.exp2(-2.0 * rng.random(one)); a = a * np.exp2(-2.0 * rng.random(a.shape))
    cur = np.where(rng.random((N, 8, 1)) < 0.5, rng.integers(0, CR, cur.shape), cur)
    return pack(q, v, k, a, con, cur)
def setup_inputs_ties(rng):
    q, v, k, a, con, cur = parts(rng); edge = brink(rng)
    q = rng.integers(-8, 9, q.shape) * 0.125; v = rng.integers(-1, 2, v.shape) * 2.0; k = np.where(rng.random(k.shape) < 0.9, 0.5, 0.0625); a = rng.integers(-8, 9, a.shape) * 0.125
    for r in range(N):
        for g in range(8):
            b = int(rng.integers(0, CR)); row = con[r, g, b]; x = np.flatnonzero(np.arange(W) < row); x = rng.permutation(x)[:len(x) // 4]; y = row[x]
            n = rng.integers(NEED - 1, NEED + 1, len(x)); low = rng.integers(-8, 2, (16, len(x))); place = np.argsort(rng.random((16, len(x))), axis=0)
            q[r, g][:, x] = low * 0.125; q[r, g][:, y] = (low + np.where(place < n[None, :], 6, 7)) * 0.125; v[r, g][:, y] = v[r, g][:, x]
            cur[r, g] = (cur[r, g] - cur[r, g, 0] + b) & (CR - 1); cur[r, g, x] = b; cur[r, g, y] = b
            o = rng.permutation(V)
            for p in range(4):
                x, y = int(o[2 * p]), int(o[2 * p + 1]); e = signs(rng, 16)
                for m in range(CR): join(con[r, g, m], x, y)
                a[r, g, x] = 0.25; a[r, g, y] = -0.25
                if p < 2: z = edge[:, np.arange(16) % 3, rng.integers(0, 96, 16)].astype(np.float64)
                else:
                    lane = rng.permutation(16); near = lane < 8; one = lane == 8
                    z = np.stack([np.where(near, -0.25, np.where(one, 0.75, -0.875)), np.where(near, 0.25, np.where(one, 2.0 ** -20, 0.875)),
                                  np.where(near, 1.0, 0.0), np.where(near, -1.0, np.where(one, -129.0 * 2.0 ** -23, 0.0)), np.full(16, 0.375), np.full(16, 0.375)])
                q[r, g, :, x] = e * z[0]; q[r, g, :, y] = e * z[1]; v[r, g, :, x] = e * z[2]; v[r, g, :, y] = e * z[3]; k[r, g, :, x] = z[4]; k[r, g, :, y] = z[5]
    return pack(q, v, k, a, con, cur)
def check_ranges(d):
    bad = []
    for n, lo, hi, least in (("q0", -1.0, 1.0, 2.0 ** -20), ("v0", -2.0, 2.0, 2.0 ** -16), ("kap", 0.0625, 0.5, 0.0625), ("aim", -1.0, 1.0, 2.0 ** -20)):
        x = np.asarray(d[n]).astype(np.float64); s = np.abs(x)
        if not np.all((x >= lo) & (x <= hi) & ((s == 0) | (s >= least))): bad.append("range of " + n)
    for n, hi in (("con", W - 1), ("cur", CR - 1)):
        if np.min(d[n]) < 0 or np.max(d[n]) > hi: bad.append("range of " + n)
    if "range of con" not in bad:
        c = np.asarray(d["con"]).astype(np.int64)
        if np.any(np.take_along_axis(c, c, 2) != np.arange(W)): bad.append("a row of con is no involution")
    return bad
def pick(x, j):
    y = np.empty_like(x)
    for r in range(N):
        for g in range(8): y[r, g] = np.take(x[r, g], j[r, g], axis=1)
    return y
def travel(x, d):
    y = x.copy(); H = V + VI // 2
    y[..., V:H] = np.roll(x[..., V:H], (d, d), axis=(0, 1)); y[..., H:] = np.roll(x[..., H:], (d, 4 * d), axis=(0, 1))
    return y
def reference(q0, v0, kap, aim, con, cur):
    F = np.float32; sh = (N, 8, 16, W)
    qs = q0.astype(F).reshape(sh); vs = v0.astype(F).reshape(sh); ks = kap.astype(F).reshape(sh); target = aim.astype(F).reshape(N, 8, 1, W)
    ct = con.astype(np.int64).reshape(N, 8, CR, W); cs = cur.astype(np.int64).reshape(N, 8, W); here = np.arange(W)[None, None, :]
    total = ks.astype(np.float64)
    for shot in range(2):
        q, v, k, c, log = qs, vs, ks, cs, []
        for t in range(1, S + 1):
            j0 = np.take_along_axis(ct, c[:, :, None, :], 2)[:, :, 0]; j1 = np.take_along_axis(ct, ((c + 1) & (CR - 1))[:, :, None, :], 2)[:, :, 0]
            d0 = q - pick(q, j0); d1 = q - pick(q, j1)
            o0 = np.sum(np.abs(d0) <= F(R), axis=2) >= NEED; o1 = np.sum(np.abs(d1) <= F(R), axis=2) >= NEED
            some = o0 | o1; j = np.where(o0, j0, np.where(o1, j1, here)); choice = np.where(some, j, -1)
            mutual = some & (np.take_along_axis(choice, j, 2) == here)
            dq = np.where(o0[:, :, None], d0, d1); dv = v - pick(v, j); kj = pick(k, j)
            hit = mutual[:, :, None] & (dq * dv < F(0))
            kk = np.where(hit, k * kj, F(0)); w = np.where(hit, kj.astype(np.float64) * dv, 0.0); log.append((j, kk, w))
            v = v - kk * dv
            c = np.where(mutual & o0, c + 1, c + 2) & (CR - 1)
            q = q + F(DT) * v
            if t % EV == 0 and t < S: q, v, k = travel(q, 1), travel(v, 1), travel(k, 1)
        aq = q - target; av = np.zeros(sh, F); gain = np.zeros(sh, np.float64)
        for t in range(S, 0, -1):
            if t % EV == 0 and t < S: aq, av, gain = travel(aq, -1), travel(av, -1), travel(gain, -1)
            av = av + F(DT) * aq
            j, kk, w = log[t - 1]; da = av - pick(av, j)
            gain = gain - w * da.astype(np.float64)
            av = av - kk * da
        total = total + gain
        vs = vs - np.clip(av, F(-DL), F(DL))
    return {"yg": total.reshape(N, 128, W).astype(np.float32), "yv": vs.reshape(N, 128, W).astype(np.float32)}

def check_inputs(d):
    bad = list(check_ranges(d))
    if not bad:
        for name, y in reference(**d).items():
            for q in range(N):
                v = np.abs(np.asarray(y[q], np.float64)); s = np.sqrt(np.mean(v * v))
                if v.max() > 14 * s or s < 2.0 ** -4: bad.append('%s of rank %d is uneven or too small' % (name, q))
    return bad

@@ -1,0 +1,621 @@
+from concourse.mybir import AluOpType, ActivationFunctionType
+
+ALU = AluOpType
+ACT = ActivationFunctionType
+W, NV = 1024, 768
+H = ((0, 512), (512, 1024))
+VIS, N1 = (768, 1024), (512, 768)
+ABS_SCALE = 167.0 / 128.0
+NEAR = 250.0 / 256.0
+TIE = 501.0 / 512.0
+CLIP = 0.1875 / 16.0
+UNIT = 1.0 / 1024.0
+
+F, B, HF, I32, U16 = "float32", "bfloat16", "float16", "int32", "uint16"
+
+
+def sb(cols, dt):
+    return ("sbuf", [128, cols], dt)
+
+
+SCRATCH = {
+    "X": ("psum", [128, 1024], F), "TP": ("psum", [128, 1024], F), "QP": ("psum", [128, 1024], F),
+    "C6": ("psum", [128, 512], F), "C7": ("psum", [128, 512], F),
+    "ci": sb(W, I32), "ch": sb(W, HF), "ones": sb(2048, B), "onef": sb(256, F), "bc": sb(720, B), "bn": sb(144, B),
+    "bl": sb(8, B), "wr": sb(2048, B), "wa": sb(128, B), "zb": sb(256, B), "zf": sb(256, F), "iw": sb(64, F),
+    "iw0": sb(64, F), "pi": sb(4, I32), "pj": sb(4, I32), "pf": sb(4, F), "ee": sb(448, F), "cc": sb(256, F),
+    "mm": ("sbuf", [128, 2, 256], F), "ma": ("sbuf", [128, 2, 128], F),
+    "r0": ("sbuf", [128, 4, 64], F), "r1": sb(256, F), "r2": sb(256, F), "r3": sb(128, F),
+    "d0": sb(256, F), "d1": sb(256, F), "d2": sb(128, F),
+    "e0": sb(64, B), "eps": sb(64, B), "ja": sb(128, F), "cw": sb(64, HF),
+    "D": sb(2048, F), "AB": sb(2048, B), "NB": sb(2048, B),
+    "qov": sb(256, F), "ahv": sb(256, F), "gr": sb(256, F), "vo": sb(256, F), "ao": sb(256, F), "gv": sb(512, F),
+    "lk": sb(256, B),
+}
+for _n in "qb qb2 vb kh ka am pa sa kj mu kj1 mu1".split():
+    SCRATCH[_n] = sb(W, B)
+for _n in ("ir R dq1 va vc v0a v0b v2 qa qc q2 dv1 dv2 dv3 dv4 kl1 kl2 kl3 aq A av1 av2 avc da ga gb ge G kn rk ov ou").split():
+    SCRATCH[_n] = sb(W, F)
+for _t in "1234":
+    SCRATCH["s" + _t], SCRATCH["l" + _t], SCRATCH["j" + _t] = sb(64, F), sb(128, U16), sb(128, U16)
+for _s in (0, 1):
+    for _n, _c in (("lq", 256), ("lv", 256), ("la", 256), ("lw", 256), ("lg", 512)):
+        SCRATCH[_n + str(_s)] = sb(_c, F)
+PSUM = ("X", "TP", "QP", "C6", "C7")
+ENG = ("V", "S", "P", "G", "Y")
+NDMA, NREM = 24, 11
+SEMAPHORES = (["e" + e for e in ENG] + ["dm%d" % i for i in range(NDMA)]
+              + ["ls%d" % i for i in range(NREM)] + ["ar%d" % i for i in range(NREM)])
+
+
+def emit(ops, g, T):
+    q = {"V": g.vector, "S": g.scalar, "P": g.tensor, "G": g, "Y": g.sync}
+    hist, banks, clock, deps, order = {}, {}, {e: {} for e in ENG}, [], {e: 0 for e in ENG}
+    know = []
+    for n, o in enumerate(ops):
+        e = o["e"]
+        need = set()
+        touch = [(r, False) for r in o["r"]] + [(r, True) for r in o["w"]]
+        for (name, a, b), wr in touch:
+            for (a2, b2, wr2, m) in hist.get(name, []):
+                if a < b2 and a2 < b and (wr or wr2):
+                    if not (e == "P" and ops[m]["e"] == "P"):
+                        need.add(m)
+            if name in PSUM:
+                for bk in range(a // 512, (b - 1) // 512 + 1):
+                    m = banks.get((name, bk))
+                    if m is not None and ops[m]["e"] != e:
+                        need.add(m)
+        for (name, a, b), wr in touch:
+            h = hist.setdefault(name, [])
+            if wr:
+                h[:] = [x for x in h if not (a <= x[0] and x[1] <= b)]
+            h.append((a, b, wr, n))
+            if name in PSUM:
+                for bk in range(a // 512, (b - 1) // 512 + 1):
+                    banks[(name, bk)] = n
+        need.discard(n)
+        if e is None:
+            deps.append([])
+            know.append({("t", n): 1})
+            continue
+        ck = clock[e]
+        waits = []
+        for m in sorted(need, reverse=True):
+            key, val = (("t", m), 1) if ops[m]["tok"] is not None else (ops[m]["e"], ops[m]["i"])
+            if ck.get(key, 0) >= val:
+                continue
+            waits.append(m)
+            for k2, v2 in know[m].items():
+                if ck.get(k2, 0) < v2:
+                    ck[k2] = v2
+        deps.append(waits)
+        kn = dict(ck)
+        if o["tok"] is None:
+            order[e] += 1
+            o["i"] = order[e]
+            kn[e] = o["i"]
+        else:
+            kn[("t", n)] = 1
+        know.append(kn)
+    wanted = set(m for ws in deps for m in ws)
+    last = {}
+    for n, o in enumerate(ops):
+        if o["tok"] is None:
+            last[o["e"]] = n
+    wanted |= set(last.values())
+    count = {e: 0 for e in ENG}
+    val, waited = {}, set()
+    for n, o in enumerate(ops):
+        if o["tok"] is None and n in wanted:
+            count[o["e"]] += 1
+            val[n] = ("e" + o["e"], count[o["e"]])
+        elif o["tok"] is not None:
+            val[n] = o["tok"]
+    for n, o in enumerate(ops):
+        if o["e"] is None:
+            continue
+        for m in deps[n]:
+            q[o["e"]].wait_ge(T.sem[val[m][0]], val[m][1])
+            waited.add(m)
+        ins = o["f"]()
+        if o["kind"] == "dma":
+            ins.then_inc(T.sem[o["tok"][0]], 16)
+        elif o["kind"] == "op" and n in wanted:
+            ins.then_inc(T.sem[val[n][0]], 1)
+    for n, o in enumerate(ops):
+        if (o["tok"] is not None and n not in waited) or (o["tok"] is None and last[o["e"]] == n):
+            g.sync.wait_ge(T.sem[val[n][0]], val[n][1])
+
+
+def rank_program(g, core, T, topo):
+    rank = T.rank_of(core)
+    if rank is None:
+        return
+    n_ranks = len(T.cores)
+    nxt, prv = T.cores[(rank + 1) % n_ranks], T.cores[(rank - 1) % n_ranks]
+    ops = []
+    cnt = {"dma": 0, "rem": 0}
+    V, S, P = g.vector, g.scalar, g.tensor
+
+    def op(e, f, r, w):
+        ops.append({"e": e, "f": f, "r": r, "w": w, "tok": None, "kind": "op"})
+
+    def dma(e, out, in_, r, w, add=False):
+        qq = {"S": S, "Y": g.sync, "G": g}[e]
+        f = (lambda: qq.dma_start(out, in_, accum_op=ALU.add)) if add else (lambda: qq.dma_start(out, in_))
+        ops.append({"e": e, "f": f, "r": r, "w": w, "tok": ("dm%d" % cnt["dma"], 16), "kind": "dma"})
+        cnt["dma"] += 1
+
+    def send(src, land, forward, after=()):
+        k = cnt["rem"]
+        cnt["rem"] += 1
+        dst, frm = (nxt, prv) if forward else (prv, nxt)
+        rid, pid = topo.addr(dst, core)
+        name, a, b = src
+        ops.append({"e": "G", "kind": "rem", "r": [src] + list(after), "w": [],
+                    "tok": ("ls%d" % k, len(topo.engines(core, dst))),
+                    "f": lambda: g.remote_dma(T[land][:], T[name][:, a:b], T.sem["ar%d" % k], T.sem["ls%d" % k],
+                                              pid, rid, topo.mask(core, dst))})
+        ops.append({"e": None, "kind": "arr", "r": [], "w": [(land, 0, b - a)], "f": None,
+                    "tok": ("ar%d" % k, len(topo.engines(frm, core)))})
+
+    def ap(x):
+        return T[x[0]][:, x[1]:x[2]]
+
+    def at(name, c, off=0):
+        return (name, c[0] + off, c[1] + off)
+
+    def full(name):
+        return (name, 0, W)
+
+    def tt(out, a, b, alu):
+        op("V", lambda: V.tensor_tensor(ap(out), ap(a), ap(b), alu), [a, b], [out])
+
+    def ts(out, a, s1, o1, s2=None, o2=None):
+        if o2 is None:
+            op("V", lambda: V.tensor_scalar(ap(out), ap(a), s1, None, o1), [a], [out])
+        else:
+            op("V", lambda: V.tensor_scalar(ap(out), ap(a), s1, s2, o1, o2), [a], [out])
+
+    def offs(lst, c, off):
+        return (lst, off + c[0] // 16, off + c[1] // 16)
+
+    def gt(out, win, of, b, alu):
+        op("V", lambda: V.tensor_tensor(ap(out), ap(win).indirect(ap(of)), ap(b), alu), [win, of, b], [out])
+
+    def act(out, a, fn=ACT.Copy, scale=1.0, bias=0.0):
+        op("S", lambda: S.activation(ap(out), ap(a), fn, bias=bias, scale=scale), [a], [out])
+
+    def gact(out, win, of):
+        op("S", lambda: S.activation(ap(out), ap(win).indirect(ap(of)), ACT.Copy), [win, of], [out])
+
+    def mm(o_ap, l_ap, r_ap, st, sp, r, w):
+        op("P", lambda: P.matmul(o_ap, l_ap, r_ap, st, sp), r, w)
+
+    def wrap(out, src, first=True):
+        for l in range(16):
+            mm(ap(out), T.bn[:, 15 - l:143 - l], T[src[0]][:, src[1] + l:src[2]:16], first and l == 0, l == 15,
+               [src, ("bn", 0, 144)], [out])
+
+    def ident(out, src, st, sp):
+        mm(ap(out), T.zb[:, 0:128], ap(src), st, sp, [src, ("zb", 0, 256)], [out])
+
+    def turn(land, forward, z="zf", pieces=1):
+        for half, s in ((0, 16 if forward else 112), (1, 64)):
+            for k in range(pieces):
+                src = (land, 256 * k + 128 * half, 256 * k + 128 * half + 128)
+                out = ("C7", 256 + 128 * half, 384 + 128 * half)
+                mm(ap(out), T[z][:, 128 - s:256 - s], ap(src), k == 0, k == pieces - 1, [src, (z, 0, 256)], [out])
+    ROT = ("C7", 256, 512)
+
+    dma("Y", T.ci[0:32, :], T.con[:], [], [("ci", 0, 512)])
+    dma("S", T.ci[32:40, :], T.cur[:], [], [("ci", 512, 1024)])
+    dma("Y", T.qb[:], T.q0[:], [], [full("qb")])
+    dma("S", T.vb[:], T.v0[:], [], [full("vb")])
+    dma("Y", T.qb2[:], T.q0[:], [], [full("qb2")])
+    dma("S", T.kh[:], T.kap[:], [], [full("kh")])
+    dma("Y", T.ka[:, 0:NV], T.kap[:, 0:NV], [], [("ka", 0, NV)])
+    dma("Y", T.am[0:8, :], T.aim[:], [], [full("am")])
+    op("V", lambda: V.memset(T.bc[:], 0.0), [], [("bc", 0, 720)])
+    op("V", lambda: V.memset(T.ones[:, 0:256], 1.0), [], [("ones", 0, 256)])
+    op("V", lambda: V.memset(T.bn[:], 0.0), [], [("bn", 0, 144)])
+    op("V", lambda: V.memset(T.ones[:, 256:2048], 1.0), [], [("ones", 256, 2048)])
+    op("V", lambda: V.memset(T.onef[:], 1.0), [], [("onef", 0, 256)])
+    op("V", lambda: V.memset(T.eps[:], -UNIT), [], [("eps", 0, 64)])
+    ON = [("ones", 0, 256)]
+    op("G", lambda: g.iota(T.pi[:, 0:1], [[0, 1]], 0, 1), [], [("pi", 0, 4)])
+    op("G", lambda: g.affine_select(T.bc[:, 591:720:16], T.ones[:, 0:9], [[-1, 9]], ALU.is_equal, 0.0, -32, 1),
+       ON, [("bc", 576, 720)])
+    op("G", lambda: g.affine_select(T.bc[:, 15:576:16], T.ones[:, 0:36], [[-4, 4], [-16, 9]], ALU.is_equal, 0.0, 0, 4),
+       ON, [("bc", 0, 576)])
+    op("G", lambda: g.affine_select(T.bl[:], T.ones[:, 0:8], [[-16, 8]], ALU.is_ge, 0.0, 0, 1), ON, [("bl", 0, 8)])
+    op("G", lambda: g.iota(T.iw0[:], [[16, 64]], 0, 1, allow_small_or_imprecise_dtypes=True), [], [("iw0", 0, 64)])
+    op("G", lambda: g.affine_select(T.bn[:, 15:143:16], T.bl[:], [[16, 8]], ALU.is_ge, 0.0, 15, -1),
+       [("bl", 0, 8)], [("bn", 0, 144)])
+    op("G", lambda: g.affine_select(T.zb[:], T.ones[:, 0:256], [[0, 2], [-1, 128]], ALU.is_equal, 0.0, 0, 1),
+       ON, [("zb", 0, 256)])
+    op("G", lambda: g.affine_select(T.wr[:], T.ones[:], [[-1, 16], [-16, 8], [0, 16]], ALU.is_equal, 0.0, 0, 1),
+       [("ones", 0, 2048)], [("wr", 0, 2048)])
+    op("G", lambda: g.iota(T.ir[:], [[1, W]], 0, 0, allow_small_or_imprecise_dtypes=True), [], [full("ir")])
+    send(at("kh", VIS), "lk", True)
+    op("G", lambda: g.affine_select(T.zf[:], T.onef[:], [[0, 2], [-1, 128]], ALU.is_equal, 0.0, 0, 1),
+       [("onef", 0, 256)], [("zf", 0, 256)])
+    op("G", lambda: g.affine_select(T.wa[0:8, :], T.ones[0:8, 0:128], [[-1, 8], [0, 16]], ALU.is_equal, 0.0, 0, 1),
+       ON, [("wa", 0, 128)])
+    op("V", lambda: V.tensor_scalar(T.pj[:, 0:1], T.pi[:, 0:1], 112, None, ALU.bitwise_and), [("pi", 0, 4)], [("pj", 0, 4)])
+    op("V", lambda: V.tensor_copy(T.ch[0:40, :], T.ci[0:40, :]), [full("ci")], [full("ch")])
+    op("V", lambda: V.tensor_copy(T.pf[:, 0:1], T.pj[:, 0:1]), [("pj", 0, 4)], [("pf", 0, 4)])
+    for m in (4, 0, 1, 2, 3):
+        out = ("C7", 0, 64) if m == 4 else ("C6", 64 * m, 64 * m + 64)
+        for l in range(16):
+            mm(ap(out), T.bc[0:40, 144 * m + 15 - l:144 * m + 143 - l], T.ch[0:40, l:W:16], l == 0, l == 15,
+               [full("ch"), ("bc", 0, 720)], [out])
+    op("V", lambda: V.tensor_scalar(T.iw[:], T.iw0[:], T.pf[:, 0:1], UNIT, ALU.subtract, ALU.mult),
+       [("iw0", 0, 64), ("pf", 0, 4)], [("iw", 0, 64)])
+    for k, m in enumerate((1, 2, 3, 0, 1, 2, 3)):
+        ts(("ee", 64 * k, 64 * k + 64), ("C7", 0, 64), float(m), ALU.is_equal, UNIT, ALU.mult)
+    for h in (1, 0):
+        act(at("v0a", H[h]), at("vb", H[h]), scale=0.0625)
+        act(at("v2", H[h]), at("vb", H[h]), scale=0.0625)
+
+    def by_cursor(k0):
+        src = "cc" if k0 else "C6"
+        for k in (0, 1):
+            o = 64 * (3 - k0 - k)
+            op("V", lambda k=k, o=o: V.tensor_tensor(T.mm[:, k, :], T[src][:, 0:256], T.ee[:, o:o + 256], ALU.mult),
+               [(src, 0, 256), ("ee", o, o + 256)], [("mm", k, k + 1)])
+        op("V", lambda: V.tensor_tensor(T.ma[:], T.mm[:, :, 0:128], T.mm[:, :, 128:256], ALU.add), [("mm", 0, 2)], [("ma", 0, 2)])
+        op("V", lambda: V.tensor_tensor(T.r0[:, k0:k0 + 2, :], T.ma[:, :, 0:64], T.ma[:, :, 64:128], ALU.add),
+           [("ma", 0, 2)], [("r0", 64 * k0, 64 * k0 + 128)])
+    by_cursor(0)
+    op("V", lambda: V.tensor_scalar(T.l1[:], T.r0[:, 0:2, :], 1024.0, None, ALU.mult), [("r0", 0, 128)], [("l1", 0, 128)])
+    act(("cc", 0, 256), ("C6", 0, 256))
+
+    def rr(name, a, n):
+        return T.r0[:, a:a + n, :] if name == "r0" else T[name][:, 64 * a:64 * (a + n)]
+
+    def rsub(out, name, a, b, n):
+        op("V", lambda: V.tensor_tensor(ap(out), rr(name, a, n), rr(name, b, n), ALU.subtract), [(name, 0, 256)], [out])
+
+    def radd(out, name, a, n, m):
+        op("V", lambda: V.tensor_tensor(ap(out), rr(name, a, n), ap(m), ALU.add), [(name, 64 * a, 64 * (a + n)), m], [out])
+
+    FL, MT = ("C7", 192, 256), 64
+    F0, TJ = ("C6", 128, 192), ("C6", 192, 256)
+    stacks = {1: "r0", 2: "r1", 3: "r2", 4: "r3"}
+    dels = {1: "d0", 2: "d1", 3: "d2"}
+
+    def deltas(name, d, s, four):
+        rsub((s, 0, 64), name, 1, 0, 1)
+        if d:
+            rsub((d, 0, 128), name, 1, 2, 2)
+        if four:
+            rsub((d, 128, 192), name, 3, 0, 1)
+            rsub((d, 192, 256), name, 0, 1, 1)
+
+    def advance(name, d, new, k0):
+        for k in (0, 1):
+            tt(("C7", MT + 64 * k, MT + 64 * k + 64), FL, (d, 64 * (k0 + k), 64 * (k0 + k) + 64), ALU.mult)
+        yield
+        radd((new, 64 * k0, 64 * k0 + 128), name, (k0 + 2) % 4, 2, ("C7", MT, MT + 128))
+        yield
+
+    def decide(t, q, filler, busy):
+        lst, st = "l%d" % t, stacks[t]
+        hs = (0, 1) if t == 3 else (1, 0)
+        for w in (0, 1):
+            for h in hs:
+                c = H[h]
+                gt(at("D", c, 1024 * w), full(q), offs(lst, c, 64 * w), at("qb2" if t == 1 else "q2", c), ALU.subtract)
+                act(at("AB", c, 1024 * w), at("D", c, 1024 * w), ACT.Abs, scale=ABS_SCALE)
+                if w == 0:
+                    act(at("NB", c), at("AB", c), ACT.Sign, scale=-1.0, bias=TIE)
+            if w == 0:
+                wrap(("C6", 0, 64), ("NB", 0, 1024))
+        if busy:
+            act(at("NB", H[hs[0]], 1024), at("AB", H[hs[0]], 1024), ACT.Sign, scale=-1.0, bias=TIE)
+        for h in (1, 0):
+            act(at("QP", H[h]), at(q, H[h]))
+        filler()
+        if not busy:
+            ts(at("NB", H[hs[0]], 1024), at("AB", H[hs[0]], 1024), NEAR, ALU.is_le, 0.5, ALU.subtract)
+        ts(F0, ("C6", 0, 64), 0.25, ALU.is_lt)
+        ts(("e0", 0, 64), ("C6", 0, 64), 0.25, ALU.is_ge, 32.0, ALU.mult)
+        tt(TJ, F0, ("s%d" % t, 0, 64), ALU.mult)
+        tt(("ja", 64, 128), F0, ("iw", 0, 64), ALU.add)
+        ts(at("NB", H[hs[1]], 1024), at("AB", H[hs[1]], 1024), NEAR, ALU.is_le, 0.5, ALU.subtract)
+        radd(("ja", 0, 64), st, 0, 1, TJ)
+        ts(("j%d" % t, 0, 128), ("ja", 0, 128), 1024.0, ALU.mult)
+        ident(("C7", 0, 64), ("eps", 0, 64), True, False)
+        ident(("C7", 0, 64), ("e0", 0, 64), False, False)
+        wrap(("C7", 0, 64), ("NB", 1024, 2048), False)
+
+    def choices():
+        tt(("cw", 0, 64), ("C7", 0, 64), ("ja", 0, 64), ALU.min)
+        for h in (1, 0):
+            a, b = H[h]
+            for l in range(16):
+                mm(T.X[:, a + l:b:16], T.wr[:, 128 * l:128 * l + 128], T.cw[:, a // 16:b // 16], True, True,
+                   [("cw", 0, 64), ("wr", 0, 2048)], [("X", a, b)])
+            act(at("R", H[h]), at("X", H[h]), scale=1024.0)
+
+    def half6(h):
+        return ("C6" if h == 0 else "C7", 0, 512)
+
+    def forward(shot, t, q, v, qn, vn, filler, filler2):
+        again = shot == 1 and t == 1
+        jl, dv = "j%d" % t, "dq1" if again else "dv%d" % t
+        k = "kh" if t <= 2 else "ka"
+        kj, mu = ("kj1", "mu1") if t == 1 else ("kj", "mu")
+        if not again:
+            decide(t, q, filler, t == 3 if shot else t < 3)
+        if t == 2:
+            send(at(q, VIS), "lq%d" % shot, True)
+
+        def g_dv(h):
+            gt(at(dv, H[h]), full(v), offs(jl, H[h], 0), at("v2", H[h]), ALU.subtract)
+
+        def g_a(h):
+            if again:
+                tt(at("pa", H[h]), half6(h), at(dv, H[h]), ALU.mult)
+            else:
+                gt(at("pa", H[h]), ("D", 0, 2048), offs(jl, H[h], 64), at(dv, H[h]), ALU.mult)
+            act(at("sa", H[h]), at("pa", H[h]), ACT.Sign, scale=-1.0)
+
+        def g_mu(c):
+            gt(at(mu, c), full("R"), offs(jl, c, 0), at("ir", c), ALU.is_equal)
+
+        def xx(c):
+            return ("C6", 256, 512) if c == VIS else at("X", c)
+
+        def mask(c):
+            ident(xx(c), at(kj, c), True, False)
+            ident(xx(c), at("sa", c), False, False)
+            ident(xx(c), at(mu, c), False, True)
+            act(xx(c), xx(c), ACT.Relu, bias=-2.0)
+
+        def kk(c):
+            tt(xx(c), xx(c), at(k, c), ALU.mult)
+
+        def tp(c):
+            tt(at("TP", c), xx(c), at(dv, c), ALU.mult)
+
+        def vv(c, out=None):
+            tt(out or at(vn, c), at("TP", c), at(v, c), ALU.add)
+
+        def v2(c):
+            if t < 4:
+                act(at("v2", c), at(vn, c))
+
+        def qq(c):
+            tt(at(qn, c), at("QP", c), at(vn, c), ALU.add)
+            if t < 4:
+                act(at("q2", c), at(qn, c))
+
+        if again:
+            act(full("ga"), full("ga"), scale=-1.0)
+            add_g("ga", (0, W))
+            g_dv(1); g_dv(0); g_a(1); g_a(0); mask(H[1]); mask(H[0])
+            filler()
+        elif t == 2:
+            gact(at(kj, H[1]), full(k), offs(jl, H[1], 0))
+            g_dv(1); choices(); g_a(1); g_dv(0)
+            g_mu(VIS); mask(VIS); g_mu(N1); mask(N1)
+            gact(at(kj, H[0]), full(k), offs(jl, H[0], 0))
+            g_a(0); kk(VIS); g_mu((0, 256)); tp(VIS); g_mu((256, 512)); vv(VIS, ("vo", 0, 256))
+            send(("vo", 0, 256), "lv%d" % shot, True)
+            mask(H[0])
+        else:
+            for h in (1, 0):
+                gact(at(kj, H[h]), full(k), offs(jl, H[h], 0))
+            g_dv(1); choices(); g_dv(0); g_a(1); g_a(0); g_mu(H[1]); mask(H[1]); g_mu(H[0]); mask(H[0])
+            if shot == 0 and t == 4:
+                act(full("kn"), full("kn"), ACT.Exp, scale=-1.0)
+            if t == 1:
+                for h in (1, 0):
+                    gact(at("dq1", H[h]), ("D", 0, 2048), offs("j1", H[h], 64))
+        step_on = t < 4 and not again
+        if step_on:
+            ident(("C7", 0, 64), ("e0", 0, 64), True, False)
+            wrap(("C7", 0, 64), full(mu), False)
+        if t == 4:
+            for h in (1, 0):
+                mm(ap(half6(h)), T.wa[0:8, :], T.am[0:8, H[h][0]:H[h][1]], True, True, [("wa", 0, 128), full("am")], [half6(h)])
+
+        def small():
+            if step_on:
+                ts(FL, ("C7", 0, 64), 40.0, ALU.is_gt)
+                yield
+                for _ in advance(stacks[t], dels[t], stacks[t + 1], 0):
+                    yield
+                ts(("l%d" % (t + 1), 0, 128), (stacks[t + 1], 0, 128), 1024.0, ALU.mult)
+            yield
+        sm = small()
+
+        def logk(h):
+            if t < 4:
+                act(at("kl%d" % t, H[h]), at("X", H[h]))
+            else:
+                act(at("X", H[h]), at("X", H[h]), scale=1.0 / 256.0)
+        if t == 2:
+            act(at("kl2", VIS), xx(VIS))
+            kk(N1); tp(N1); kk(H[0])
+            act(at("kl2", N1), at("X", N1))
+            vv(N1); v2(N1); tp(H[0])
+            if shot:
+                act(at("X", H[1]), at("kn", H[1]), ACT.Square, scale=16.0)
+            next(sm, 0); qq(N1); logk(0); vv(H[0]); next(sm, 0)
+            if shot:
+                act(at("X", H[0]), at("kn", H[0]), ACT.Square, scale=16.0)
+            qq(H[0]); next(sm, 0)
+            turn("lq%d" % shot, True)
+            act(("qov", 0, 256), ROT)
+            v2(H[0])
+            next(sm, 0)
+            filler2()
+            turn("lv%d" % shot, True)
+            tt(at(qn, VIS), ROT, ("qov", 0, 256), ALU.add)
+            act(at("q2", VIS), at(qn, VIS))
+            act(at(vn, VIS), ROT)
+            act(at("v2", VIS), ROT)
+        else:
+            a, b = 1, 0
+            kk(H[a]); tp(H[a]); kk(H[b]); logk(a); vv(H[a]); v2(H[a]); tp(H[b]); next(sm, 0); logk(b); qq(H[a]); next(sm, 0)
+            vv(H[b]); next(sm, 0); v2(H[b])
+            if t == 4:
+                tt(at("aq", H[1]), at(qn, H[1]), half6(1), ALU.subtract)
+                act(at("avc", H[1]), at("aq", H[1]))
+            qq(H[b]); next(sm, 0)
+            if t == 4:
+                tt(at("aq", H[0]), at(qn, H[0]), half6(0), ALU.subtract)
+                act(half6(0), at("aq", H[0]))
+            filler2()
+
+    def rest_of(t, four):
+        def f():
+            if t < 4:
+                for _ in advance(stacks[t - 1], dels[t - 1], stacks[t], 2):
+                    pass
+            deltas(stacks[t], dels.get(t), "s%d" % t, four)
+        return f
+
+    def nothing():
+        pass
+
+    def bank(t):
+        return "X" if t % 2 == 0 else "TP"
+
+    def gain(t, out, c, off=0):
+        tt(at(out, c, off), at(bank(t), c), at("dv%d" % t, c), ALU.mult)
+
+    def add_g(src, c, off=0):
+        dma("G", ap(at("G", c)), ap(at(src, c, off)), [at(src, c, off), at("G", c)], [at("G", c)], add=True)
+
+    def backward(shot, v0, v0n):
+        def load(t, hs=(1, 0)):
+            for h in hs:
+                act(at(bank(t), H[h]), at("kl%d" % t, H[h]))
+
+        def da(t, src, c):
+            gt(at("da", c), full(src), offs("j%d" % t, c, 0), at("avc", c), ALU.subtract)
+
+        def tb(t, c):
+            tt(at(bank(t), c), at(bank(t), c), at("da", c), ALU.mult)
+
+        def av(t, src, c, out=None):
+            tt(out or at("av2", c), at(bank(t), c), at(src, c), ALU.add)
+
+        def twin(c, h):
+            act(at("avc", c) if h is None else at("C6", c, -H[h][0]), at("av1", c))
+
+        def drift(c, h=None):
+            tt(at("av1", c), at("QP", c), at("av2", c), ALU.add)
+            twin(c, h)
+
+        def fetch(t, src, h):
+            gact(at("da", H[h]), full(src), offs("j%d" % t, H[h], 0))
+
+        def less(h):
+            tt(at("da", H[h]), at("da", H[h]), ("C6", 0, 512), ALU.subtract)
+        fetch(4, "aq", 0)
+        for h in (1, 0):
+            act(at("A", H[h]), at("aq", H[h]), scale=1.0 / 256.0)
+            act(at("QP", H[h]), at("aq", H[h]), scale=1.0 / 256.0)
+            if h:
+                send(at("A", VIS), "la%d" % shot, False)
+        da(4, "aq", H[1]); tb(4, H[1]); less(0); av(4, "A", H[1]); tb(4, H[0]); drift(H[1]); av(4, "A", H[0])
+        load(3, (1,))
+        gain(4, "gv", VIS, -768)
+        drift(H[0], 0)
+        fetch(3, "av1", 0)
+        load(3, (0,))
+        da(3, "av1", VIS); da(3, "av1", N1); tb(3, VIS); tb(3, N1); av(3, "av1", VIS, ("ao", 0, 256))
+        send(("ao", 0, 256), "lw%d" % shot, False)
+        turn("la%d" % shot, False)
+        act(("ahv", 0, 256), ROT)
+        less(0); av(3, "av1", N1); tb(3, H[0])
+        ga = "ga" if shot else "G"
+        gain(4, ga, N1); av(3, "av1", H[0]); drift(N1, 1); gain(4, ga, H[0])
+        if shot:
+            add_g("ga", (0, NV))
+        drift(H[0])
+        act(at("QP", VIS), ("ahv", 0, 256))
+        load(2)
+        if shot == 0:
+            act(at("rk", H[0]), at("kn", H[0]), scale=-512.0)
+        gain(3, "gv", VIS, -512)
+        send(("gv", 0, 512), "lg%d" % shot, False)
+        gain(3, "gb", N1); gain(3, "gb", H[0])
+        add_g("gb", (0, NV))
+        turn("lw%d" % shot, False)
+        tt(at("av1", VIS), ROT, ("ahv", 0, 256), ALU.add)
+        twin(VIS, 1)
+        fetch(2, "av1", 1)
+        load(1)
+        if shot == 0:
+            act(at("rk", H[1]), at("kn", H[1]), scale=-512.0)
+        da(2, "av1", H[0]); tb(2, H[0]); less(1); av(2, "av1", H[0]); tb(2, H[1]); drift(H[0]); av(2, "av1", H[1])
+        gain(2, "ge", H[0]); drift(H[1], 1)
+        add_g("ge", H[0])
+        fetch(1, "av1", 1)
+        da(1, "av1", H[0]); gain(2, "ge", H[1]); tb(1, H[0]); less(1)
+        turn("lg%d" % shot, False, pieces=2)
+        act(("gr", 0, 256) if shot else at("G", VIS), ROT)
+        add_g("ge", H[1])
+        if shot == 0:
+            act(half6(0), at("dq1", H[0]))
+            act(half6(1), at("dq1", H[1]))
+            for h in (0, 1):
+                act(at("QP", H[h]), at("qb", H[h]))
+            act(full("ga"), full("kh"), ACT.Square, scale=0.0625)
+        av(1, "av1", H[0]); tb(1, H[1])
+        ts(at("X", H[0]), at("av2", H[0]), CLIP, ALU.min, -CLIP, ALU.max)
+        av(1, "av1", H[1])
+        ts(at("X", H[1]), at("av2", H[1]), CLIP, ALU.min, -CLIP, ALU.max)
+        for h in (0, 1) if shot else (1, 0):
+            tt(at(v0n, H[h]), at(v0, H[h]), at("X", H[h]), ALU.subtract)
+            if shot == 0:
+                act(at("v2", H[h]), at(v0n, H[h]))
+
+    def first_extras():
+        turn("lk", True, z="zb")
+        act(at("ka", VIS), ROT)
+
+    def late_gain():
+        gain(1, "gb", H[1]); gain(1, "gb", H[0])
+        add_g("gb", (0, W))
+
+    def first_rest():
+        by_cursor(2)
+        deltas("r0", "d0", "s1", True)
+
+    def newton():
+        for h in (1, 0):
+            tt(at("ou", H[h]), at("X", H[h]), at("kh", H[h]), ALU.mult)
+        dma("G", T.rk[:], T.ou[:], [full("ou"), full("rk")], [full("rk")], add=True)
+
+    act(full("kn"), full("kh"), ACT.Ln)
+    for shot in (0, 1):
+        v0 = "v0a" if shot == 0 else "v0b"
+        if shot == 0:
+            forward(0, 1, "qb", v0, "qa", "va", first_rest, first_extras)
+            forward(0, 2, "qa", "va", "qc", "vc", rest_of(2, True), rest_of(3, False))
+        else:
+            forward(1, 1, "qb", v0, "qa", "va", late_gain, nothing)
+            forward(1, 2, "qa", "va", "qc", "vc", nothing, newton)
+        forward(shot, 3, "qc", "vc", "qa", "va", rest_of(3, False) if shot else nothing, nothing)
+        forward(shot, 4, "qa", "va", "qc", "vc", rest_of(4, False), nothing)
+        backward(shot, v0, "v0b" if shot == 0 else "va")
+    for h in (0, 1):
+        act(at("ov", H[h]), at("va", H[h]), scale=16.0)
+        dma("Y", T.yv[:, H[h][0]:H[h][1]], ap(at("ov", H[h])), [at("ov", H[h])], [])
+    for h in (1, 0):
+        tt(at("QP", H[h]), at("TP", H[h]), at("dq1", H[h]), ALU.mult)
+    tt(at("QP", VIS), at("QP", VIS), ("gr", 0, 256), ALU.add)
+    for h in (0, 1):
+        tt(at("QP", H[h]), at("QP", H[h]), at("G", H[h]), ALU.add)
+    for n, c in enumerate((H[0], N1, VIS)):
+        tt(at("ou", c), at("QP", c), at("rk", c), ALU.mult)
+        dma("S" if n == 1 else "Y", T.yg[:, c[0]:c[1]], ap(at("ou", c)), [at("ou", c)], [])
+    emit(ops, g, T)

@@ -3,13 +3,17 @@ from concourse.mybir import AluOpType, ActivationFunctionType
 ALU = AluOpType
 ACT = ActivationFunctionType
 W, NV = 1024, 768
-H = ((0, 512), (512, 1024))
-VIS, N1 = (768, 1024), (512, 768)
+H1, H0 = (512, 1024), (0, 512)
+VIS, N1, NAT, ALL = (768, 1024), (512, 768), (0, 768), (0, 1024)
 ABS_SCALE = 167.0 / 128.0
 NEAR = 250.0 / 256.0
 TIE = 501.0 / 512.0
-CLIP = 0.1875 / 16.0
-UNIT = 1.0 / 1024.0
+CLIP = 0.1875 * 16.0
+UNITS = (1.0 / 256.0, 1.0 / 16.0)
+
+Q1, Q0 = (256, 512), (0, 256)
+SPLIT0, SPLIT1, NEAR0, NEAR1, R_COPY, SIGN_B = True, True, "VVV", "SVV", "S", "S"
+PE_BACK = {}
 
 F, B, HF, I32, U16 = "float32", "bfloat16", "float16", "int32", "uint16"
 
@@ -19,33 +23,126 @@ def sb(cols, dt):
 
 
 SCRATCH = {
-    "X": ("psum", [128, 1024], F), "TP": ("psum", [128, 1024], F), "QP": ("psum", [128, 1024], F),
+    "PA": ("psum", [128, 1024], F), "PB": ("psum", [128, 1024], F), "PY": ("psum", [128, 1024], F),
     "C6": ("psum", [128, 512], F), "C7": ("psum", [128, 512], F),
-    "ci": sb(W, I32), "ch": sb(W, HF), "ones": sb(2048, B), "onef": sb(256, F), "bc": sb(720, B), "bn": sb(144, B),
-    "bl": sb(8, B), "wr": sb(2048, B), "wa": sb(128, B), "zb": sb(256, B), "zf": sb(256, F), "iw": sb(64, F),
-    "iw0": sb(64, F), "pi": sb(4, I32), "pj": sb(4, I32), "pf": sb(4, F), "ee": sb(448, F), "cc": sb(256, F),
-    "mm": ("sbuf", [128, 2, 256], F), "ma": ("sbuf", [128, 2, 128], F),
-    "r0": ("sbuf", [128, 4, 64], F), "r1": sb(256, F), "r2": sb(256, F), "r3": sb(128, F),
-    "d0": sb(256, F), "d1": sb(256, F), "d2": sb(128, F),
-    "e0": sb(64, B), "eps": sb(64, B), "ja": sb(128, F), "cw": sb(64, HF),
+    "ci": sb(W, I32), "ch": sb(W, HF), "ones": sb(2048, B), "big": sb(16, B), "cz": sb(768, B), "zz": sb(768, B),
+    "cf": sb(512, F), "zf": sb(512, F), "bc": sb(720, B), "bn": sb(144, B), "bl": sb(8, B), "wr": sb(2048, B),
+    "wa": sb(128, B), "iw": sb(64, HF), "iw0": sb(64, F), "pi": sb(4, I32), "pj": sb(4, I32), "pf": sb(4, F),
+    "top": sb(64, B), "ee": sb(448, B), "cc": sb(256, HF), "uu": sb(512, HF),
+    "mm": ("sbuf", [128, 2, 256], F), "ma": ("sbuf", [128, 2, 128], F), "r0": ("sbuf", [128, 2, 64], F),
+    "f0": sb(64, B), "fl": sb(64, B), "jf": sb(64, F), "cw": sb(64, HF),
     "D": sb(2048, F), "AB": sb(2048, B), "NB": sb(2048, B),
-    "qov": sb(256, F), "ahv": sb(256, F), "gr": sb(256, F), "vo": sb(256, F), "ao": sb(256, F), "gv": sb(512, F),
-    "lk": sb(256, B),
+    "qov": sb(256, F), "gr": sb(256, F), "vo": sb(256, F), "ao": sb(256, F), "gg": sb(2048, F), "lk": sb(256, B),
 }
-for _n in "qb qb2 vb kh ka am pa sa kj mu kj1 mu1".split():
+for _n in "qb qb2 vb vb2 kh ka am pa sa kj kj1 mu mu1 sq1".split():
     SCRATCH[_n] = sb(W, B)
-for _n in ("ir R dq1 va vc v0a v0b v2 qa qc q2 dv1 dv2 dv3 dv4 kl1 kl2 kl3 aq A av1 av2 avc da ga gb ge G kn rk ov ou").split():
+for _n in "ir R q q2 v v2 vs dv A av1 av2 ag tb cl gb ge G kn rk ov ou".split():
     SCRATCH[_n] = sb(W, F)
 for _t in "1234":
-    SCRATCH["s" + _t], SCRATCH["l" + _t], SCRATCH["j" + _t] = sb(64, F), sb(128, U16), sb(128, U16)
+    SCRATCH["st" + _t], SCRATCH["l" + _t], SCRATCH["j" + _t] = sb(256, HF), sb(128, U16), sb(128, U16)
+    SCRATCH["kl" + _t], SCRATCH["tp" + _t] = sb(W, F), sb(W, F)
 for _s in (0, 1):
     for _n, _c in (("lq", 256), ("lv", 256), ("la", 256), ("lw", 256), ("lg", 512)):
         SCRATCH[_n + str(_s)] = sb(_c, F)
-PSUM = ("X", "TP", "QP", "C6", "C7")
+PSUM = ("PA", "PB", "PY", "C6", "C7")
 ENG = ("V", "S", "P", "G", "Y")
 NDMA, NREM = 24, 11
 SEMAPHORES = (["e" + e for e in ENG] + ["dm%d" % i for i in range(NDMA)]
               + ["ls%d" % i for i in range(NREM)] + ["ar%d" % i for i in range(NREM)])
+
+CYCLE, PE_CYCLE, HOP, SAME = 0.83, 0.45, 250.0, 250.0
+GATHER = 1.45
+ROUNDS = 2
+RERUNS = 2
+LOOK = 0.25
+
+
+def banks_of(o):
+    return set((name, bk) for name, a, b in o["r"] + o["w"] if name in PSUM for bk in range(a // 512, (b - 1) // 512 + 1))
+
+
+def arrange(ops):
+    n = len(ops)
+    hist, pred, succ = {}, [set() for _ in ops], [[] for _ in ops]
+    for i, o in enumerate(ops):
+        touch = [(r, False) for r in o["r"]] + [(r, True) for r in o["w"]]
+        for (name, a, b), wr in touch:
+            pred[i].update(m for a2, b2, wr2, m in hist.get(name, []) if a < b2 and a2 < b and (wr or wr2))
+        for (name, a, b), wr in touch:
+            h = hist.setdefault(name, [])
+            if wr:
+                h[:] = [x for x in h if not (a <= x[0] and x[1] <= b)]
+            h.append((a, b, wr, i))
+        if o["kind"] == "arr":
+            pred[i].add(i - 1)
+        pred[i].discard(i)
+        for m in pred[i]:
+            succ[m].append(i)
+
+    def hop(m, i):
+        return 0.0 if ops[m]["e"] == ops[i]["e"] == "P" else SAME if ops[m]["e"] == ops[i]["e"] else HOP
+    uses = [[(o["e"], None)] + [(bk, o["e"]) for bk in sorted(banks_of(o))] if o["e"] else [] for o in ops]
+
+    def place(rank, back):
+        before, after = (succ, pred) if back else (pred, succ)
+        ready = [o["lat"] if back else 0.0 for o in ops]
+        held, start, left = {}, [0.0] * n, [len(p) for p in before]
+        free = [i for i in range(n) if not left[i]]
+        while free:
+            i = min(free, key=lambda k: rank[k])
+            free.remove(i)
+            s, c, moved = ready[i], ops[i]["c"], True
+            while moved:
+                moved = False
+                for key, who in uses[i]:
+                    pad = 0.0 if who is None else HOP
+                    for a, b, w in held.get(key, []):
+                        if s < b + pad and a < s + c + pad and (who is None or w != who):
+                            s, moved = b + pad, True
+            start[i] = s
+            for key, who in uses[i]:
+                held.setdefault(key, []).append((s, s + c, who))
+            for k in after[i]:
+                ready[k] = max(ready[k], s + c + (ops[k]["lat"] + hop(k, i) if back else ops[i]["lat"] + hop(i, k)))
+                left[k] -= 1
+                if left[k] == 0:
+                    free.append(k)
+        return start, max(start[i] + ops[i]["c"] + (0.0 if back else ops[i]["lat"]) for i in range(n))
+    def run(rank):
+        ready, start, left, until = [0.0] * n, [0.0] * n, [len(p) for p in pred], {}
+        free = [i for i in range(n) if not left[i]]
+        while free:
+            soon = {}
+            for i in free:
+                s = ready[i]
+                for key, who in uses[i]:
+                    end, w = until.get(key, (0.0, who))
+                    s = max(s, end + (0.0 if w == who else HOP))
+                soon[i] = s
+            i = min(free, key=lambda k: (soon[k], rank[k]))
+            i = min((k for k in free if ops[k]["e"] == ops[i]["e"] and soon[k] <= soon[i] + LOOK * ops[i]["c"]), key=lambda k: rank[k])
+            free.remove(i)
+            start[i] = soon[i]
+            for key, who in uses[i]:
+                until[key] = (start[i] + ops[i]["c"], who)
+            for k in succ[i]:
+                ready[k] = max(ready[k], start[i] + ops[i]["c"] + ops[i]["lat"] + hop(i, k))
+                left[k] -= 1
+                if left[k] == 0:
+                    free.append(k)
+        return start, max(start[i] + ops[i]["c"] + ops[i]["lat"] for i in range(n))
+    start, span = run(list(range(n)))
+    best = (span, start)
+    for _ in range(RERUNS):
+        late, _span = place([(-start[i] - ops[i]["c"], -i) for i in range(n)], True)
+        start, span = run([(-late[i] - ops[i]["c"], i) for i in range(n)])
+        best = min(best, (span, start))
+    start = best[1]
+    for _ in range(ROUNDS):
+        late, _span = place([(-start[i] - ops[i]["c"], -i) for i in range(n)], True)
+        start, span = place([(-late[i] - ops[i]["c"], i) for i in range(n)], False)
+        best = min(best, (span, start))
+    return sorted(range(n), key=lambda i: (best[1][i], i))
 
 
 def emit(ops, g, T):
@@ -61,19 +158,16 @@ def emit(ops, g, T):
                 if a < b2 and a2 < b and (wr or wr2):
                     if not (e == "P" and ops[m]["e"] == "P"):
                         need.add(m)
-            if name in PSUM:
-                for bk in range(a // 512, (b - 1) // 512 + 1):
-                    m = banks.get((name, bk))
-                    if m is not None and ops[m]["e"] != e:
-                        need.add(m)
+        for bk in banks_of(o):
+            m = banks.get(bk)
+            if m is not None and ops[m]["e"] != e:
+                need.add(m)
+            banks[bk] = n
         for (name, a, b), wr in touch:
             h = hist.setdefault(name, [])
             if wr:
                 h[:] = [x for x in h if not (a <= x[0] and x[1] <= b)]
             h.append((a, b, wr, n))
-            if name in PSUM:
-                for bk in range(a // 512, (b - 1) // 512 + 1):
-                    banks[(name, bk)] = n
         need.discard(n)
         if e is None:
             deps.append([])
@@ -128,6 +222,9 @@ def emit(ops, g, T):
             g.sync.wait_ge(T.sem[val[n][0]], val[n][1])
 
 
+ORDER = []
+
+
 def rank_program(g, core, T, topo):
     rank = T.rank_of(core)
     if rank is None:
@@ -138,26 +235,29 @@ def rank_program(g, core, T, topo):
     cnt = {"dma": 0, "rem": 0}
     V, S, P = g.vector, g.scalar, g.tensor
 
-    def op(e, f, r, w):
-        ops.append({"e": e, "f": f, "r": r, "w": w, "tok": None, "kind": "op"})
+    def op(e, f, r, w, cycles):
+        fixed = {"V": 5.0, "S": 40.0, "G": 170.0, "P": 0.0}[e]
+        c = cycles * PE_CYCLE if e == "P" else fixed + max(cycles, 64) * CYCLE
+        ops.append({"e": e, "f": f, "r": r, "w": w, "tok": None, "kind": "op", "c": c, "lat": 0.0})
 
-    def dma(e, out, in_, r, w, add=False):
+    def dma(e, out, in_, r, w, add=False, lat=2500.0):
         qq = {"S": S, "Y": g.sync, "G": g}[e]
         f = (lambda: qq.dma_start(out, in_, accum_op=ALU.add)) if add else (lambda: qq.dma_start(out, in_))
-        ops.append({"e": e, "f": f, "r": r, "w": w, "tok": ("dm%d" % cnt["dma"], 16), "kind": "dma"})
+        ops.append({"e": e, "f": f, "r": r, "w": w, "tok": ("dm%d" % cnt["dma"], 16), "kind": "dma",
+                    "c": 1000.0 if e == "G" else 60.0, "lat": lat})
         cnt["dma"] += 1
 
-    def send(src, land, forward, after=()):
+    def send(src, land, forward):
         k = cnt["rem"]
         cnt["rem"] += 1
         dst, frm = (nxt, prv) if forward else (prv, nxt)
         rid, pid = topo.addr(dst, core)
         name, a, b = src
-        ops.append({"e": "G", "kind": "rem", "r": [src] + list(after), "w": [],
+        ops.append({"e": "G", "kind": "rem", "r": [src], "w": [], "c": 700.0, "lat": 3500.0,
                     "tok": ("ls%d" % k, len(topo.engines(core, dst))),
                     "f": lambda: g.remote_dma(T[land][:], T[name][:, a:b], T.sem["ar%d" % k], T.sem["ls%d" % k],
                                               pid, rid, topo.mask(core, dst))})
-        ops.append({"e": None, "kind": "arr", "r": [], "w": [(land, 0, b - a)], "f": None,
+        ops.append({"e": None, "kind": "arr", "r": [], "w": [(land, 0, b - a)], "f": None, "c": 0.0, "lat": 0.0,
                     "tok": ("ar%d" % k, len(topo.engines(frm, core)))})
 
     def ap(x):
@@ -169,453 +269,446 @@ def rank_program(g, core, T, topo):
     def full(name):
         return (name, 0, W)
 
+    def wide(x):
+        return x[2] - x[1]
+
+    def short(*xs):
+        return all(SCRATCH[x[0]][2] in (B, HF, U16) for x in xs)
+
     def tt(out, a, b, alu):
-        op("V", lambda: V.tensor_tensor(ap(out), ap(a), ap(b), alu), [a, b], [out])
+        op("V", lambda: V.tensor_tensor(ap(out), ap(a), ap(b), alu), [a, b], [out],
+           wide(out) * (1 if a[0] in PSUM or b[0] in PSUM else 2))
 
     def ts(out, a, s1, o1, s2=None, o2=None):
+        c = wide(out) * (0.5 if short(out, a) else 1)
         if o2 is None:
-            op("V", lambda: V.tensor_scalar(ap(out), ap(a), s1, None, o1), [a], [out])
+            op("V", lambda: V.tensor_scalar(ap(out), ap(a), s1, None, o1), [a], [out], c)
         else:
-            op("V", lambda: V.tensor_scalar(ap(out), ap(a), s1, s2, o1, o2), [a], [out])
+            op("V", lambda: V.tensor_scalar(ap(out), ap(a), s1, s2, o1, o2), [a], [out], c)
 
-    def offs(lst, c, off):
+    def fill(out, value):
+        op("V", lambda: V.memset(ap(out), value), [], [out], wide(out) * (0.5 if short(out) else 1))
+
+    def offs(lst, c, off=0):
         return (lst, off + c[0] // 16, off + c[1] // 16)
 
     def gt(out, win, of, b, alu):
-        op("V", lambda: V.tensor_tensor(ap(out), ap(win).indirect(ap(of)), ap(b), alu), [win, of, b], [out])
+        op("V", lambda: V.tensor_tensor(ap(out), ap(win).indirect(ap(of)), ap(b), alu), [win, of, b], [out], wide(out) * GATHER + 55)
 
-    def act(out, a, fn=ACT.Copy, scale=1.0, bias=0.0):
-        op("S", lambda: S.activation(ap(out), ap(a), fn, bias=bias, scale=scale), [a], [out])
+    def act(out, a, fn=ACT.Copy, scale=1.0, bias=0.0, more=0):
+        op("S", lambda: S.activation(ap(out), ap(a), fn, bias=bias, scale=scale), [a], [out], wide(out) + more)
 
-    def gact(out, win, of):
-        op("S", lambda: S.activation(ap(out), ap(win).indirect(ap(of)), ACT.Copy), [win, of], [out])
+    def gact(out, win, of, fn=ACT.Copy, scale=1.0):
+        op("S", lambda: S.activation(ap(out), ap(win).indirect(ap(of)), fn, scale=scale), [win, of], [out], wide(out) * GATHER)
 
-    def mm(o_ap, l_ap, r_ap, st, sp, r, w):
-        op("P", lambda: P.matmul(o_ap, l_ap, r_ap, st, sp), r, w)
+    def select(out, a, pattern, cmp, base, cm, r, w, n):
+        op("G", lambda: g.affine_select(out, a, pattern, cmp, 0.0, base, cm), r, w, 2 * n)
 
-    def wrap(out, src, first=True):
-        for l in range(16):
-            mm(ap(out), T.bn[:, 15 - l:143 - l], T[src[0]][:, src[1] + l:src[2]:16], first and l == 0, l == 15,
-               [src, ("bn", 0, 144)], [out])
+    def twin(e, out, a):
+        if e == "S":
+            act(out, a)
+        else:
+            select(ap(out), ap(a), [[0, wide(out)]], ALU.is_ge, 0, 0, [a], [out], wide(out))
 
-    def ident(out, src, st, sp):
-        mm(ap(out), T.zb[:, 0:128], ap(src), st, sp, [src, ("zb", 0, 256)], [out])
+    def pe(terms, out, first=True, last=True):
+        def f():
+            for n, (o_ap, l_ap, r_ap, _, _) in enumerate(terms):
+                ins = P.matmul(o_ap, l_ap, r_ap, first and n == 0, last and n == len(terms) - 1)
+            return ins
+        op("P", f, [x for t in terms for x in t[3]], [out, ("sum" + out[0], out[1] // 512, out[1] // 512 + 1)],
+           sum(t[4] for t in terms))
 
-    def turn(land, forward, z="zf", pieces=1):
-        for half, s in ((0, 16 if forward else 112), (1, 64)):
-            for k in range(pieces):
-                src = (land, 256 * k + 128 * half, 256 * k + 128 * half + 128)
-                out = ("C7", 256 + 128 * half, 384 + 128 * half)
-                mm(ap(out), T[z][:, 128 - s:256 - s], ap(src), k == 0, k == pieces - 1, [src, (z, 0, 256)], [out])
-    ROT = ("C7", 256, 512)
+    ONE, NEG, K1, M512, FAR = 0, 256, 384, 512, 640
 
-    dma("Y", T.ci[0:32, :], T.con[:], [], [("ci", 0, 512)])
-    dma("S", T.ci[32:40, :], T.cur[:], [], [("ci", 512, 1024)])
-    dma("Y", T.qb[:], T.q0[:], [], [full("qb")])
-    dma("S", T.vb[:], T.v0[:], [], [full("vb")])
-    dma("Y", T.qb2[:], T.q0[:], [], [full("qb2")])
-    dma("S", T.kh[:], T.kap[:], [], [full("kh")])
-    dma("Y", T.ka[:, 0:NV], T.kap[:, 0:NV], [], [("ka", 0, NV)])
-    dma("Y", T.am[0:8, :], T.aim[:], [], [full("am")])
-    op("V", lambda: V.memset(T.bc[:], 0.0), [], [("bc", 0, 720)])
-    op("V", lambda: V.memset(T.ones[:, 0:256], 1.0), [], [("ones", 0, 256)])
-    op("V", lambda: V.memset(T.bn[:], 0.0), [], [("bn", 0, 144)])
-    op("V", lambda: V.memset(T.ones[:, 256:2048], 1.0), [], [("ones", 256, 2048)])
-    op("V", lambda: V.memset(T.onef[:], 1.0), [], [("onef", 0, 256)])
-    op("V", lambda: V.memset(T.eps[:], -UNIT), [], [("eps", 0, 64)])
-    ON = [("ones", 0, 256)]
-    op("G", lambda: g.iota(T.pi[:, 0:1], [[0, 1]], 0, 1), [], [("pi", 0, 4)])
-    op("G", lambda: g.affine_select(T.bc[:, 591:720:16], T.ones[:, 0:9], [[-1, 9]], ALU.is_equal, 0.0, -32, 1),
-       ON, [("bc", 576, 720)])
-    op("G", lambda: g.affine_select(T.bc[:, 15:576:16], T.ones[:, 0:36], [[-4, 4], [-16, 9]], ALU.is_equal, 0.0, 0, 4),
-       ON, [("bc", 0, 576)])
-    op("G", lambda: g.affine_select(T.bl[:], T.ones[:, 0:8], [[-16, 8]], ALU.is_ge, 0.0, 0, 1), ON, [("bl", 0, 8)])
-    op("G", lambda: g.iota(T.iw0[:], [[16, 64]], 0, 1, allow_small_or_imprecise_dtypes=True), [], [("iw0", 0, 64)])
-    op("G", lambda: g.affine_select(T.bn[:, 15:143:16], T.bl[:], [[16, 8]], ALU.is_ge, 0.0, 15, -1),
-       [("bl", 0, 8)], [("bn", 0, 144)])
-    op("G", lambda: g.affine_select(T.zb[:], T.ones[:, 0:256], [[0, 2], [-1, 128]], ALU.is_equal, 0.0, 0, 1),
-       ON, [("zb", 0, 256)])
-    op("G", lambda: g.affine_select(T.wr[:], T.ones[:], [[-1, 16], [-16, 8], [0, 16]], ALU.is_equal, 0.0, 0, 1),
-       [("ones", 0, 2048)], [("wr", 0, 2048)])
-    op("G", lambda: g.iota(T.ir[:], [[1, W]], 0, 0, allow_small_or_imprecise_dtypes=True), [], [full("ir")])
+    def times(out, m, src):
+        return (ap(out), T.zz[:, m:m + 128], ap(src), [src, ("zz", 0, 768)], max(64, wide(src)))
+
+    def exact(out, src, m=0):
+        return (ap(out), T.zf[:, m:m + 128], ap(src), [src, ("zf", 0, 512)], 4 * max(64, wide(src)))
+
+    def wrap(out, src):
+        return [(ap(out), T.bn[:, 15 - l:143 - l], T[src[0]][:, src[1] + l:src[2]:16], [src, ("bn", 0, 144)], 64) for l in range(16)]
+
+    def turn(out, land, forward, z="zf", pieces=1):
+        for h, s in ((0, 16 if forward else 112), (1, 64)):
+            o = (out[0], out[1] + 128 * h, out[1] + 128 * h + 128)
+            pe([(ap(o), T[z][:, 128 - s:256 - s], T[land][:, 256 * k + 128 * h:256 * k + 128 * h + 128],
+                 [(land, 0, 256 * pieces), (z, 0, 256)], 128 * (4 if z == "zf" else 1)) for k in range(pieces)], o)
+
+    def half6(c):
+        return ("C6", c[0], c[1]) if c[0] < 512 else ("C7", c[0] - 512, c[1] - 512)
+
+    def quarters(c):
+        return [VIS, N1] if c == H1 else [Q1, Q0] if c == H0 else [c]
+
+    dma("Y", T.ci[0:32, :], T.con[:], [], [("ci", 0, 512)], lat=3500.0)
+    dma("S", T.ci[32:40, :], T.cur[:], [], [("ci", 512, 1024)], lat=3500.0)
+    dma("Y", T.qb[:], T.q0[:], [], [full("qb")], lat=4000.0)
+    dma("S", T.kh[:], T.kap[:], [], [full("kh")], lat=4500.0)
+    dma("Y", T.qb2[:], T.q0[:], [], [full("qb2")], lat=5000.0)
+    dma("S", T.vb[:], T.v0[:], [], [full("vb")], lat=5500.0)
+    dma("Y", T.vb2[:], T.v0[:], [], [full("vb2")], lat=6000.0)
+    dma("Y", T.ka[:, 0:NV], T.kap[:, 0:NV], [], [at("ka", NAT)], lat=6000.0)
+    dma("Y", T.am[0:8, :], T.aim[:], [], [full("am")], lat=6000.0)
+    fill(("bc", 0, 720), 0.0)
+    fill(("cz", 0, 256), 1.0)
+    fill(("bn", 0, 144), 0.0)
+    fill(("big", 0, 16), 2048.0)
+    for c, x in (((NEG, K1), -1.0), ((K1, M512), 1024.0), ((M512, FAR), -512.0), ((FAR, 768), -35840.0)):
+        fill(at("cz", c), x)
+    fill(("ones", 0, 2048), 1.0)
+    fill(("cf", 0, 256), 1.0)
+    fill(("cf", 256, 384), UNITS[0])
+    fill(("cf", 384, 512), UNITS[1])
+    fill(("top", 0, 64), 34816.0)
+    ON = [("cz", 0, 256)]
+    op("G", lambda: g.iota(T.pi[:, 0:1], [[0, 1]], 0, 1), [], [("pi", 0, 4)], 2)
+    select(T.bc[:, 591:720:16], T.cz[:, 0:9], [[-1, 9]], ALU.is_equal, -32, 1, ON, [("bc", 576, 720)], 9)
+    select(T.bc[:, 15:576:16], T.cz[:, 0:36], [[-4, 4], [-16, 9]], ALU.is_equal, 0, 4, ON, [("bc", 0, 576)], 36)
+    select(T.bl[:], T.big[:, 0:8], [[-16, 8]], ALU.is_ge, 0, 1, [("big", 0, 16)], [("bl", 0, 8)], 8)
+    select(T.bn[:, 15:143:16], T.bl[:], [[16, 8]], ALU.is_ge, 15, -1, [("bl", 0, 8)], [("bn", 0, 144)], 8)
+    op("G", lambda: g.iota(T.iw0[:], [[16, 64]], 0, 1, allow_small_or_imprecise_dtypes=True), [], [("iw0", 0, 64)], 128)
+    select(T.zz[:], T.cz[:], [[0, 6], [-1, 128]], ALU.is_equal, 0, 1, [("cz", 0, 768)], [("zz", 0, 768)], 768)
+    select(T.wr[:], T.ones[:], [[-1, 16], [-16, 8], [0, 16]], ALU.is_equal, 0, 1, [("ones", 0, 2048)], [("wr", 0, 2048)], 2048)
+    op("G", lambda: g.iota(T.ir[:], [[1, W]], 0, 0, allow_small_or_imprecise_dtypes=True), [], [full("ir")], 2 * W)
     send(at("kh", VIS), "lk", True)
-    op("G", lambda: g.affine_select(T.zf[:], T.onef[:], [[0, 2], [-1, 128]], ALU.is_equal, 0.0, 0, 1),
-       [("onef", 0, 256)], [("zf", 0, 256)])
-    op("G", lambda: g.affine_select(T.wa[0:8, :], T.ones[0:8, 0:128], [[-1, 8], [0, 16]], ALU.is_equal, 0.0, 0, 1),
-       ON, [("wa", 0, 128)])
-    op("V", lambda: V.tensor_scalar(T.pj[:, 0:1], T.pi[:, 0:1], 112, None, ALU.bitwise_and), [("pi", 0, 4)], [("pj", 0, 4)])
-    op("V", lambda: V.tensor_copy(T.ch[0:40, :], T.ci[0:40, :]), [full("ci")], [full("ch")])
-    op("V", lambda: V.tensor_copy(T.pf[:, 0:1], T.pj[:, 0:1]), [("pj", 0, 4)], [("pf", 0, 4)])
+    select(T.zf[:], T.cf[:], [[0, 4], [-1, 128]], ALU.is_equal, 0, 1, [("cf", 0, 512)], [("zf", 0, 512)], 512)
+    select(T.wa[0:8, :], T.cz[0:8, 0:128], [[-1, 8], [0, 16]], ALU.is_equal, 0, 1, ON, [("wa", 0, 128)], 128)
+    op("V", lambda: V.tensor_scalar(T.pj[:, 0:1], T.pi[:, 0:1], 112, None, ALU.bitwise_and), [("pi", 0, 4)], [("pj", 0, 4)], 1)
+    op("V", lambda: V.tensor_copy(T.pf[:, 0:1], T.pj[:, 0:1]), [("pj", 0, 4)], [("pf", 0, 4)], 1)
+    op("V", lambda: V.tensor_scalar(T.iw[:], T.iw0[:], T.pf[:, 0:1], None, ALU.subtract),
+       [("iw0", 0, 64), ("pf", 0, 4)], [("iw", 0, 64)], 64)
+    op("V", lambda: V.tensor_copy(T.ch[0:40, :], T.ci[0:40, :]), [full("ci")], [full("ch")], W)
     for m in (4, 0, 1, 2, 3):
         out = ("C7", 0, 64) if m == 4 else ("C6", 64 * m, 64 * m + 64)
-        for l in range(16):
-            mm(ap(out), T.bc[0:40, 144 * m + 15 - l:144 * m + 143 - l], T.ch[0:40, l:W:16], l == 0, l == 15,
-               [full("ch"), ("bc", 0, 720)], [out])
-    op("V", lambda: V.tensor_scalar(T.iw[:], T.iw0[:], T.pf[:, 0:1], UNIT, ALU.subtract, ALU.mult),
-       [("iw0", 0, 64), ("pf", 0, 4)], [("iw", 0, 64)])
+        pe([(ap(out), T.bc[0:40, 144 * m + 15 - l:144 * m + 143 - l], T.ch[0:40, l:W:16], [full("ch"), ("bc", 0, 720)], 64)
+            for l in range(16)], out)
     for k, m in enumerate((1, 2, 3, 0, 1, 2, 3)):
-        ts(("ee", 64 * k, 64 * k + 64), ("C7", 0, 64), float(m), ALU.is_equal, UNIT, ALU.mult)
-    for h in (1, 0):
-        act(at("v0a", H[h]), at("vb", H[h]), scale=0.0625)
-        act(at("v2", H[h]), at("vb", H[h]), scale=0.0625)
-
-    def by_cursor(k0):
-        src = "cc" if k0 else "C6"
-        for k in (0, 1):
-            o = 64 * (3 - k0 - k)
-            op("V", lambda k=k, o=o: V.tensor_tensor(T.mm[:, k, :], T[src][:, 0:256], T.ee[:, o:o + 256], ALU.mult),
-               [(src, 0, 256), ("ee", o, o + 256)], [("mm", k, k + 1)])
-        op("V", lambda: V.tensor_tensor(T.ma[:], T.mm[:, :, 0:128], T.mm[:, :, 128:256], ALU.add), [("mm", 0, 2)], [("ma", 0, 2)])
-        op("V", lambda: V.tensor_tensor(T.r0[:, k0:k0 + 2, :], T.ma[:, :, 0:64], T.ma[:, :, 64:128], ALU.add),
-           [("ma", 0, 2)], [("r0", 64 * k0, 64 * k0 + 128)])
-    by_cursor(0)
-    op("V", lambda: V.tensor_scalar(T.l1[:], T.r0[:, 0:2, :], 1024.0, None, ALU.mult), [("r0", 0, 128)], [("l1", 0, 128)])
+        ts(("ee", 64 * k, 64 * k + 64), ("C7", 0, 64), float(m), ALU.is_equal, 2048.0, ALU.mult)
+    for k in (0, 1):
+        o = 64 * (3 - k)
+        op("V", lambda k=k, o=o: V.tensor_tensor(T.mm[:, k, :], T.C6[:, 0:256], T.ee[:, o:o + 256], ALU.mult),
+           [("C6", 0, 256), ("ee", o, o + 256)], [("mm", k, k + 1)], 256)
+    op("V", lambda: V.tensor_tensor(T.ma[:], T.mm[:, :, 0:128], T.mm[:, :, 128:256], ALU.add), [("mm", 0, 2)], [("ma", 0, 2)], 512)
+    op("V", lambda: V.tensor_tensor(T.r0[:], T.ma[:, :, 0:64], T.ma[:, :, 64:128], ALU.add), [("ma", 0, 2)], [("r0", 0, 128)], 256)
+    op("V", lambda: V.tensor_scalar(T.l1[:], T.r0[:], 1.0 / 2048.0, None, ALU.mult), [("r0", 0, 128)], [("l1", 0, 128)], 128)
+    op("S", lambda: S.activation(T.st1[:, 0:128], T.r0[:], ACT.Copy, scale=1.0 / 2048.0), [("r0", 0, 128)], [("st1", 0, 128)], 128)
+    act(full("kn"), full("kh"), ACT.Ln, more=1600)
+    act(full("kn"), full("kn"), ACT.Exp, scale=-1.0, more=1800)
     act(("cc", 0, 256), ("C6", 0, 256))
+    ops[-1]["r"].append(full("kn"))
 
-    def rr(name, a, n):
-        return T.r0[:, a:a + n, :] if name == "r0" else T[name][:, 64 * a:64 * (a + n)]
-
-    def rsub(out, name, a, b, n):
-        op("V", lambda: V.tensor_tensor(ap(out), rr(name, a, n), rr(name, b, n), ALU.subtract), [(name, 0, 256)], [out])
-
-    def radd(out, name, a, n, m):
-        op("V", lambda: V.tensor_tensor(ap(out), rr(name, a, n), ap(m), ALU.add), [(name, 64 * a, 64 * (a + n)), m], [out])
-
-    FL, MT = ("C7", 192, 256), 64
-    F0, TJ = ("C6", 128, 192), ("C6", 192, 256)
-    stacks = {1: "r0", 2: "r1", 3: "r2", 4: "r3"}
-    dels = {1: "d0", 2: "d1", 3: "d2"}
-
-    def deltas(name, d, s, four):
-        rsub((s, 0, 64), name, 1, 0, 1)
-        if d:
-            rsub((d, 0, 128), name, 1, 2, 2)
-        if four:
-            rsub((d, 128, 192), name, 3, 0, 1)
-            rsub((d, 192, 256), name, 0, 1, 1)
-
-    def advance(name, d, new, k0):
+    def later_rows():
+        for k in (2, 3):
+            y = ("PB", 256 * (k - 2), 256 * (k - 1))
+            pe([times(y, ONE, ("cc", 0, 256)), times(y, ONE, ("ee", 64 * (3 - k), 64 * (3 - k) + 256))], y)
+        act(("uu", 0, 512), at("PB", H0), ACT.Relu, bias=-2048.0)
         for k in (0, 1):
-            tt(("C7", MT + 64 * k, MT + 64 * k + 64), FL, (d, 64 * (k0 + k), 64 * (k0 + k) + 64), ALU.mult)
-        yield
-        radd((new, 64 * k0, 64 * k0 + 128), name, (k0 + 2) % 4, 2, ("C7", MT, MT + 128))
-        yield
+            y = ("PB", 512 + 64 * k, 576 + 64 * k)
+            pe([times(y, ONE, ("uu", 256 * k + 64 * m, 256 * k + 64 * m + 64)) for m in range(4)], y)
+        act(("st1", 128, 256), ("PB", 512, 640))
 
-    def decide(t, q, filler, busy):
-        lst, st = "l%d" % t, stacks[t]
-        hs = (0, 1) if t == 3 else (1, 0)
-        for w in (0, 1):
-            for h in hs:
-                c = H[h]
-                gt(at("D", c, 1024 * w), full(q), offs(lst, c, 64 * w), at("qb2" if t == 1 else "q2", c), ALU.subtract)
-                act(at("AB", c, 1024 * w), at("D", c, 1024 * w), ACT.Abs, scale=ABS_SCALE)
-                if w == 0:
-                    act(at("NB", c), at("AB", c), ACT.Sign, scale=-1.0, bias=TIE)
-            if w == 0:
-                wrap(("C6", 0, 64), ("NB", 0, 1024))
-        if busy:
-            act(at("NB", H[hs[0]], 1024), at("AB", H[hs[0]], 1024), ACT.Sign, scale=-1.0, bias=TIE)
-        for h in (1, 0):
-            act(at("QP", H[h]), at(q, H[h]))
-        filler()
-        if not busy:
-            ts(at("NB", H[hs[0]], 1024), at("AB", H[hs[0]], 1024), NEAR, ALU.is_le, 0.5, ALU.subtract)
-        ts(F0, ("C6", 0, 64), 0.25, ALU.is_lt)
-        ts(("e0", 0, 64), ("C6", 0, 64), 0.25, ALU.is_ge, 32.0, ALU.mult)
-        tt(TJ, F0, ("s%d" % t, 0, 64), ALU.mult)
-        tt(("ja", 64, 128), F0, ("iw", 0, 64), ALU.add)
-        ts(at("NB", H[hs[1]], 1024), at("AB", H[hs[1]], 1024), NEAR, ALU.is_le, 0.5, ALU.subtract)
-        radd(("ja", 0, 64), st, 0, 1, TJ)
-        ts(("j%d" % t, 0, 128), ("ja", 0, 128), 1024.0, ALU.mult)
-        ident(("C7", 0, 64), ("eps", 0, 64), True, False)
-        ident(("C7", 0, 64), ("e0", 0, 64), False, False)
-        wrap(("C7", 0, 64), ("NB", 1024, 2048), False)
+    def row(t, k, n=1):
+        p = 64 * ((k + 2 * (t - 1)) % 4)
+        return ("st%d" % t, p, p + 64 * n)
 
-    def choices():
-        tt(("cw", 0, 64), ("C7", 0, 64), ("ja", 0, 64), ALU.min)
-        for h in (1, 0):
-            a, b = H[h]
-            for l in range(16):
-                mm(T.X[:, a + l:b:16], T.wr[:, 128 * l:128 * l + 128], T.cw[:, a // 16:b // 16], True, True,
-                   [("cw", 0, 64), ("wr", 0, 2048)], [("X", a, b)])
-            act(at("R", H[h]), at("X", H[h]), scale=1024.0)
+    def advance(t, mu):
+        z2, fl = ("C7", 64, 128), ("fl", 0, 64)
+        pe([times(z2, FAR, ("f0", 0, 64))] + wrap(z2, full(mu)), z2)
+        act(fl, z2, ACT.Sign, bias=-16384.0)
+        n = 4 if t < 3 else 2
+        new = row(t + 1, 0, 2) if n == 2 else ("st%d" % (t + 1), 0, 256)
+        old = ("st%d" % t, new[1], new[2])
+        y, z, u = ("C6", 256, 256 + 64 * n), ("C7", 128, 128 + 64 * n), ("uu", 0, 64 * n)
 
-    def half6(h):
-        return ("C6" if h == 0 else "C7", 0, 512)
+        def col(x, p):
+            return (x[0], x[1] + 64 * p, x[1] + 64 * p + 64)
+        before = [("st%d" % t, (old[1] + 64 * p - 64) % 256, (old[1] + 64 * p - 64) % 256 + 64) for p in range(n)]
+        pe([times(y, NEG, old)] + [times(col(y, p), ONE, before[p]) for p in range(n)], y, True, False)
+        pe([times(col(y, p), K1, fl) for p in range(n)], y, False, True)
+        pe([times(z, ONE, old)] + [times(col(z, p), M512, fl) for p in range(n)], z, True, False)
+        act(u, y, ACT.Relu)
+        pe([times(z, ONE, u)], z, False, True)
+        p = row(t + 1, 0)[1] - new[1]
+        ts(("l%d" % (t + 1), 0, 128), ("C7", 128 + p, 256 + p), -512.0, ALU.add)
+        act(new, z, ACT.Identity, bias=-512.0)
 
-    def forward(shot, t, q, v, qn, vn, filler, filler2):
-        again = shot == 1 and t == 1
-        jl, dv = "j%d" % t, "dq1" if again else "dv%d" % t
-        k = "kh" if t <= 2 else "ka"
-        kj, mu = ("kj1", "mu1") if t == 1 else ("kj", "mu")
-        if not again:
-            decide(t, q, filler, t == 3 if shot else t < 3)
-        if t == 2:
-            send(at(q, VIS), "lq%d" % shot, True)
+    def decide(t):
+        lst, jl = "l%d" % t, "j%d" % t
+        q, q2 = ("qb", "qb2") if t == 1 else ("q", "q2")
+        a, b = (H0, H1) if t == 3 else (H1, H0)
 
-        def g_dv(h):
-            gt(at(dv, H[h]), full(v), offs(jl, H[h], 0), at("v2", H[h]), ALU.subtract)
+        def diff(w, c):
+            gt(at("D", c, W * w), full(q), offs(lst, c, 64 * w), at(q2, c), ALU.subtract)
 
-        def g_a(h):
-            if again:
-                tt(at("pa", H[h]), half6(h), at(dv, H[h]), ALU.mult)
+        def size(w, c):
+            act(at("AB", c, W * w), at("D", c, W * w), ACT.Abs, scale=ABS_SCALE)
+
+        def near(w, c, e):
+            if e == "V":
+                ts(at("NB", c, W * w), at("AB", c, W * w), NEAR, ALU.is_le, 0.5, ALU.subtract)
             else:
-                gt(at("pa", H[h]), ("D", 0, 2048), offs(jl, H[h], 64), at(dv, H[h]), ALU.mult)
-            act(at("sa", H[h]), at("pa", H[h]), ACT.Sign, scale=-1.0)
+                act(at("NB", c, W * w), at("AB", c, W * w), ACT.Sign, scale=-1.0, bias=TIE)
+        n0, d, zs, n1, f0, jf = ("C6", 0, 64), ("C6", 64, 128), ("C7", 64, 128), ("C7", 0, 64), ("f0", 0, 64), ("jf", 0, 64)
+        pe([times(d, ONE, row(t, 1)), times(d, NEG, row(t, 0))], d)
+        first = [a] + quarters(b) if SPLIT0 else [a, b]
+        second = [a] + quarters(b) if SPLIT1 else [a, b]
+        for c in first:
+            diff(0, c); size(0, c)
+        for n, c in enumerate(first):
+            near(0, c, NEAR0[n])
+        pe(wrap(n0, ("NB", 0, W)), n0)
+        ts(f0, n0, 1024.0, ALU.is_lt)
+        tt(d, d, f0, ALU.mult)
+        tt(jf, d, row(t, 0), ALU.add)
+        ts((jl, 0, 64), jf, 1.0, ALU.mult)
+        for c in second:
+            diff(1, c); size(1, c)
+        for n, c in enumerate(second):
+            near(1, c, NEAR1[n])
+        pe([times(zs, ONE, ("iw", 0, 64)), times(zs, K1, f0)], zs)
+        pe(wrap(n1, ("NB", W, 2 * W)) + [times(n1, ONE, ("top", 0, 64)), times(n1, FAR, f0)], n1)
 
-        def g_mu(c):
-            gt(at(mu, c), full("R"), offs(jl, c, 0), at("ir", c), ALU.is_equal)
+    def publish(t):
+        tt(("cw", 0, 64), ("C7", 0, 64), ("jf", 0, 64), ALU.min)
+        ts(("j%d" % t, 64, 128), ("C7", 64, 128), 1.0, ALU.mult)
+        for a, b in (H1, H0):
+            for l in range(16):
+                op("P", lambda a=a, b=b, l=l: P.matmul(T.PY[:, a + l:b:16], T.wr[:, 128 * l:128 * l + 128],
+                                                       T.cw[:, a // 16:b // 16], True, True),
+                   [("cw", 0, 64), ("wr", 0, 2048)], [("PY", a, b), ("sumPY", a // 512, a // 512 + 1)], 64)
+            if a or R_COPY == "S":
+                act(("R", a, b), ("PY", a, b))
+            else:
+                ts(("R", a, b), ("PY", a, b), 1.0, ALU.mult)
+
+    def forward(shot, t, VP, X):
+        again = shot == 1 and t == 1
+        jl, kl, tp = "j%d" % t, "kl%d" % t, "tp%d" % t
+        k = "kh" if t <= 2 else "ka"
+        q, v, v2 = ("q", "v", "v2") if t > 1 else ("qb", "vs", "v2") if again else ("qb", "vb", "vb2")
+        unit = 16.0 if v == "vb" else 1.0
+        kj, mu = ("kj1", "mu1") if t == 1 else ("kj", "mu")
 
         def xx(c):
-            return ("C6", 256, 512) if c == VIS else at("X", c)
+            return at("PY" if c in (VIS, Q1) and not again else X, c)
+
+        def dv(c):
+            gt(at("dv", c), full(v), offs(jl, c), at(v2, c), ALU.subtract)
+
+        def pa(c, e):
+            if again:
+                pe([times(half6(c), ONE, at("sq1", c))], half6(c))
+                tt(at("pa", c), half6(c), at("dv", c), ALU.mult)
+            else:
+                gt(at("pa", c), ("D", 0, 2 * W), offs(jl, c, 64), at("dv", c), ALU.mult)
+            if e == "V":
+                ts(at("sa", c), at("pa", c), 0.0, ALU.is_lt)
+            else:
+                act(at("sa", c), at("pa", c), ACT.Sign, scale=-1.0)
+
+        def partner(c):
+            gact(at(kj, c), full(k), offs(jl, c))
+
+        def mutual(c):
+            gt(at(mu, c), full("R"), offs(jl, c), at("ir", c), ALU.is_equal)
 
         def mask(c):
-            ident(xx(c), at(kj, c), True, False)
-            ident(xx(c), at("sa", c), False, False)
-            ident(xx(c), at(mu, c), False, True)
-            act(xx(c), xx(c), ACT.Relu, bias=-2.0)
+            early, late = (mu, "sa") if again else ("sa", mu)
+            pe([times(xx(c), ONE, at(kj, c))], xx(c), True, False)
+            pe([times(xx(c), ONE, at(early, c))], xx(c), False, False)
+            pe([times(xx(c), ONE, at(late, c))], xx(c), False, True)
+            act(xx(c), xx(c), ACT.Relu, scale=1.0 / unit, bias=-2.0 / unit)
 
-        def kk(c):
-            tt(xx(c), xx(c), at(k, c), ALU.mult)
+        def push(parts):
+            for c in parts:
+                tt(xx(c), xx(c), at(k, c), ALU.mult)
+            for c in parts:
+                tt(at(tp, c), xx(c), at("dv", c), ALU.mult)
+            for c in parts:
+                tt(at(VP, c), at(VP, c), at(tp, c), ALU.add)
+            for c in parts:
+                tt(at("q", c), at(VP, c), at(q, c), ALU.add)
 
-        def tp(c):
-            tt(at("TP", c), xx(c), at(dv, c), ALU.mult)
-
-        def vv(c, out=None):
-            tt(out or at(vn, c), at("TP", c), at(v, c), ALU.add)
-
-        def v2(c):
+        def copies(c):
             if t < 4:
-                act(at("v2", c), at(vn, c))
+                twin("S", at("q2", c), at("q", c))
 
-        def qq(c):
-            tt(at(qn, c), at("QP", c), at(vn, c), ALU.add)
+        def keep(parts, c):
+            for x in parts:
+                act(at(kl, x), xx(x), scale=unit)
             if t < 4:
-                act(at("q2", c), at(qn, c))
-
+                act(at("v", c), at(VP, c))
+                twin("G", at("v2", c), at("v", c))
+        a, b = H1, H0
         if again:
-            act(full("ga"), full("ga"), scale=-1.0)
-            add_g("ga", (0, W))
-            g_dv(1); g_dv(0); g_a(1); g_a(0); mask(H[1]); mask(H[0])
-            filler()
-        elif t == 2:
-            gact(at(kj, H[1]), full(k), offs(jl, H[1], 0))
-            g_dv(1); choices(); g_a(1); g_dv(0)
-            g_mu(VIS); mask(VIS); g_mu(N1); mask(N1)
-            gact(at(kj, H[0]), full(k), offs(jl, H[0], 0))
-            g_a(0); kk(VIS); g_mu((0, 256)); tp(VIS); g_mu((256, 512)); vv(VIS, ("vo", 0, 256))
-            send(("vo", 0, 256), "lv%d" % shot, True)
-            mask(H[0])
-        else:
-            for h in (1, 0):
-                gact(at(kj, H[h]), full(k), offs(jl, H[h], 0))
-            g_dv(1); choices(); g_dv(0); g_a(1); g_a(0); g_mu(H[1]); mask(H[1]); g_mu(H[0]); mask(H[0])
-            if shot == 0 and t == 4:
-                act(full("kn"), full("kn"), ACT.Exp, scale=-1.0)
-            if t == 1:
-                for h in (1, 0):
-                    gact(at("dq1", H[h]), ("D", 0, 2048), offs("j1", H[h], 64))
-        step_on = t < 4 and not again
-        if step_on:
-            ident(("C7", 0, 64), ("e0", 0, 64), True, False)
-            wrap(("C7", 0, 64), full(mu), False)
-        if t == 4:
-            for h in (1, 0):
-                mm(ap(half6(h)), T.wa[0:8, :], T.am[0:8, H[h][0]:H[h][1]], True, True, [("wa", 0, 128), full("am")], [half6(h)])
-
-        def small():
-            if step_on:
-                ts(FL, ("C7", 0, 64), 40.0, ALU.is_gt)
-                yield
-                for _ in advance(stacks[t], dels[t], stacks[t + 1], 0):
-                    yield
-                ts(("l%d" % (t + 1), 0, 128), (stacks[t + 1], 0, 128), 1024.0, ALU.mult)
-            yield
-        sm = small()
-
-        def logk(h):
-            if t < 4:
-                act(at("kl%d" % t, H[h]), at("X", H[h]))
-            else:
-                act(at("X", H[h]), at("X", H[h]), scale=1.0 / 256.0)
+            dv(a)
+            for c in (H0, H1):
+                tt(at("ge", c), at("PY", c), at("tp1", c), ALU.mult)
+            add_g("ge", ALL)
+            pa(a, "S"); dv(b); mask(a); pa(b, "S"); mask(b)
+            push(quarters(a)); copies(a); push(quarters(b)); copies(b); keep([a], a); keep([b], b)
+            return
         if t == 2:
-            act(at("kl2", VIS), xx(VIS))
-            kk(N1); tp(N1); kk(H[0])
-            act(at("kl2", N1), at("X", N1))
-            vv(N1); v2(N1); tp(H[0])
-            if shot:
-                act(at("X", H[1]), at("kn", H[1]), ACT.Square, scale=16.0)
-            next(sm, 0); qq(N1); logk(0); vv(H[0]); next(sm, 0)
-            if shot:
-                act(at("X", H[0]), at("kn", H[0]), ACT.Square, scale=16.0)
-            qq(H[0]); next(sm, 0)
-            turn("lq%d" % shot, True)
-            act(("qov", 0, 256), ROT)
-            v2(H[0])
-            next(sm, 0)
-            filler2()
-            turn("lv%d" % shot, True)
-            tt(at(qn, VIS), ROT, ("qov", 0, 256), ALU.add)
-            act(at("q2", VIS), at(qn, VIS))
-            act(at(vn, VIS), ROT)
-            act(at("v2", VIS), ROT)
-        else:
-            a, b = 1, 0
-            kk(H[a]); tp(H[a]); kk(H[b]); logk(a); vv(H[a]); v2(H[a]); tp(H[b]); next(sm, 0); logk(b); qq(H[a]); next(sm, 0)
-            vv(H[b]); next(sm, 0); v2(H[b])
-            if t == 4:
-                tt(at("aq", H[1]), at(qn, H[1]), half6(1), ALU.subtract)
-                act(at("avc", H[1]), at("aq", H[1]))
-            qq(H[b]); next(sm, 0)
-            if t == 4:
-                tt(at("aq", H[0]), at(qn, H[0]), half6(0), ALU.subtract)
-                act(half6(0), at("aq", H[0]))
-            filler2()
-
-    def rest_of(t, four):
-        def f():
-            if t < 4:
-                for _ in advance(stacks[t - 1], dels[t - 1], stacks[t], 2):
-                    pass
-            deltas(stacks[t], dels.get(t), "s%d" % t, four)
-        return f
-
-    def nothing():
-        pass
-
-    def bank(t):
-        return "X" if t % 2 == 0 else "TP"
-
-    def gain(t, out, c, off=0):
-        tt(at(out, c, off), at(bank(t), c), at("dv%d" % t, c), ALU.mult)
+            send(at("q", VIS), "lq%d" % shot, True)
+        decide(t)
+        publish(t); dv(a); partner(a); dv(b); pa(a, "S"); partner(b)
+        if t == 1:
+            later_rows()
+            for c in (a, b):
+                act(at(VP, c), at("vb", c), scale=0.0625)
+        mutual(VIS); mask(VIS); mutual(N1); mask(N1); pa(b, SIGN_B)
+        if t == 2:
+            rot = ("C6", 256, 512)
+            tt(xx(VIS), xx(VIS), at(k, VIS), ALU.mult)
+            tt(at(tp, VIS), xx(VIS), at("dv", VIS), ALU.mult)
+            tt(("vo", 0, 256), at(VP, VIS), at(tp, VIS), ALU.add)
+            send(("vo", 0, 256), "lv%d" % shot, True)
+            mutual(b); mask(Q1); mask(Q0)
+            advance(t, mu)
+            push([N1, Q1, Q0]); copies(N1); copies(b)
+            rot = at("PY", VIS)
+            act(at(kl, VIS), xx(VIS))
+            turn(rot, "lq%d" % shot, True)
+            act(("qov", 0, 256), rot)
+            turn(rot, "lv%d" % shot, True)
+            tt(at("q", VIS), rot, ("qov", 0, 256), ALU.add)
+            act(at("q2", VIS), at("q", VIS))
+            keep([N1], N1); keep([Q1, Q0], b)
+            act(at("v", VIS), rot)
+            twin("G", at("v2", VIS), at("v", VIS))
+            act(at(VP, VIS), at("v", VIS))
+            return
+        mutual(b); mask(Q1); mask(Q0)
+        push([VIS, N1]); copies(a)
+        if t < 4:
+            advance(t, mu)
+        push([Q1, Q0]); copies(b); keep([VIS, N1], a); keep([Q1, Q0], b)
+        if t == 1:
+            for c in (a, b):
+                gact(at("sq1", c), ("D", 0, 2 * W), offs(jl, c, 64), ACT.Sign)
+            turn(at("PY", VIS), "lk", True, z="zz")
+            act(at("ka", VIS), at("PY", VIS))
 
     def add_g(src, c, off=0):
-        dma("G", ap(at("G", c)), ap(at(src, c, off)), [at(src, c, off), at("G", c)], [at("G", c)], add=True)
+        dma("G", ap(at("G", c)), ap(at(src, c, off)), [at(src, c, off), at("G", c)], [at("G", c)], add=True, lat=3500.0)
 
-    def backward(shot, v0, v0n):
-        def load(t, hs=(1, 0)):
-            for h in hs:
-                act(at(bank(t), H[h]), at("kl%d" % t, H[h]))
+    def backward(shot, VP, X):
+        rot = ("C7", 256, 512)
+        for c in (H1, H0):
+            pe([(ap(half6(c)), T.wa[0:8, :], T.am[0:8, c[0]:c[1]], [("wa", 0, 128), full("am")], 512)], half6(c))
+            for x in quarters(c):
+                tt(at("A", x), at("q", x), half6(x), ALU.subtract)
+        send(at("A", VIS), "la%d" % shot, False)
+        wins = {4: "A", 3: "av1", 2: "av2", 1: "av1"}
+        unit = UNITS[shot]
 
-        def da(t, src, c):
-            gt(at("da", c), full(src), offs("j%d" % t, c, 0), at("avc", c), ALU.subtract)
+        def da(t):
+            return X if t % 2 == 0 else "PY"
 
-        def tb(t, c):
-            tt(at(bank(t), c), at(bank(t), c), at("da", c), ALU.mult)
+        def av(t, c):
+            p = PE_BACK.get(t, (0, 0))
+            return at("C6", c, -p[0]) if p[0] <= c[0] < p[1] else at(VP, c)
 
-        def av(t, src, c, out=None):
-            tt(out or at("av2", c), at(bank(t), c), at(src, c), ALU.add)
+        def pull(t, c, fine=False):
+            act(at(VP, c), at(wins[t], c), scale=unit if t == 1 else 1.0)
+            for x in (quarters(c) if fine else [c]):
+                gact(at("ag", x), full(wins[t]), offs("j%d" % t, x), scale=unit if t == 1 else 1.0)
+            for x in quarters(c):
+                tt(at(da(t), x), at("ag", x), at(VP, x), ALU.subtract)
+            for x in quarters(c):
+                tt(at("tb", x), at(da(t), x), at("kl%d" % t, x), ALU.mult)
 
-        def twin(c, h):
-            act(at("avc", c) if h is None else at("C6", c, -H[h][0]), at("av1", c))
+        def add(t, c):
+            if PE_BACK.get(t) == c:
+                pe([exact(av(t, c), at(wins[t], c), 256 + 128 * shot if t == 1 else 0)], av(t, c), True, False)
+                for x in quarters(c):
+                    pe([exact(av(t, x), at("tb", x))], av(t, x), False, x == quarters(c)[-1])
+            else:
+                for x in quarters(c):
+                    tt(at(VP, x), at(VP, x), at("tb", x), ALU.add)
 
-        def drift(c, h=None):
-            tt(at("av1", c), at("QP", c), at("av2", c), ALU.add)
-            twin(c, h)
+        def drift(t, c):
+            for x in quarters(c):
+                tt(at(wins[t - 1], x), av(t, x), at("A", x), ALU.add)
 
-        def fetch(t, src, h):
-            gact(at("da", H[h]), full(src), offs("j%d" % t, H[h], 0))
-
-        def less(h):
-            tt(at("da", H[h]), at("da", H[h]), ("C6", 0, 512), ALU.subtract)
-        fetch(4, "aq", 0)
-        for h in (1, 0):
-            act(at("A", H[h]), at("aq", H[h]), scale=1.0 / 256.0)
-            act(at("QP", H[h]), at("aq", H[h]), scale=1.0 / 256.0)
-            if h:
-                send(at("A", VIS), "la%d" % shot, False)
-        da(4, "aq", H[1]); tb(4, H[1]); less(0); av(4, "A", H[1]); tb(4, H[0]); drift(H[1]); av(4, "A", H[0])
-        load(3, (1,))
-        gain(4, "gv", VIS, -768)
-        drift(H[0], 0)
-        fetch(3, "av1", 0)
-        load(3, (0,))
-        da(3, "av1", VIS); da(3, "av1", N1); tb(3, VIS); tb(3, N1); av(3, "av1", VIS, ("ao", 0, 256))
+        def gain(t, c):
+            out = {4: at("gg", c), 3: at("gg", c, 256 if c == VIS else 1280), 2: at("gb", c), 1: at("ge", c)}[t]
+            tt(out, at(da(t), c), at("tp%d" % t, c), ALU.mult)
+        if shot == 0:
+            act(full("G"), full("kh"), ACT.Square)
+            act(full("G"), full("G"), scale=-1.0)
+        pull(4, H1, True); add(4, H1); pull(4, H0); add(4, H0); drift(4, H0); drift(4, H1)
+        gain(4, H1)
+        if shot == 0:
+            newton()
+        pull(3, VIS)
+        tt(("ao", 0, 256), at(VP, VIS), at("tb", VIS), ALU.add)
         send(("ao", 0, 256), "lw%d" % shot, False)
-        turn("la%d" % shot, False)
-        act(("ahv", 0, 256), ROT)
-        less(0); av(3, "av1", N1); tb(3, H[0])
-        ga = "ga" if shot else "G"
-        gain(4, ga, N1); av(3, "av1", H[0]); drift(N1, 1); gain(4, ga, H[0])
-        if shot:
-            add_g("ga", (0, NV))
-        drift(H[0])
-        act(at("QP", VIS), ("ahv", 0, 256))
-        load(2)
+        turn(rot, "la%d" % shot, False)
+        act(at("A", VIS), rot)
+        pull(3, N1); add(3, N1); pull(3, H0); add(3, H0); drift(3, H0); drift(3, N1)
+        gain(3, VIS)
+        send(("gg", NV, NV + 512), "lg%d" % shot, False)
+        gain(3, N1); gain(3, H0)
+        turn(rot, "lw%d" % shot, False)
+        tt(at("av2", VIS), rot, at("A", VIS), ALU.add)
+        gain(4, H0)
+        add_g("gg", NAT, 1280)
+        add_g("gg", NAT)
+        pull(2, H0, True); add(2, H0); pull(2, H1); add(2, H1); drift(2, H1); drift(2, H0)
+        gain(2, H0); gain(2, H1)
+        turn(rot, "lg%d" % shot, False, pieces=2)
         if shot == 0:
-            act(at("rk", H[0]), at("kn", H[0]), scale=-512.0)
-        gain(3, "gv", VIS, -512)
-        send(("gv", 0, 512), "lg%d" % shot, False)
-        gain(3, "gb", N1); gain(3, "gb", H[0])
-        add_g("gb", (0, NV))
-        turn("lw%d" % shot, False)
-        tt(at("av1", VIS), ROT, ("ahv", 0, 256), ALU.add)
-        twin(VIS, 1)
-        fetch(2, "av1", 1)
-        load(1)
-        if shot == 0:
-            act(at("rk", H[1]), at("kn", H[1]), scale=-512.0)
-        da(2, "av1", H[0]); tb(2, H[0]); less(1); av(2, "av1", H[0]); tb(2, H[1]); drift(H[0]); av(2, "av1", H[1])
-        gain(2, "ge", H[0]); drift(H[1], 1)
-        add_g("ge", H[0])
-        fetch(1, "av1", 1)
-        da(1, "av1", H[0]); gain(2, "ge", H[1]); tb(1, H[0]); less(1)
-        turn("lg%d" % shot, False, pieces=2)
-        act(("gr", 0, 256) if shot else at("G", VIS), ROT)
-        add_g("ge", H[1])
-        if shot == 0:
-            act(half6(0), at("dq1", H[0]))
-            act(half6(1), at("dq1", H[1]))
-            for h in (0, 1):
-                act(at("QP", H[h]), at("qb", H[h]))
-            act(full("ga"), full("kh"), ACT.Square, scale=0.0625)
-        av(1, "av1", H[0]); tb(1, H[1])
-        ts(at("X", H[0]), at("av2", H[0]), CLIP, ALU.min, -CLIP, ALU.max)
-        av(1, "av1", H[1])
-        ts(at("X", H[1]), at("av2", H[1]), CLIP, ALU.min, -CLIP, ALU.max)
-        for h in (0, 1) if shot else (1, 0):
-            tt(at(v0n, H[h]), at(v0, H[h]), at("X", H[h]), ALU.subtract)
+            act(("gr", 0, 256), rot)
+            add_g("gr", VIS, -NV)
+            add_g("gb", ALL)
+        else:
+            tt(at("gb", VIS), rot, at("gb", VIS), ALU.add)
+            add_g("gb", H0)
+            add_g("gb", H1)
+        act(full("tp1"), full("tp1"), scale=1.0 / unit)
+
+        def settle(c):
+            v0 = "ov" if shot else "vs"
+            for x in quarters(c):
+                ts(av(1, x), av(1, x), CLIP * unit, ALU.min, -CLIP * unit, ALU.max)
+            for x in quarters(c):
+                tt(at(v0, x), at(v0, x), av(1, x), ALU.subtract)
             if shot == 0:
-                act(at("v2", H[h]), at(v0n, H[h]))
+                act(at("v2", c), at("vs", c))
+            else:
+                dma("Y", T.yv[:, c[0]:c[1]], ap(at("ov", c)), [at("ov", c)], [])
 
-    def first_extras():
-        turn("lk", True, z="zb")
-        act(at("ka", VIS), ROT)
-
-    def late_gain():
-        gain(1, "gb", H[1]); gain(1, "gb", H[0])
-        add_g("gb", (0, W))
-
-    def first_rest():
-        by_cursor(2)
-        deltas("r0", "d0", "s1", True)
+        def result(c, e):
+            tt(at("ou", c), at(X if c == H0 else "PY", c), at("rk", c), ALU.mult)
+            dma(e, T.yg[:, c[0]:c[1]], ap(at("ou", c)), [at("ou", c)], [])
+        if shot == 0:
+            pull(1, H0, True); add(1, H0); pull(1, H1); add(1, H1); settle(H1); settle(H0)
+            for c in (H1, H0):
+                act(at(VP, c), at("vs", c))
+        else:
+            act(full("ov"), full("vs"), scale=16.0)
+            pe([exact(at(X, H0), at("G", H0))], at(X, H0), True, False)
+            pull(1, H0, True); add(1, H0); gain(1, H0)
+            pe([exact(at(X, H0), at("ge", H0))], at(X, H0), False, True)
+            pull(1, H1); add(1, H1); settle(H1)
+            tt(at("PY", H1), at("PY", H1), at("tp1", H1), ALU.mult)
+            tt(at("PY", H1), at("PY", H1), at("G", H1), ALU.add)
+            result(H1, "S"); settle(H0); result(H0, "S")
 
     def newton():
-        for h in (1, 0):
-            tt(at("ou", H[h]), at("X", H[h]), at("kh", H[h]), ALU.mult)
-        dma("G", T.rk[:], T.ou[:], [full("ou"), full("rk")], [full("rk")], add=True)
+        act(full("vs"), full("vb"), scale=0.0625)
+        for c in (H1, H0):
+            act(("C7", 0, 512), at("kn", c), ACT.Square)
+            tt(at("ou", c), ("C7", 0, 512), at("kh", c), ALU.mult)
+        act(full("rk"), full("kn"), scale=-2.0)
+        dma("G", T.rk[:], T.ou[:], [full("ou"), full("rk")], [full("rk")], add=True, lat=3500.0)
 
-    act(full("kn"), full("kh"), ACT.Ln)
     for shot in (0, 1):
-        v0 = "v0a" if shot == 0 else "v0b"
-        if shot == 0:
-            forward(0, 1, "qb", v0, "qa", "va", first_rest, first_extras)
-            forward(0, 2, "qa", "va", "qc", "vc", rest_of(2, True), rest_of(3, False))
-        else:
-            forward(1, 1, "qb", v0, "qa", "va", late_gain, nothing)
-            forward(1, 2, "qa", "va", "qc", "vc", nothing, newton)
-        forward(shot, 3, "qc", "vc", "qa", "va", rest_of(3, False) if shot else nothing, nothing)
-        forward(shot, 4, "qa", "va", "qc", "vc", rest_of(4, False), nothing)
-        backward(shot, v0, "v0b" if shot == 0 else "va")
-    for h in (0, 1):
-        act(at("ov", H[h]), at("va", H[h]), scale=16.0)
-        dma("Y", T.yv[:, H[h][0]:H[h][1]], ap(at("ov", H[h])), [at("ov", H[h])], [])
-    for h in (1, 0):
-        tt(at("QP", H[h]), at("TP", H[h]), at("dq1", H[h]), ALU.mult)
-    tt(at("QP", VIS), at("QP", VIS), ("gr", 0, 256), ALU.add)
-    for h in (0, 1):
-        tt(at("QP", H[h]), at("QP", H[h]), at("G", H[h]), ALU.add)
-    for n, c in enumerate((H[0], N1, VIS)):
-        tt(at("ou", c), at("QP", c), at("rk", c), ALU.mult)
-        dma("S" if n == 1 else "Y", T.yg[:, c[0]:c[1]], ap(at("ou", c)), [at("ou", c)], [])
-    emit(ops, g, T)
+        for t in (1, 2, 3, 4):
+            forward(shot, t, "PA", "PB")
+        backward(shot, "PA", "PB")
+    if not ORDER:
+        ORDER.extend(arrange(ops))
+    emit([ops[i] for i in ORDER], g, T)

@@ -13,7 +13,13 @@ UNITS = (1.0 / 256.0, 1.0 / 16.0)
 
 Q1, Q0 = (256, 512), (0, 256)
 SPLIT0, SPLIT1, NEAR0, NEAR1, R_COPY, SIGN_B = True, True, "VVV", "SVV", "S", "S"
-PE_BACK = {}
+PE_LOAD, FINE, PE_SPEED, PE_SETTLE, PE_Q1 = False, True, True, False, False
+AGAIN = "SS"
+CHAIN = False
+PE_STEPS = ((0, 1), (0, 3), (0, 4), (1, 1), (1, 3), (1, 4))
+V_GATHERS = ((2, 0), (2, 1), (4, 1), (1, 0))
+Q1_PE = (2,)
+ON_PE = H1
 
 F, B, HF, I32, U16 = "float32", "bfloat16", "float16", "int32", "uint16"
 
@@ -25,16 +31,16 @@ def sb(cols, dt):
 SCRATCH = {
     "PA": ("psum", [128, 1024], F), "PB": ("psum", [128, 1024], F), "PY": ("psum", [128, 1024], F),
     "C6": ("psum", [128, 512], F), "C7": ("psum", [128, 512], F),
-    "ci": sb(W, I32), "ch": sb(W, HF), "ones": sb(2048, B), "big": sb(16, B), "cz": sb(768, B), "zz": sb(768, B),
-    "cf": sb(512, F), "zf": sb(512, F), "bc": sb(720, B), "bn": sb(144, B), "bl": sb(8, B), "wr": sb(2048, B),
+    "ci": sb(W, I32), "ch": sb(W, HF), "ones": sb(2048, B), "big": sb(16, B), "cz": sb(896, B), "zz": sb(896, B),
+    "cf": sb(640, F), "zf": sb(640, F), "bc": sb(720, B), "bn": sb(144, B), "bl": sb(8, B), "wr": sb(2048, B),
     "wa": sb(128, B), "iw": sb(64, HF), "iw0": sb(64, F), "pi": sb(4, I32), "pj": sb(4, I32), "pf": sb(4, F),
     "top": sb(64, B), "ee": sb(448, B), "cc": sb(256, HF), "uu": sb(512, HF),
-    "mm": ("sbuf", [128, 2, 256], F), "ma": ("sbuf", [128, 2, 128], F), "r0": ("sbuf", [128, 2, 64], F),
-    "f0": sb(64, B), "fl": sb(64, B), "jf": sb(64, F), "cw": sb(64, HF),
-    "D": sb(2048, F), "AB": sb(2048, B), "NB": sb(2048, B),
+    "mm": sb(512, HF),
+    "f0": sb(64, B), "fl": sb(64, B), "jf": sb(64, F), "cw": sb(64, HF), "hb": sb(64, B), "j64": sb(64, HF), "jr": sb(64, U16),
+    "D": sb(2048, F), "D1": sb(2048, F), "AB": sb(2048, B), "NB": sb(2048, B),
     "qov": sb(256, F), "gr": sb(256, F), "vo": sb(256, F), "ao": sb(256, F), "gg": sb(2048, F), "lk": sb(256, B),
 }
-for _n in "qb qb2 vb vb2 kh ka am pa sa kj kj1 mu mu1 sq1".split():
+for _n in "qb qb2 vb vb2 kh ka am amr pa sa kj kj1 mu mu1 sq1".split():
     SCRATCH[_n] = sb(W, B)
 for _n in "ir R q q2 v v2 vs dv A av1 av2 ag tb cl gb ge G kn rk ov ou".split():
     SCRATCH[_n] = sb(W, F)
@@ -50,11 +56,15 @@ NDMA, NREM = 24, 11
 SEMAPHORES = (["e" + e for e in ENG] + ["dm%d" % i for i in range(NDMA)]
               + ["ls%d" % i for i in range(NREM)] + ["ar%d" % i for i in range(NREM)])
 
-CYCLE, PE_CYCLE, HOP, SAME = 0.83, 0.45, 250.0, 250.0
-GATHER = 1.45
+CYCLE, PE_CYCLE, HOP, SAME = 0.83, 0.6, 250.0, 250.0
+GATHER = 1.56
 ROUNDS = 2
-RERUNS = 2
-LOOK = 0.25
+LOOKS = (0.0, 0.15, 0.3, 0.5, 0.8)
+SPAN = []
+PICK = None
+Q0_G = False
+EARLY_MU = False
+NEAR_A, MU_Q, EIGHTH, TAIL_PE = "V", True, False, True
 
 
 def banks_of(o):
@@ -63,7 +73,7 @@ def banks_of(o):
 
 def arrange(ops):
     n = len(ops)
-    hist, pred, succ = {}, [set() for _ in ops], [[] for _ in ops]
+    hist, pred, succ, loose = {}, [set() for _ in ops], [[] for _ in ops], set()
     for i, o in enumerate(ops):
         touch = [(r, False) for r in o["r"]] + [(r, True) for r in o["w"]]
         for (name, a, b), wr in touch:
@@ -76,10 +86,15 @@ def arrange(ops):
         if o["kind"] == "arr":
             pred[i].add(i - 1)
         pred[i].discard(i)
+        if o.get("after") is not None and o["after"] not in pred[i]:
+            pred[i].add(o["after"])
+            loose.add((o["after"], i))
         for m in pred[i]:
             succ[m].append(i)
 
     def hop(m, i):
+        if (m, i) in loose:
+            return 0.0
         return 0.0 if ops[m]["e"] == ops[i]["e"] == "P" else SAME if ops[m]["e"] == ops[i]["e"] else HOP
     uses = [[(o["e"], None)] + [(bk, o["e"]) for bk in sorted(banks_of(o))] if o["e"] else [] for o in ops]
 
@@ -108,7 +123,8 @@ def arrange(ops):
                 if left[k] == 0:
                     free.append(k)
         return start, max(start[i] + ops[i]["c"] + (0.0 if back else ops[i]["lat"]) for i in range(n))
-    def run(rank):
+
+    def run(rank, look):
         ready, start, left, until = [0.0] * n, [0.0] * n, [len(p) for p in pred], {}
         free = [i for i in range(n) if not left[i]]
         while free:
@@ -120,7 +136,7 @@ def arrange(ops):
                     s = max(s, end + (0.0 if w == who else HOP))
                 soon[i] = s
             i = min(free, key=lambda k: (soon[k], rank[k]))
-            i = min((k for k in free if ops[k]["e"] == ops[i]["e"] and soon[k] <= soon[i] + LOOK * ops[i]["c"]), key=lambda k: rank[k])
+            i = min((k for k in free if ops[k]["e"] == ops[i]["e"] and soon[k] <= soon[i] + look * ops[i]["c"]), key=lambda k: rank[k])
             free.remove(i)
             start[i] = soon[i]
             for key, who in uses[i]:
@@ -131,17 +147,25 @@ def arrange(ops):
                 if left[k] == 0:
                     free.append(k)
         return start, max(start[i] + ops[i]["c"] + ops[i]["lat"] for i in range(n))
-    start, span = run(list(range(n)))
-    best = (span, start)
-    for _ in range(RERUNS):
-        late, _span = place([(-start[i] - ops[i]["c"], -i) for i in range(n)], True)
-        start, span = run([(-late[i] - ops[i]["c"], i) for i in range(n)])
-        best = min(best, (span, start))
-    start = best[1]
+    tries = []
+    for look in LOOKS:
+        start, span = run(list(range(n)), look)
+        for _ in range(ROUNDS):
+            late, _span = place([(-start[i] - ops[i]["c"], -i) for i in range(n)], True)
+            start, span = place([(-late[i] - ops[i]["c"], i) for i in range(n)], False)
+            tries.append((span, start))
+    rank = [float(i) for i in range(n)]
+    for i in range(n - 1, -1, -1):
+        if ops[i].get("lazy"):
+            rank[i] = min([rank[k] for k in succ[i]] + [float(n)]) - 0.001
+    start, span = place(rank, False)
+    tries.append((span, start))
     for _ in range(ROUNDS):
         late, _span = place([(-start[i] - ops[i]["c"], -i) for i in range(n)], True)
         start, span = place([(-late[i] - ops[i]["c"], i) for i in range(n)], False)
-        best = min(best, (span, start))
+        tries.append((span, start))
+    best = min(tries) if PICK is None else tries[PICK]
+    SPAN[:] = [round(x[0] / 1000, 1) for x in tries]
     return sorted(range(n), key=lambda i: (best[1][i], i))
 
 
@@ -232,13 +256,24 @@ def rank_program(g, core, T, topo):
     n_ranks = len(T.cores)
     nxt, prv = T.cores[(rank + 1) % n_ranks], T.cores[(rank - 1) % n_ranks]
     ops = []
-    cnt = {"dma": 0, "rem": 0}
+    cnt, opened = {"dma": 0, "rem": 0}, {}
     V, S, P = g.vector, g.scalar, g.tensor
 
     def op(e, f, r, w, cycles):
-        fixed = {"V": 5.0, "S": 40.0, "G": 170.0, "P": 0.0}[e]
+        fixed = {"V": 5.0, "S": 65.0, "G": 170.0, "P": 0.0}[e]
         c = cycles * PE_CYCLE if e == "P" else fixed + max(cycles, 64) * CYCLE
         ops.append({"e": e, "f": f, "r": r, "w": w, "tok": None, "kind": "op", "c": c, "lat": 0.0})
+
+    def in_turn(since, e="V"):
+        mine = [i for i in range(since, len(ops)) if ops[i]["e"] == e]
+        for a, b in zip(mine, mine[1:]):
+            ops[b]["after"] = a
+
+    def can_wait(f, *args, **kw):
+        since = len(ops)
+        f(*args, **kw)
+        for o in ops[since:]:
+            o["lazy"] = True
 
     def dma(e, out, in_, r, w, add=False, lat=2500.0):
         qq = {"S": S, "Y": g.sync, "G": g}[e]
@@ -253,7 +288,7 @@ def rank_program(g, core, T, topo):
         dst, frm = (nxt, prv) if forward else (prv, nxt)
         rid, pid = topo.addr(dst, core)
         name, a, b = src
-        ops.append({"e": "G", "kind": "rem", "r": [src], "w": [], "c": 700.0, "lat": 3500.0,
+        ops.append({"e": "G", "kind": "rem", "r": [src], "w": [], "c": 700.0, "lat": 3500.0 if land[:2] in ("lv", "lw") else 5500.0,
                     "tok": ("ls%d" % k, len(topo.engines(core, dst))),
                     "f": lambda: g.remote_dma(T[land][:], T[name][:, a:b], T.sem["ar%d" % k], T.sem["ls%d" % k],
                                               pid, rid, topo.mask(core, dst))})
@@ -315,25 +350,56 @@ def rank_program(g, core, T, topo):
             for n, (o_ap, l_ap, r_ap, _, _) in enumerate(terms):
                 ins = P.matmul(o_ap, l_ap, r_ap, first and n == 0, last and n == len(terms) - 1)
             return ins
-        op("P", f, [x for t in terms for x in t[3]], [out, ("sum" + out[0], out[1] // 512, out[1] // 512 + 1)],
+        bank = (out[0], out[1] // 512)
+        if first:
+            opened[bank] = out
+        op("P", f, [x for t in terms for x in t[3]], [opened[bank] if last else out, ("sum" + bank[0], bank[1], bank[1] + 1)],
            sum(t[4] for t in terms))
 
-    ONE, NEG, K1, M512, FAR = 0, 256, 384, 512, 640
+    ONE, NEG, K1, M512, FAR, S16 = 0, 256, 384, 512, 640, 768
 
     def times(out, m, src):
-        return (ap(out), T.zz[:, m:m + 128], ap(src), [src, ("zz", 0, 768)], max(64, wide(src)))
+        return (ap(out), T.zz[:, m:m + 128], ap(src), [src, ("zz", 0, 896)], max(64, wide(src)))
 
     def exact(out, src, m=0):
-        return (ap(out), T.zf[:, m:m + 128], ap(src), [src, ("zf", 0, 512)], 4 * max(64, wide(src)))
+        return (ap(out), T.zf[:, m:m + 128], ap(src), [src, ("zf", 0, 640)], 4 * max(64, wide(src)))
 
     def wrap(out, src):
         return [(ap(out), T.bn[:, 15 - l:143 - l], T[src[0]][:, src[1] + l:src[2]:16], [src, ("bn", 0, 144)], 64) for l in range(16)]
 
-    def turn(out, land, forward, z="zf", pieces=1):
+    def turn(out, land, forward, z="zf", pieces=1, first=True):
         for h, s in ((0, 16 if forward else 112), (1, 64)):
             o = (out[0], out[1] + 128 * h, out[1] + 128 * h + 128)
             pe([(ap(o), T[z][:, 128 - s:256 - s], T[land][:, 256 * k + 128 * h:256 * k + 128 * h + 128],
-                 [(land, 0, 256 * pieces), (z, 0, 256)], 128 * (4 if z == "zf" else 1)) for k in range(pieces)], o)
+                 [(land, 0, 256 * pieces), (z, 0, 256)], 128 * (4 if z == "zf" else 1)) for k in range(pieces)], o, first, first)
+
+    V1, V4 = (768, 896), (896, 1024)
+
+    def leave(out, a, b):
+        tt((out, 0, 128), at(a, V1), at(b, V1), ALU.add)
+        for p in (0, 64):
+            op("V", lambda p=p: V.tensor_tensor(T[out][64 - p:128 - p, 128:256], T[a][p:p + 64, V4[0]:V4[1]],
+                                                T[b][p:p + 64, V4[0]:V4[1]], ALU.add),
+               [at(a, V4), at(b, V4)], [(out + "h", p, p + 64)], 128)
+
+    def arrive(out, rot, land, forward, b, off):
+        o = (rot[0], rot[1], rot[1] + 128)
+        s = 16 if forward else 112
+        pe([(ap(o), T.zf[:, 128 - s:256 - s], T[land][:, 0:128], [(land, 0, 256), ("zf", 0, 256)], 512)], o)
+        tt(at(out, V4), (land, 128, 256), at(b, V4, off), ALU.add)
+        tt(at(out, V1), o, at(b, V1, off), ALU.add)
+        return o
+
+    def fetch(out, off, rot, land, forward):
+        o = (rot[0], rot[1], rot[1] + 128)
+        s = 16 if forward else 112
+        pe([(ap(o), T.zf[:, 128 - s:256 - s], T[land][:, 0:128], [(land, 0, 256), ("zf", 0, 256)], 512)], o)
+        first = len(ops) - 1
+        act(at(out, V1, off), o)
+        for p in (0, 64):
+            op("S", lambda p=p: S.activation(T[out][64 - p:128 - p, V4[0] + off:V4[1] + off], T[land][p:p + 64, 128:256], ACT.Copy),
+               [(land, 0, 256)], [at(out, V4, off)], 128)
+        return first
 
     def half6(c):
         return ("C6", c[0], c[1]) if c[0] < 512 else ("C7", c[0] - 512, c[1] - 512)
@@ -342,7 +408,7 @@ def rank_program(g, core, T, topo):
         return [VIS, N1] if c == H1 else [Q1, Q0] if c == H0 else [c]
 
     dma("Y", T.ci[0:32, :], T.con[:], [], [("ci", 0, 512)], lat=3500.0)
-    dma("S", T.ci[32:40, :], T.cur[:], [], [("ci", 512, 1024)], lat=3500.0)
+    dma("S", T.ci[64:72, :], T.cur[:], [], [("ci", 512, 1024)], lat=3500.0)
     dma("Y", T.qb[:], T.q0[:], [], [full("qb")], lat=4000.0)
     dma("S", T.kh[:], T.kap[:], [], [full("kh")], lat=4500.0)
     dma("Y", T.qb2[:], T.q0[:], [], [full("qb2")], lat=5000.0)
@@ -350,63 +416,84 @@ def rank_program(g, core, T, topo):
     dma("Y", T.vb2[:], T.v0[:], [], [full("vb2")], lat=6000.0)
     dma("Y", T.ka[:, 0:NV], T.kap[:, 0:NV], [], [at("ka", NAT)], lat=6000.0)
     dma("Y", T.am[0:8, :], T.aim[:], [], [full("am")], lat=6000.0)
+    in_turn(0, "Y"); in_turn(0, "S")
     fill(("bc", 0, 720), 0.0)
     fill(("cz", 0, 256), 1.0)
     fill(("bn", 0, 144), 0.0)
     fill(("big", 0, 16), 2048.0)
-    for c, x in (((NEG, K1), -1.0), ((K1, M512), 1024.0), ((M512, FAR), -512.0), ((FAR, 768), -35840.0)):
+    for c, x in (((NEG, K1), -1.0), ((K1, M512), 1024.0), ((M512, FAR), -512.0), ((FAR, S16), -35840.0), ((S16, 896), 0.0625)):
         fill(at("cz", c), x)
     fill(("ones", 0, 2048), 1.0)
     fill(("cf", 0, 256), 1.0)
     fill(("cf", 256, 384), UNITS[0])
     fill(("cf", 384, 512), UNITS[1])
+    fill(("cf", 512, 640), -1.0)
     fill(("top", 0, 64), 34816.0)
     ON = [("cz", 0, 256)]
     op("G", lambda: g.iota(T.pi[:, 0:1], [[0, 1]], 0, 1), [], [("pi", 0, 4)], 2)
-    select(T.bc[:, 591:720:16], T.cz[:, 0:9], [[-1, 9]], ALU.is_equal, -32, 1, ON, [("bc", 576, 720)], 9)
+    select(T.bc[:, 591:720:16], T.cz[:, 0:9], [[-1, 9]], ALU.is_equal, -64, 1, ON, [("bc", 576, 720)], 9)
     select(T.bc[:, 15:576:16], T.cz[:, 0:36], [[-4, 4], [-16, 9]], ALU.is_equal, 0, 4, ON, [("bc", 0, 576)], 36)
     select(T.bl[:], T.big[:, 0:8], [[-16, 8]], ALU.is_ge, 0, 1, [("big", 0, 16)], [("bl", 0, 8)], 8)
     select(T.bn[:, 15:143:16], T.bl[:], [[16, 8]], ALU.is_ge, 15, -1, [("bl", 0, 8)], [("bn", 0, 144)], 8)
     op("G", lambda: g.iota(T.iw0[:], [[16, 64]], 0, 1, allow_small_or_imprecise_dtypes=True), [], [("iw0", 0, 64)], 128)
-    select(T.zz[:], T.cz[:], [[0, 6], [-1, 128]], ALU.is_equal, 0, 1, [("cz", 0, 768)], [("zz", 0, 768)], 768)
+    select(T.zz[:], T.cz[:], [[0, 7], [-1, 128]], ALU.is_equal, 0, 1, [("cz", 0, 896)], [("zz", 0, 896)], 896)
     select(T.wr[:], T.ones[:], [[-1, 16], [-16, 8], [0, 16]], ALU.is_equal, 0, 1, [("ones", 0, 2048)], [("wr", 0, 2048)], 2048)
     op("G", lambda: g.iota(T.ir[:], [[1, W]], 0, 0, allow_small_or_imprecise_dtypes=True), [], [full("ir")], 2 * W)
     send(at("kh", VIS), "lk", True)
-    select(T.zf[:], T.cf[:], [[0, 4], [-1, 128]], ALU.is_equal, 0, 1, [("cf", 0, 512)], [("zf", 0, 512)], 512)
+    select(T.zf[:], T.cf[:], [[0, 5], [-1, 128]], ALU.is_equal, 0, 1, [("cf", 0, 640)], [("zf", 0, 640)], 640)
     select(T.wa[0:8, :], T.cz[0:8, 0:128], [[-1, 8], [0, 16]], ALU.is_equal, 0, 1, ON, [("wa", 0, 128)], 128)
     op("V", lambda: V.tensor_scalar(T.pj[:, 0:1], T.pi[:, 0:1], 112, None, ALU.bitwise_and), [("pi", 0, 4)], [("pj", 0, 4)], 1)
     op("V", lambda: V.tensor_copy(T.pf[:, 0:1], T.pj[:, 0:1]), [("pj", 0, 4)], [("pf", 0, 4)], 1)
     op("V", lambda: V.tensor_scalar(T.iw[:], T.iw0[:], T.pf[:, 0:1], None, ALU.subtract),
        [("iw0", 0, 64), ("pf", 0, 4)], [("iw", 0, 64)], 64)
-    op("V", lambda: V.tensor_copy(T.ch[0:40, :], T.ci[0:40, :]), [full("ci")], [full("ch")], W)
-    for m in (4, 0, 1, 2, 3):
-        out = ("C7", 0, 64) if m == 4 else ("C6", 64 * m, 64 * m + 64)
-        pe([(ap(out), T.bc[0:40, 144 * m + 15 - l:144 * m + 143 - l], T.ch[0:40, l:W:16], [full("ch"), ("bc", 0, 720)], 64)
-            for l in range(16)], out)
+    since = len(ops)
+    op("V", lambda: V.tensor_copy(T.ch[0:32, :], T.ci[0:32, :]), [("ci", 0, 512)], [("ch", 0, 512)], W)
+    op("V", lambda: V.tensor_copy(T.ch[64:72, :], T.ci[64:72, :]), [("ci", 512, 1024)], [("ch", 512, 1024)], W)
+    rows = [("PY", 0, 64), ("PY", 512, 576), ("PB", 0, 64), ("PB", 512, 576), ("C7", 0, 64)]
+    for m in (0, 1, 4, 2, 3):
+        a, b, part = (64, 72, ("ch", 512, 1024)) if m == 4 else (0, 32, ("ch", 0, 512))
+        pe([(ap(rows[m]), T.bc[a:b, 144 * m + 15 - l:144 * m + 143 - l], T.ch[a:b, l:W:16], [part, ("bc", 0, 720)], 64)
+            for l in range(16)], rows[m])
+    in_turn(since, "V"); in_turn(since, "P")
     for k, m in enumerate((1, 2, 3, 0, 1, 2, 3)):
-        ts(("ee", 64 * k, 64 * k + 64), ("C7", 0, 64), float(m), ALU.is_equal, 2048.0, ALU.mult)
+        ts(("ee", 64 * k, 64 * k + 64), rows[4], float(m), ALU.is_equal)
+    for m in range(4):
+        for k in (0, 1):
+            tt(("mm", 256 * k + 64 * m, 256 * k + 64 * m + 64), rows[m], ("ee", 64 * (3 - k + m), 64 * (4 - k + m)), ALU.mult)
     for k in (0, 1):
-        o = 64 * (3 - k)
-        op("V", lambda k=k, o=o: V.tensor_tensor(T.mm[:, k, :], T.C6[:, 0:256], T.ee[:, o:o + 256], ALU.mult),
-           [("C6", 0, 256), ("ee", o, o + 256)], [("mm", k, k + 1)], 256)
-    op("V", lambda: V.tensor_tensor(T.ma[:], T.mm[:, :, 0:128], T.mm[:, :, 128:256], ALU.add), [("mm", 0, 2)], [("ma", 0, 2)], 512)
-    op("V", lambda: V.tensor_tensor(T.r0[:], T.ma[:, :, 0:64], T.ma[:, :, 64:128], ALU.add), [("ma", 0, 2)], [("r0", 0, 128)], 256)
-    op("V", lambda: V.tensor_scalar(T.l1[:], T.r0[:], 1.0 / 2048.0, None, ALU.mult), [("r0", 0, 128)], [("l1", 0, 128)], 128)
-    op("S", lambda: S.activation(T.st1[:, 0:128], T.r0[:], ACT.Copy, scale=1.0 / 2048.0), [("r0", 0, 128)], [("st1", 0, 128)], 128)
+        y = ("C6", 256 + 64 * k, 320 + 64 * k)
+        pe([times(y, ONE, ("mm", 256 * k + 64 * m, 256 * k + 64 * m + 64)) for m in range(4)], y)
+    ts(("l1", 0, 128), ("C6", 256, 384), 1.0, ALU.mult)
+    since = len(ops)
     act(full("kn"), full("kh"), ACT.Ln, more=1600)
     act(full("kn"), full("kn"), ACT.Exp, scale=-1.0, more=1800)
-    act(("cc", 0, 256), ("C6", 0, 256))
-    ops[-1]["r"].append(full("kn"))
+    for c in [H0] + ([] if (0, 1) in PE_STEPS else [H1]):
+        act(at("PA", c), at("vb", c), scale=0.0625)
+    act(("st1", 0, 128), ("C6", 256, 384))
+    ops[-1]["r"].append(("l1", 0, 128))
+    in_turn(since, "S")
 
     def later_rows():
+        last = max(i for i, o in enumerate(ops) if o["e"] == "S")
+        for m in range(4):
+            act(("cc", 64 * m, 64 * m + 64), rows[m])
+            ops[-1]["after"] = last
+
+        def rest():
+            last = dict((e, max(i for i, o in enumerate(ops) if o["e"] == e)) for e in "SP")
+            act(("uu", 0, 512), at("PB", H0), ACT.Relu, bias=-1024.0)
+            ops[-1]["after"] = last["S"]
+            for k in (0, 1):
+                y = ("PB", 512 + 64 * k, 576 + 64 * k)
+                pe([times(y, ONE, ("uu", 256 * k + 64 * m, 256 * k + 64 * m + 64)) for m in range(4)], y)
+                ops[-1]["after"] = last["P"]
+            act(("st1", 128, 256), ("PB", 512, 640))
+        last = len(ops) - 5
         for k in (2, 3):
             y = ("PB", 256 * (k - 2), 256 * (k - 1))
-            pe([times(y, ONE, ("cc", 0, 256)), times(y, ONE, ("ee", 64 * (3 - k), 64 * (3 - k) + 256))], y)
-        act(("uu", 0, 512), at("PB", H0), ACT.Relu, bias=-2048.0)
-        for k in (0, 1):
-            y = ("PB", 512 + 64 * k, 576 + 64 * k)
-            pe([times(y, ONE, ("uu", 256 * k + 64 * m, 256 * k + 64 * m + 64)) for m in range(4)], y)
-        act(("st1", 128, 256), ("PB", 512, 640))
+            pe([times(y, ONE, ("cc", 0, 256)), times(y, K1, ("ee", 64 * (3 - k), 64 * (3 - k) + 256))], y)
+            ops[-1]["after"] = last
+        return rest
 
     def row(t, k, n=1):
         p = 64 * ((k + 2 * (t - 1)) % 4)
@@ -415,6 +502,7 @@ def rank_program(g, core, T, topo):
     def advance(t, mu):
         z2, fl = ("C7", 64, 128), ("fl", 0, 64)
         pe([times(z2, FAR, ("f0", 0, 64))] + wrap(z2, full(mu)), z2)
+        ops[-1]["after"] = max(i for i in range(len(ops) - 1) if ops[i]["e"] == "P")
         act(fl, z2, ACT.Sign, bias=-16384.0)
         n = 4 if t < 3 else 2
         new = row(t + 1, 0, 2) if n == 2 else ("st%d" % (t + 1), 0, 256)
@@ -428,15 +516,19 @@ def rank_program(g, core, T, topo):
         pe([times(col(y, p), K1, fl) for p in range(n)], y, False, True)
         pe([times(z, ONE, old)] + [times(col(z, p), M512, fl) for p in range(n)], z, True, False)
         act(u, y, ACT.Relu)
-        pe([times(z, ONE, u)], z, False, True)
         p = row(t + 1, 0)[1] - new[1]
-        ts(("l%d" % (t + 1), 0, 128), ("C7", 128 + p, 256 + p), -512.0, ALU.add)
-        act(new, z, ACT.Identity, bias=-512.0)
+
+        def relist():
+            pe([times(z, ONE, u)], z, False, True)
+            ts(("l%d" % (t + 1), 0, 128), ("C7", 128 + p, 256 + p), -512.0, ALU.add)
+            act(new, z, ACT.Identity, bias=-512.0)
+            ops[-1]["r"].append(("l%d" % (t + 1), 0, 128))
+        return relist
 
     def decide(t):
         lst, jl = "l%d" % t, "j%d" % t
         q, q2 = ("qb", "qb2") if t == 1 else ("q", "q2")
-        a, b = (H0, H1) if t == 3 else (H1, H0)
+        a, b = (H0, H1) if t == 3 or PE_SPEED else (H1, H0)
 
         def diff(w, c):
             gt(at("D", c, W * w), full(q), offs(lst, c, 64 * w), at(q2, c), ALU.subtract)
@@ -451,12 +543,12 @@ def rank_program(g, core, T, topo):
                 act(at("NB", c, W * w), at("AB", c, W * w), ACT.Sign, scale=-1.0, bias=TIE)
         n0, d, zs, n1, f0, jf = ("C6", 0, 64), ("C6", 64, 128), ("C7", 64, 128), ("C7", 0, 64), ("f0", 0, 64), ("jf", 0, 64)
         pe([times(d, ONE, row(t, 1)), times(d, NEG, row(t, 0))], d)
-        first = [a] + quarters(b) if SPLIT0 else [a, b]
+        first = ([a] if t == 1 or not PE_SPEED else quarters(a)) + quarters(b)
         second = [a] + quarters(b) if SPLIT1 else [a, b]
         for c in first:
-            diff(0, c); size(0, c)
-        for n, c in enumerate(first):
-            near(0, c, NEAR0[n])
+            diff(0, c)
+        for n, c in enumerate([a] + quarters(b)):
+            size(0, c); near(0, c, NEAR0[n])
         pe(wrap(n0, ("NB", 0, W)), n0)
         ts(f0, n0, 1024.0, ALU.is_lt)
         tt(d, d, f0, ALU.mult)
@@ -525,29 +617,56 @@ def rank_program(g, core, T, topo):
                 tt(xx(c), xx(c), at(k, c), ALU.mult)
             for c in parts:
                 tt(at(tp, c), xx(c), at("dv", c), ALU.mult)
+            on_pe = PE_SPEED and parts == [VIS, N1]
+            if on_pe:
+                pe([times(at(VP, H1), S16, at(v, H1)) if v == "vb" else exact(at(VP, H1), at(v, H1))], at(VP, H1), True, False)
             for c in parts:
-                tt(at(VP, c), at(VP, c), at(tp, c), ALU.add)
+                if on_pe:
+                    pe([exact(at(VP, c), at(tp, c))], at(VP, c), False, c == N1)
+                elif PE_Q1 and c == Q1 and t != 2:
+                    pe([times(at(VP, c), S16, at(v, c)) if v == "vb" else exact(at(VP, c), at(v, c))], at(VP, c), True, False)
+                    pe([exact(at(VP, c), at(tp, c))], at(VP, c), False, True)
+                else:
+                    tt(at(VP, c), at(VP, c), at(tp, c), ALU.add)
+            if not on_pe:
+                move(parts)
+
+        def move(parts):
             for c in parts:
                 tt(at("q", c), at(VP, c), at(q, c), ALU.add)
 
         def copies(c):
-            if t < 4:
-                twin("S", at("q2", c), at("q", c))
+            for x in (quarters(c) if PE_SPEED and c == H0 else [c]) if t < 4 else []:
+                twin("S", at("q2", x), at("q", x))
 
         def keep(parts, c):
             for x in parts:
                 act(at(kl, x), xx(x), scale=unit)
+                ops[-1]["r"].append(at(tp, x))
             if t < 4:
                 act(at("v", c), at(VP, c))
+                ops[-1]["r"].append(at("q", c))
                 twin("G", at("v2", c), at("v", c))
+
+        def both():
+            push(quarters(H1))
+            if not PE_SPEED:
+                copies(H1)
+            if t < 4 and not again:
+                advance(t, mu)
+            push(quarters(H0)); copies(H0)
+            if PE_SPEED:
+                move(quarters(H1)); copies(H1)
         a, b = H1, H0
         if again:
-            dv(a)
-            for c in (H0, H1):
+            def product(c):
                 tt(at("ge", c), at("PY", c), at("tp1", c), ALU.mult)
+            since = len(ops)
+            dv(a); product(VIS); pa(VIS, "S"); pa(N1, "S"); mask(VIS); mask(N1); dv(b); product(N1)
+            pa(Q1, "S"); pa(Q0, "S"); mask(Q1); mask(Q0); product(Q1); product(Q0)
+            in_turn(since)
             add_g("ge", ALL)
-            pa(a, "S"); dv(b); mask(a); pa(b, "S"); mask(b)
-            push(quarters(a)); copies(a); push(quarters(b)); copies(b); keep([a], a); keep([b], b)
+            both(); keep([a], a); keep([b], b)
             return
         if t == 2:
             send(at("q", VIS), "lq%d" % shot, True)
@@ -555,7 +674,7 @@ def rank_program(g, core, T, topo):
         publish(t); dv(a); partner(a); dv(b); pa(a, "S"); partner(b)
         if t == 1:
             later_rows()
-            for c in (a, b):
+            for c in (b,) if PE_SPEED else (a, b):
                 act(at(VP, c), at("vb", c), scale=0.0625)
         mutual(VIS); mask(VIS); mutual(N1); mask(N1); pa(b, SIGN_B)
         if t == 2:
@@ -577,16 +696,245 @@ def rank_program(g, core, T, topo):
             keep([N1], N1); keep([Q1, Q0], b)
             act(at("v", VIS), rot)
             twin("G", at("v2", VIS), at("v", VIS))
-            act(at(VP, VIS), at("v", VIS))
+            if not PE_SPEED:
+                act(at(VP, VIS), at("v", VIS))
             return
         mutual(b); mask(Q1); mask(Q0)
-        push([VIS, N1]); copies(a)
-        if t < 4:
-            advance(t, mu)
-        push([Q1, Q0]); copies(b); keep([VIS, N1], a); keep([Q1, Q0], b)
+        both(); keep([VIS, N1], a); keep([Q1, Q0], b)
         if t == 1:
             for c in (a, b):
                 gact(at("sq1", c), ("D", 0, 2 * W), offs(jl, c, 64), ACT.Sign)
+                ops[-1]["r"].append(xx(Q0))
+            turn(at("PY", VIS), "lk", True, z="zz")
+            act(at("ka", VIS), at("PY", VIS))
+
+    def forward(shot, t, VP, X):
+        again = shot == 1 and t == 1
+        lst, jl, kl, tp = "l%d" % t, "j%d" % t, "kl%d" % t, "tp%d" % t
+        k = "kh" if t <= 2 else "ka"
+        q, q2 = ("qb", "qb2") if t == 1 else ("q", "q2")
+        v, v2 = ("v", "v2") if t > 1 else ("vs", "v2") if again else ("vb", "vb2")
+        unit = 16.0 if v == "vb" else 1.0
+        kj, mu = ("kj1", "mu1") if t == 1 else ("kj", "mu")
+        n0, d, zs, n1, f0, jf = ("C6", 0, 64), ("C6", 64, 128), ("C7", 64, 128), ("C7", 0, 64), ("f0", 0, 64), ("jf", 0, 64)
+        D = "D1" if t == 1 else "D"
+
+        def diff(w, c):
+            gt(at(D, c, W * w), full(q), offs(lst, c, 64 * w), at(q2, c), ALU.subtract)
+            act(at("AB", c, W * w), at(D, c, W * w), ACT.Abs, scale=ABS_SCALE)
+
+        def near(w, c, e="V"):
+            if e == "V":
+                ts(at("NB", c, W * w), at("AB", c, W * w), NEAR, ALU.is_le, 0.5, ALU.subtract)
+            else:
+                act(at("NB", c, W * w), at("AB", c, W * w), ACT.Sign, scale=-1.0, bias=TIE)
+
+        def publish(e):
+            tt(("cw", 0, 64), n1, jf, ALU.min)
+            ts((jl, 64, 128), zs, 1.0, ALU.mult)
+            for c in (H1, H0):
+                for x in range(c[0], c[1], 64):
+                    pe([(T.PY[:, x:x + 64], T.wr[:, 2 * x:2 * x + 128], T.cw[:], [("cw", 0, 64), ("wr", 0, 2048)], 64)],
+                       ("PY", x, x + 64))
+                told[:] = [len(ops) - 1]
+                if c == H1 or e == "S":
+                    act(at("R", c), at("PY", c))
+
+        def behind():
+            rest = [i for i in range(told[0] + 1, len(ops)) if ops[i]["e"] == "P"]
+            masks = [i for i in rest if ops[i].get("mask")]
+            turns = [told[0], rest[0]] + [masks[n] for n in (0, 3, 6, 9, 1, 4, 2, 5, 7, 10, 8, 11)]
+            if t == 2:
+                turns = [told[0], rest[0]] + [masks[n] for n in (0, 3, 1, 2, 4, 5, 6, 9, 7, 8, 10, 11)]
+            for a, b in zip(turns, turns[1:]):
+                ops[b]["after"] = a
+            for i in rest:
+                if ops[i].get("after") is None:
+                    ops[i]["after"] = rest[0]
+
+        def column():
+            zp, hb = ("C6", 128, 192), ("hb", 0, 64)
+            pe([times(zp, K1, hb), times(zp, NEG, hb), times(zp, ONE, ("j64", 0, 64))], zp)
+            return lambda: ts(("jr", 0, 64), zp, 1023.0 * 160.0, ALU.add)
+
+        def xx(c):
+            return at("PY" if c in (VIS, Q1) else X, c)
+
+        def dv(c):
+            gt(at("dv", c), full(v), offs(jl, c), at(v2, c), ALU.subtract)
+
+        def pa(c):
+            if again:
+                pe([times(half6(c), ONE, at("sq1", c))], half6(c))
+                ops[-1]["after"] = max(i for i in range(since) if ops[i]["e"] == "P")
+                tt(at("pa", c), half6(c), at("dv", c), ALU.mult)
+            else:
+                gt(at("pa", c), (D, 0, 2 * W), offs(jl, c, 64), at("dv", c), ALU.mult)
+            act(at("sa", c), at("pa", c), ACT.Sign, scale=-1.0)
+
+        def partner(c):
+            gact(at(kj, c), full(k), offs(jl, c))
+
+        def mutual(c):
+            gt(at(mu, c), full("R"), offs("jr", c), at("ir", c), ALU.is_equal)
+
+        def mask(c):
+            early, late = (mu, "sa") if again else ("sa", mu)
+            pe([times(xx(c), ONE, at(kj, c))], xx(c), True, False)
+            pe([times(xx(c), ONE, at(early, c))], xx(c), False, False)
+            pe([times(xx(c), ONE, at(late, c))], xx(c), False, True)
+            for o in ops[-3:]:
+                o["mask"] = True
+            act(xx(c), xx(c), ACT.Relu, scale=1.0 / unit, bias=-2.0 / unit)
+
+        def kk(*parts):
+            for c in parts:
+                tt(xx(c), xx(c), at(k, c), ALU.mult)
+
+        def push(*parts):
+            for c in parts:
+                tt(at(tp, c), xx(c), at("dv", c), ALU.mult)
+
+        def speed(*parts):
+            for c in parts:
+                tt(at(VP, c), at(VP, c), at(tp, c), ALU.add)
+
+        def speed_pe(c):
+            pe([times(at(VP, c), S16, at(v, c)) if v == "vb" else exact(at(VP, c), at(v, c))], at(VP, c), True, False)
+            for x in quarters(c):
+                pe([exact(at(VP, x), at(tp, x))], at(VP, x), False, x == quarters(c)[-1])
+
+        def move(*parts):
+            for c in parts:
+                tt(at("q" if t < 4 else VP, c), at(VP, c), at(q, c), ALU.add)
+
+        def copies(*parts):
+            for c in parts if t < 4 else []:
+                twin("G" if c == Q0 and Q0_G else "S", at("q2", c), at("q", c))
+
+        def keep(parts, c):
+            for x in parts:
+                act(at(kl, x), xx(x), scale=unit)
+                ops[-1]["r"].append(at(tp, x))
+            if t < 4:
+                act(at("v", c), at(VP, c))
+                ops[-1]["r"].append(at("q", c))
+                twin("G", at("v2", c), at("v", c))
+
+        def finish():
+            first = len(ops)
+            relist = advance(t, mu) if t < 4 and not again else None
+            kk(VIS, N1); push(VIS, N1)
+            if (shot, t) in PE_STEPS:
+                for x in quarters(ON_PE):
+                    pe([exact(at(VP, x), at(tp, x))], at(VP, x), False, x == quarters(ON_PE)[-1])
+                if relist:
+                    mine = [i for i in range(first, len(ops)) if ops[i]["e"] == "P"]
+                    turns = [mine[0], mine[4], mine[2]] + mine[5:] + [mine[3]]
+                    for a, b in zip(turns, turns[1:]):
+                        ops[b]["after"] = a
+                kk(Q1, Q0); push(Q1, Q0); speed(Q1, Q0); move(Q1, Q0); copies(Q1, Q0)
+                if ON_PE == VIS:
+                    speed(N1)
+                move(VIS, N1); copies(H1)
+                if relist:
+                    relist()
+            else:
+                speed(VIS, N1); move(VIS, N1); copies(H1); kk(Q1, Q0); push(Q1, Q0)
+                if relist:
+                    relist()
+                speed(Q1, Q0); move(Q1, Q0); copies(H0)
+
+        def preload(c):
+            pe([times(at(VP, c), S16, at(v, c)) if v == "vb" else exact(at(VP, c), at(v, c))], at(VP, c), True, False)
+        since, told = len(ops), []
+        if (shot, t) in PE_STEPS:
+            can_wait(preload, ON_PE)
+            if t == 1 and ON_PE == VIS:
+                can_wait(act, at(VP, N1), at(v, N1), scale=1.0 / unit)
+        if again:
+            def product(c):
+                tt(at("ge", c), at("PY", c), at("tp1", c), ALU.mult)
+            dv(H1); product(VIS); pa(VIS); pa(N1); mask(VIS); mask(N1); dv(H0); product(Q1)
+            pa(Q1); pa(Q0); mask(Q1); mask(Q0); product(Q0); product(N1)
+            add_g("ge", ALL)
+            finish(); keep([VIS, N1], H1); keep([Q1, Q0], H0)
+            in_turn(since)
+            return
+        if t == 2:
+            send(at("q", VIS), "lq%d" % shot, True)
+        a, b1, b2 = (H0, N1, VIS) if t == 3 or (shot, t - 1) in PE_STEPS else (H1, Q1, Q0)
+        a1, a2 = quarters(a)
+        pe([times(d, ONE, row(t, 1)), times(d, NEG, row(t, 0))], d)
+        if (shot, t - 1) in PE_STEPS:
+            diff(0, Q1); diff(0, Q0)
+        else:
+            diff(0, a)
+        diff(0, b1); diff(0, b2); diff(1, a1); near(0, a); near(0, b1); near(0, b2)
+        pe(wrap(n0, ("NB", 0, W)), n0)
+        if (shot, t) in PE_STEPS:
+            ops[-1]["after"] = since
+        if t == 1:
+            rest = later_rows()
+        diff(1, a2); diff(1, b1); diff(1, b2)
+        ts(f0, n0, 1024.0, ALU.is_lt)
+        pe([times(zs, ONE, ("iw", 0, 64)), times(zs, K1, f0)], zs)
+        near(1, a)
+        tt(d, d, f0, ALU.mult)
+        near(1, b1)
+        tt(jf, d, row(t, 0), ALU.add)
+        near(1, b2)
+        ts((jl, 0, 64), jf, 1.0, ALU.mult)
+        ts(("hb", 0, 64), jf, -1.0 / 16.0, ALU.mult, 15.0 / 32.0 - 160.0, ALU.add)
+        ts(("j64", 0, 64), jf, 64.0, ALU.mult)
+        pe([times(n1, ONE, ("top", 0, 64)), times(n1, FAR, f0)], n1, True, False)
+        pe(wrap(n1, ("NB", W, 2 * W)), n1, False, True)
+        if t == 1:
+            rest()
+        if t == 2:
+            rot = at("PY", VIS)
+            dv(VIS); partner(H1); publish("V"); jr = column(); dv(N1); pa(VIS)
+            ts(at("R", H0), at("PY", H0), 1.0, ALU.mult)
+            pa(N1); jr(); can_wait(partner, H0)
+            mutual(VIS); mask(VIS); mutual(N1); mask(N1); dv(H0); kk(VIS); kk(N1); push(VIS); push(N1)
+            leave("vo", VP, tp)
+            send(("vo", 0, 256), "lv%d" % shot, True)
+            ops[-2]["r"].append(("voh", 0, 128))
+            pa(H0); mutual(Q1); mask(Q1); mutual(Q0); mask(Q0)
+            masked = len(ops) + 3
+            relist = advance(t, mu)
+            speed(N1); move(N1); kk(Q1, Q0); push(Q1, Q0); speed(Q1, Q0); move(Q1, Q0); relist()
+            copies(N1, Q1, Q0)
+            act(at(kl, VIS), xx(VIS))
+            ops[fetch("qov", -NV, rot, "lq%d" % shot, True)]["after"] = masked
+            turned = arrive("q", rot, "lv%d" % shot, True, "qov", -NV)
+            came = len(ops) - 3
+            act(at("q2", VIS), at("q", VIS))
+            keep([N1], N1); keep([Q1, Q0], H0)
+            act(at("v", V1), turned)
+            act(at("v", V4), ("lv%d" % shot, 128, 256))
+            twin("G", at("v2", VIS), at("v", VIS))
+            if (shot, 3) not in PE_STEPS:
+                act(at(VP, VIS), at("v", VIS))
+            in_turn(since); behind()
+            for c in (H0, H1) if shot == 0 else ():
+                pe([(ap(at(X, c)), T.wa[0:8, :], T.am[0:8, c[0]:c[1]], [("wa", 0, 128), full("am")], 512)], at(X, c))
+                ops[-1]["after"] = came
+                act(at("amr", c), at(X, c))
+            return
+        dv(H1); partner(H1); publish("S"); jr = column(); dv(H0); pa(H1); can_wait(partner, H0)
+        if not EARLY_MU:
+            jr(); pa(H0)
+        mutual(VIS); mask(VIS); mutual(N1); mask(N1)
+        if EARLY_MU:
+            pa(H0)
+        if MU_Q:
+            mutual(Q1); mask(Q1); mutual(Q0); mask(Q0)
+        else:
+            mutual(H0); mask(Q1); mask(Q0)
+        finish(); keep([VIS, N1], H1); keep([Q1, Q0], H0)
+        in_turn(since); behind()
+        if t == 1:
             turn(at("PY", VIS), "lk", True, z="zz")
             act(at("ka", VIS), at("PY", VIS))
 
@@ -596,9 +944,8 @@ def rank_program(g, core, T, topo):
     def backward(shot, VP, X):
         rot = ("C7", 256, 512)
         for c in (H1, H0):
-            pe([(ap(half6(c)), T.wa[0:8, :], T.am[0:8, c[0]:c[1]], [("wa", 0, 128), full("am")], 512)], half6(c))
             for x in quarters(c):
-                tt(at("A", x), at("q", x), half6(x), ALU.subtract)
+                tt(at("A", x), at(VP, x), at("amr", x), ALU.subtract)
         send(at("A", VIS), "la%d" % shot, False)
         wins = {4: "A", 3: "av1", 2: "av2", 1: "av1"}
         unit = UNITS[shot]
@@ -607,108 +954,183 @@ def rank_program(g, core, T, topo):
             return X if t % 2 == 0 else "PY"
 
         def av(t, c):
-            p = PE_BACK.get(t, (0, 0))
-            return at("C6", c, -p[0]) if p[0] <= c[0] < p[1] else at(VP, c)
+            return ("C7" if t % 2 else "C6", 0, 256) if c == Q1 and t in Q1_PE else at(VP, c)
 
         def pull(t, c, fine=False):
-            act(at(VP, c), at(wins[t], c), scale=unit if t == 1 else 1.0)
-            for x in (quarters(c) if fine else [c]):
+            kept = c == H0 and t > 1 and t + 1 in Q1_PE
+            act(at(VP, Q0 if kept else c), at(wins[t], Q0 if kept else c), scale=unit if t == 1 else 1.0)
+            for x in (quarters(c) if fine or FINE else [c]):
                 gact(at("ag", x), full(wins[t]), offs("j%d" % t, x), scale=unit if t == 1 else 1.0)
             for x in quarters(c):
-                tt(at(da(t), x), at("ag", x), at(VP, x), ALU.subtract)
+                tt(at(da(t), x), at("ag", x), av(t + 1, x) if kept else at(VP, x), ALU.subtract)
             for x in quarters(c):
                 tt(at("tb", x), at(da(t), x), at("kl%d" % t, x), ALU.mult)
 
         def add(t, c):
-            if PE_BACK.get(t) == c:
-                pe([exact(av(t, c), at(wins[t], c), 256 + 128 * shot if t == 1 else 0)], av(t, c), True, False)
-                for x in quarters(c):
-                    pe([exact(av(t, x), at("tb", x))], av(t, x), False, x == quarters(c)[-1])
-            else:
-                for x in quarters(c):
+            for x in quarters(c):
+                if x == Q1 and t in Q1_PE:
+                    pe([exact(av(t, x), at(wins[t], x), 256 + 128 * shot if t == 1 else 0)], av(t, x), True, False)
+                    pe([exact(av(t, x), at("tb", x))], av(t, x), False, t == 1)
+                else:
                     tt(at(VP, x), at(VP, x), at("tb", x), ALU.add)
 
         def drift(t, c):
             for x in quarters(c):
-                tt(at(wins[t - 1], x), av(t, x), at("A", x), ALU.add)
+                if x == Q1 and t in Q1_PE:
+                    pe([exact(av(t, x), at("A", x))], av(t, x), False, True)
+                    act(at(wins[t - 1], x), av(t, x))
+                else:
+                    tt(at(wins[t - 1], x), av(t, x), at("A", x), ALU.add)
 
         def gain(t, c):
             out = {4: at("gg", c), 3: at("gg", c, 256 if c == VIS else 1280), 2: at("gb", c), 1: at("ge", c)}[t]
             tt(out, at(da(t), c), at("tp%d" % t, c), ALU.mult)
+        def aside(out, src, fn=ACT.Copy, scale=1.0):
+            last = max(i for i, o in enumerate(ops) if o["w"] and o["w"][0][0] == "ag")
+            for x in (VIS, N1, Q1, Q0):
+                act(at(out, x), at(src, x), fn, scale=scale)
+                ops[-1]["after"] = last
+        def step(t, order, late):
+            scale, since = unit if t == 1 else 1.0, len(ops)
+
+            def load(x):
+                if not (x == Q1 and t > 1 and t + 1 in Q1_PE):
+                    act(at(VP, x), at(wins[t], x), scale=scale)
+            for x in order:
+                if x not in late:
+                    load(x)
+            since = len(ops)
+            for x in order:
+                if x in late:
+                    load(x)
+                if x == order[0] and (t, shot) in V_GATHERS:
+                    o, w, of = at("ag", x), full(wins[t]), offs("j%d" % t, x)
+                    op("V", lambda o=o, w=w, of=of: V.tensor_scalar(ap(o), ap(w).indirect(ap(of)), scale, None, ALU.mult),
+                       [w, of], [o], 256 * GATHER + 55)
+                else:
+                    gact(at("ag", x), full(wins[t]), offs("j%d" % t, x), scale=scale)
+            in_turn(since, "S")
+            for pair in (order[:2], order[2:]):
+                for x in pair:
+                    tt(at(da(t), x), at("ag", x), av(t + 1, x) if t > 1 else at(VP, x), ALU.subtract)
+                for x in pair:
+                    tt(at("tb", x), at(da(t), x), at("kl%d" % t, x), ALU.mult)
+                for x in pair:
+                    if (t, x) == (3, VIS):
+                        leave("ao", VP, "tb")
+                        send(("ao", 0, 256), "lw%d" % shot, False)
+                        ops[-2]["r"].append(("aoh", 0, 128))
+                        fetch("A", 0, rot, "la%d" % shot, False)
+                    else:
+                        add(t, x)
+                for x in pair:
+                    if t > 1 and (t, x) != (3, VIS):
+                        drift(t, x)
+            if CHAIN:
+                in_turn(since)
+        step(4, (VIS, N1, Q1, Q0), (Q1, Q0))
         if shot == 0:
-            act(full("G"), full("kh"), ACT.Square)
-            act(full("G"), full("G"), scale=-1.0)
-        pull(4, H1, True); add(4, H1); pull(4, H0); add(4, H0); drift(4, H0); drift(4, H1)
-        gain(4, H1)
-        if shot == 0:
-            newton()
-        pull(3, VIS)
-        tt(("ao", 0, 256), at(VP, VIS), at("tb", VIS), ALU.add)
-        send(("ao", 0, 256), "lw%d" % shot, False)
-        turn(rot, "la%d" % shot, False)
-        act(at("A", VIS), rot)
-        pull(3, N1); add(3, N1); pull(3, H0); add(3, H0); drift(3, H0); drift(3, N1)
-        gain(3, VIS)
-        send(("gg", NV, NV + 512), "lg%d" % shot, False)
-        gain(3, N1); gain(3, H0)
-        turn(rot, "lw%d" % shot, False)
-        tt(at("av2", VIS), rot, at("A", VIS), ALU.add)
-        gain(4, H0)
-        add_g("gg", NAT, 1280)
-        add_g("gg", NAT)
-        pull(2, H0, True); add(2, H0); pull(2, H1); add(2, H1); drift(2, H1); drift(2, H0)
-        gain(2, H0); gain(2, H1)
-        turn(rot, "lg%d" % shot, False, pieces=2)
-        if shot == 0:
+            can_wait(newton)
+            aside("G", "kh", ACT.Square)
+            aside("G", "G", scale=-1.0)
+        else:
+            turn(rot, "lg0", False, pieces=2)
             act(("gr", 0, 256), rot)
             add_g("gr", VIS, -NV)
+            aside("rk", "kn", scale=-2.0)
+            dma("G", T.rk[:], T.ou[:], [full("ou"), full("rk")], [full("rk")], add=True, lat=3500.0)
+            aside("ov", "vs", scale=16.0)
+        step(3, (VIS, N1, Q1, Q0), (Q1, Q0))
+        last = max(i for i, o in enumerate(ops) if o["w"] and o["w"][0][0] == "ag")
+        for c in (VIS, N1, Q1, Q0) if shot == 0 else ():
+            gact(at("sq1", c), ("D1", 0, 2 * W), offs("j1", c, 64), ACT.Sign)
+            ops[-1]["after"] = last
+        arrive("av2", rot, "lw%d" % shot, False, "A", 0)
+        gain(4, VIS); gain(3, VIS)
+        send(("gg", NV, NV + 512), "lg%d" % shot, False)
+        for c in (N1, Q1, Q0):
+            gain(4, c)
+        for c in (N1, Q1, Q0):
+            gain(3, c)
+        add_g("gg", NAT, 1280)
+        add_g("gg", NAT)
+        step(2, (Q1, Q0, N1, VIS), (VIS,))
+        for c in (VIS, N1, Q1, Q0):
+            gain(2, c)
+        if shot == 0:
             add_g("gb", ALL)
         else:
+            if TAIL_PE:
+                pe([exact(half6(H0), at("G", H0))], half6(H0), True, False)
+                pe([exact(half6(H0), at("gb", H0))], half6(H0), False, False)
+            else:
+                add_g("gb", H0)
+            turn(rot, "lg1", False, pieces=2)
             tt(at("gb", VIS), rot, at("gb", VIS), ALU.add)
-            add_g("gb", H0)
             add_g("gb", H1)
-        act(full("tp1"), full("tp1"), scale=1.0 / unit)
+        aside("tp1", "tp1", scale=1.0 / unit)
+        if shot == 0:
+            aside("vs", "vb", scale=0.0625)
+        v0 = "ov" if shot else "vs"
 
-        def settle(c):
-            v0 = "ov" if shot else "vs"
+        def settle(c, on_pe):
+            if on_pe:
+                pe([exact(at(VP, c), at(v0, c))], at(VP, c), True, False)
             for x in quarters(c):
-                ts(av(1, x), av(1, x), CLIP * unit, ALU.min, -CLIP * unit, ALU.max)
+                ts(at("cl", x) if on_pe else av(1, x), av(1, x), CLIP * unit, ALU.min, -CLIP * unit, ALU.max)
             for x in quarters(c):
-                tt(at(v0, x), at(v0, x), av(1, x), ALU.subtract)
+                if on_pe:
+                    pe([exact(at(VP, x), at("cl", x), 512)], at(VP, x), False, x == quarters(c)[-1])
+                else:
+                    tt(at(v0, x), at(v0, x), av(1, x), ALU.subtract)
+            if on_pe:
+                act(at(v0, c), at(VP, c))
             if shot == 0:
-                act(at("v2", c), at("vs", c))
+                act(at("v2", c), at(VP if on_pe else "vs", c))
             else:
                 dma("Y", T.yv[:, c[0]:c[1]], ap(at("ov", c)), [at("ov", c)], [])
 
         def result(c, e):
-            tt(at("ou", c), at(X if c == H0 else "PY", c), at("rk", c), ALU.mult)
+            for src, alu in (("tp1", ALU.mult), ("G", ALU.add)):
+                for x in quarters(c):
+                    tt(at("PY", x), at("PY", x), at(src, x), alu)
+            for x in quarters(c):
+                tt(at("ou", x), at("PY", x), at("rk", x), ALU.mult)
             dma(e, T.yg[:, c[0]:c[1]], ap(at("ou", c)), [at("ou", c)], [])
         if shot == 0:
-            pull(1, H0, True); add(1, H0); pull(1, H1); add(1, H1); settle(H1); settle(H0)
-            for c in (H1, H0):
+            step(1, (Q1, Q0, N1, VIS), (N1, VIS)); settle(H0, False); settle(H1, False)
+            for c in [H0] + ([] if (1, 1) in PE_STEPS else [H1]):
                 act(at(VP, c), at("vs", c))
         else:
-            act(full("ov"), full("vs"), scale=16.0)
-            pe([exact(at(X, H0), at("G", H0))], at(X, H0), True, False)
-            pull(1, H0, True); add(1, H0); gain(1, H0)
-            pe([exact(at(X, H0), at("ge", H0))], at(X, H0), False, True)
-            pull(1, H1); add(1, H1); settle(H1)
-            tt(at("PY", H1), at("PY", H1), at("tp1", H1), ALU.mult)
-            tt(at("PY", H1), at("PY", H1), at("G", H1), ALU.add)
-            result(H1, "S"); settle(H0); result(H0, "S")
+            step(1, (Q1, Q0, N1, VIS), (N1, VIS))
+            if TAIL_PE:
+                for x in (Q1, Q0):
+                    gain(1, x)
+                pe([exact(half6(H0), at("ge", H0))], half6(H0), False, True)
+            settle(H0, False); settle(H1, False)
+            result(H1, "S")
+            if TAIL_PE:
+                for x in (Q1, Q0):
+                    tt(at("ou", x), half6(x), at("rk", x), ALU.mult)
+                dma("Y", T.yg[:, 0:512], ap(at("ou", H0)), [at("ou", H0)], [])
+            else:
+                result(H0, "Y")
 
     def newton():
-        act(full("vs"), full("vb"), scale=0.0625)
         for c in (H1, H0):
-            act(("C7", 0, 512), at("kn", c), ACT.Square)
-            tt(at("ou", c), ("C7", 0, 512), at("kh", c), ALU.mult)
-        act(full("rk"), full("kn"), scale=-2.0)
-        dma("G", T.rk[:], T.ou[:], [full("ou"), full("rk")], [full("rk")], add=True, lat=3500.0)
+            act(at("PY", c), at("kn", c), ACT.Square)
+            for x in quarters(c):
+                tt(at("ou", x), at("PY", x), at("kh", x), ALU.mult)
 
     for shot in (0, 1):
         for t in (1, 2, 3, 4):
             forward(shot, t, "PA", "PB")
         backward(shot, "PA", "PB")
+    for o in ops:
+        name = o["w"][0][0].rstrip("01234") if o["w"] else ""
+        if (o["e"] == "S" and name in ("kl", "v", "sq", "ka", "st", "cc", "qov", "G", "vs", "ov", "rk", "tp", "gr", "A")
+                or o["e"] == "V" and name in ("gg", "gb") or o["e"] == "G" and name in ("v", "G", "rk")):
+            o["lazy"] = True
     if not ORDER:
         ORDER.extend(arrange(ops))
     emit([ops[i] for i in ORDER], g, T)

from concourse.mybir import AluOpType, ActivationFunctionType

ALU = AluOpType
ACT = ActivationFunctionType
W, NV = 1024, 768
H1, H0 = (512, 1024), (0, 512)
VIS, N1, NAT, ALL = (768, 1024), (512, 768), (0, 768), (0, 1024)
ABS_SCALE = 167.0 / 128.0
NEAR = 250.0 / 256.0
TIE = 501.0 / 512.0
CLIP = 0.1875 * 16.0
UNITS = (1.0 / 256.0, 1.0 / 16.0)

Q1, Q0 = (256, 512), (0, 256)
SPLIT0, SPLIT1, NEAR0, NEAR1, R_COPY, SIGN_B = True, True, "VVV", "SVV", "S", "S"
PE_LOAD, FINE, PE_SPEED, PE_SETTLE, PE_Q1 = False, True, True, False, False
AGAIN = "SS"
CHAIN = False
PE_STEPS = ((0, 1), (0, 3), (0, 4), (1, 1), (1, 3), (1, 4))
V_GATHERS = ((2, 0), (2, 1), (4, 1), (1, 0))
Q1_PE = (2,)
ON_PE = H1

F, B, HF, I32, U16 = "float32", "bfloat16", "float16", "int32", "uint16"


def sb(cols, dt):
    return ("sbuf", [128, cols], dt)


SCRATCH = {
    "PA": ("psum", [128, 1024], F), "PB": ("psum", [128, 1024], F), "PY": ("psum", [128, 1024], F),
    "C6": ("psum", [128, 512], F), "C7": ("psum", [128, 512], F),
    "ci": sb(W, I32), "ch": sb(W, HF), "ones": sb(2048, B), "big": sb(16, B), "cz": sb(896, B), "zz": sb(896, B),
    "cf": sb(640, F), "zf": sb(640, F), "bc": sb(720, B), "bn": sb(144, B), "bl": sb(8, B), "wr": sb(2048, B),
    "wa": sb(128, B), "iw": sb(64, HF), "iw0": sb(64, F), "pi": sb(4, I32), "pj": sb(4, I32), "pf": sb(4, F),
    "top": sb(64, B), "ee": sb(448, B), "cc": sb(256, HF), "uu": sb(512, HF),
    "mm": sb(512, HF),
    "f0": sb(64, B), "fl": sb(64, B), "jf": sb(64, F), "cw": sb(64, HF), "hb": sb(64, B), "j64": sb(64, HF), "jr": sb(64, U16),
    "D": sb(2048, F), "D1": sb(2048, F), "AB": sb(2048, B), "NB": sb(2048, B),
    "qov": sb(256, F), "gr": sb(256, F), "vo": sb(256, F), "ao": sb(256, F), "gg": sb(2048, F), "lk": sb(256, B),
}
for _n in "qb qb2 vb vb2 kh ka am amr pa sa kj kj1 mu mu1 sq1".split():
    SCRATCH[_n] = sb(W, B)
for _n in "ir R q q2 v v2 vs dv A av1 av2 ag tb cl gb ge G kn rk ov ou".split():
    SCRATCH[_n] = sb(W, F)
for _t in "1234":
    SCRATCH["st" + _t], SCRATCH["l" + _t], SCRATCH["j" + _t] = sb(256, HF), sb(128, U16), sb(128, U16)
    SCRATCH["kl" + _t], SCRATCH["tp" + _t] = sb(W, F), sb(W, F)
for _s in (0, 1):
    for _n, _c in (("lq", 256), ("lv", 256), ("la", 256), ("lw", 256), ("lg", 512)):
        SCRATCH[_n + str(_s)] = sb(_c, F)
PSUM = ("PA", "PB", "PY", "C6", "C7")
ENG = ("V", "S", "P", "G", "Y")
NDMA, NREM = 24, 11
SEMAPHORES = (["e" + e for e in ENG] + ["dm%d" % i for i in range(NDMA)]
              + ["ls%d" % i for i in range(NREM)] + ["ar%d" % i for i in range(NREM)])

CYCLE, PE_CYCLE, HOP, SAME = 0.83, 0.6, 250.0, 250.0
GATHER = 1.56
ROUNDS = 2
LOOKS = (0.0, 0.15, 0.3, 0.5, 0.8)
SPAN = []
PICK = None
Q0_G = False
EARLY_MU = False
NEAR_A, MU_Q, EIGHTH, TAIL_PE = "V", True, False, True


def banks_of(o):
    return set((name, bk) for name, a, b in o["r"] + o["w"] if name in PSUM for bk in range(a // 512, (b - 1) // 512 + 1))


def arrange(ops):
    n = len(ops)
    hist, pred, succ, loose = {}, [set() for _ in ops], [[] for _ in ops], set()
    for i, o in enumerate(ops):
        touch = [(r, False) for r in o["r"]] + [(r, True) for r in o["w"]]
        for (name, a, b), wr in touch:
            pred[i].update(m for a2, b2, wr2, m in hist.get(name, []) if a < b2 and a2 < b and (wr or wr2))
        for (name, a, b), wr in touch:
            h = hist.setdefault(name, [])
            if wr:
                h[:] = [x for x in h if not (a <= x[0] and x[1] <= b)]
            h.append((a, b, wr, i))
        if o["kind"] == "arr":
            pred[i].add(i - 1)
        pred[i].discard(i)
        if o.get("after") is not None and o["after"] not in pred[i]:
            pred[i].add(o["after"])
            loose.add((o["after"], i))
        for m in pred[i]:
            succ[m].append(i)

    def hop(m, i):
        if (m, i) in loose:
            return 0.0
        return 0.0 if ops[m]["e"] == ops[i]["e"] == "P" else SAME if ops[m]["e"] == ops[i]["e"] else HOP
    uses = [[(o["e"], None)] + [(bk, o["e"]) for bk in sorted(banks_of(o))] if o["e"] else [] for o in ops]

    def place(rank, back):
        before, after = (succ, pred) if back else (pred, succ)
        ready = [o["lat"] if back else 0.0 for o in ops]
        held, start, left = {}, [0.0] * n, [len(p) for p in before]
        free = [i for i in range(n) if not left[i]]
        while free:
            i = min(free, key=lambda k: rank[k])
            free.remove(i)
            s, c, moved = ready[i], ops[i]["c"], True
            while moved:
                moved = False
                for key, who in uses[i]:
                    pad = 0.0 if who is None else HOP
                    for a, b, w in held.get(key, []):
                        if s < b + pad and a < s + c + pad and (who is None or w != who):
                            s, moved = b + pad, True
            start[i] = s
            for key, who in uses[i]:
                held.setdefault(key, []).append((s, s + c, who))
            for k in after[i]:
                ready[k] = max(ready[k], s + c + (ops[k]["lat"] + hop(k, i) if back else ops[i]["lat"] + hop(i, k)))
                left[k] -= 1
                if left[k] == 0:
                    free.append(k)
        return start, max(start[i] + ops[i]["c"] + (0.0 if back else ops[i]["lat"]) for i in range(n))

    def run(rank, look):
        ready, start, left, until = [0.0] * n, [0.0] * n, [len(p) for p in pred], {}
        free = [i for i in range(n) if not left[i]]
        while free:
            soon = {}
            for i in free:
                s = ready[i]
                for key, who in uses[i]:
                    end, w = until.get(key, (0.0, who))
                    s = max(s, end + (0.0 if w == who else HOP))
                soon[i] = s
            i = min(free, key=lambda k: (soon[k], rank[k]))
            i = min((k for k in free if ops[k]["e"] == ops[i]["e"] and soon[k] <= soon[i] + look * ops[i]["c"]), key=lambda k: rank[k])
            free.remove(i)
            start[i] = soon[i]
            for key, who in uses[i]:
                until[key] = (start[i] + ops[i]["c"], who)
            for k in succ[i]:
                ready[k] = max(ready[k], start[i] + ops[i]["c"] + ops[i]["lat"] + hop(i, k))
                left[k] -= 1
                if left[k] == 0:
                    free.append(k)
        return start, max(start[i] + ops[i]["c"] + ops[i]["lat"] for i in range(n))
    tries = []
    for look in LOOKS:
        start, span = run(list(range(n)), look)
        for _ in range(ROUNDS):
            late, _span = place([(-start[i] - ops[i]["c"], -i) for i in range(n)], True)
            start, span = place([(-late[i] - ops[i]["c"], i) for i in range(n)], False)
            tries.append((span, start))
    rank = [float(i) for i in range(n)]
    for i in range(n - 1, -1, -1):
        if ops[i].get("lazy"):
            rank[i] = min([rank[k] for k in succ[i]] + [float(n)]) - 0.001
    start, span = place(rank, False)
    tries.append((span, start))
    for _ in range(ROUNDS):
        late, _span = place([(-start[i] - ops[i]["c"], -i) for i in range(n)], True)
        start, span = place([(-late[i] - ops[i]["c"], i) for i in range(n)], False)
        tries.append((span, start))
    best = min(tries) if PICK is None else tries[PICK]
    SPAN[:] = [round(x[0] / 1000, 1) for x in tries]
    return sorted(range(n), key=lambda i: (best[1][i], i))


def emit(ops, g, T):
    q = {"V": g.vector, "S": g.scalar, "P": g.tensor, "G": g, "Y": g.sync}
    hist, banks, clock, deps, order = {}, {}, {e: {} for e in ENG}, [], {e: 0 for e in ENG}
    know = []
    for n, o in enumerate(ops):
        e = o["e"]
        need = set()
        touch = [(r, False) for r in o["r"]] + [(r, True) for r in o["w"]]
        for (name, a, b), wr in touch:
            for (a2, b2, wr2, m) in hist.get(name, []):
                if a < b2 and a2 < b and (wr or wr2):
                    if not (e == "P" and ops[m]["e"] == "P"):
                        need.add(m)
        for bk in banks_of(o):
            m = banks.get(bk)
            if m is not None and ops[m]["e"] != e:
                need.add(m)
            banks[bk] = n
        for (name, a, b), wr in touch:
            h = hist.setdefault(name, [])
            if wr:
                h[:] = [x for x in h if not (a <= x[0] and x[1] <= b)]
            h.append((a, b, wr, n))
        need.discard(n)
        if e is None:
            deps.append([])
            know.append({("t", n): 1})
            continue
        ck = clock[e]
        waits = []
        for m in sorted(need, reverse=True):
            key, val = (("t", m), 1) if ops[m]["tok"] is not None else (ops[m]["e"], ops[m]["i"])
            if ck.get(key, 0) >= val:
                continue
            waits.append(m)
            for k2, v2 in know[m].items():
                if ck.get(k2, 0) < v2:
                    ck[k2] = v2
        deps.append(waits)
        kn = dict(ck)
        if o["tok"] is None:
            order[e] += 1
            o["i"] = order[e]
            kn[e] = o["i"]
        else:
            kn[("t", n)] = 1
        know.append(kn)
    wanted = set(m for ws in deps for m in ws)
    last = {}
    for n, o in enumerate(ops):
        if o["tok"] is None:
            last[o["e"]] = n
    wanted |= set(last.values())
    count = {e: 0 for e in ENG}
    val, waited = {}, set()
    for n, o in enumerate(ops):
        if o["tok"] is None and n in wanted:
            count[o["e"]] += 1
            val[n] = ("e" + o["e"], count[o["e"]])
        elif o["tok"] is not None:
            val[n] = o["tok"]
    for n, o in enumerate(ops):
        if o["e"] is None:
            continue
        for m in deps[n]:
            q[o["e"]].wait_ge(T.sem[val[m][0]], val[m][1])
            waited.add(m)
        ins = o["f"]()
        if o["kind"] == "dma":
            ins.then_inc(T.sem[o["tok"][0]], 16)
        elif o["kind"] == "op" and n in wanted:
            ins.then_inc(T.sem[val[n][0]], 1)
    for n, o in enumerate(ops):
        if (o["tok"] is not None and n not in waited) or (o["tok"] is None and last[o["e"]] == n):
            g.sync.wait_ge(T.sem[val[n][0]], val[n][1])


ORDER = []


def rank_program(g, core, T, topo):
    rank = T.rank_of(core)
    if rank is None:
        return
    n_ranks = len(T.cores)
    nxt, prv = T.cores[(rank + 1) % n_ranks], T.cores[(rank - 1) % n_ranks]
    ops = []
    cnt, opened = {"dma": 0, "rem": 0}, {}
    V, S, P = g.vector, g.scalar, g.tensor

    def op(e, f, r, w, cycles):
        fixed = {"V": 5.0, "S": 65.0, "G": 170.0, "P": 0.0}[e]
        c = cycles * PE_CYCLE if e == "P" else fixed + max(cycles, 64) * CYCLE
        ops.append({"e": e, "f": f, "r": r, "w": w, "tok": None, "kind": "op", "c": c, "lat": 0.0})

    def in_turn(since, e="V"):
        mine = [i for i in range(since, len(ops)) if ops[i]["e"] == e]
        for a, b in zip(mine, mine[1:]):
            ops[b]["after"] = a

    def can_wait(f, *args, **kw):
        since = len(ops)
        f(*args, **kw)
        for o in ops[since:]:
            o["lazy"] = True

    def dma(e, out, in_, r, w, add=False, lat=2500.0):
        qq = {"S": S, "Y": g.sync, "G": g}[e]
        f = (lambda: qq.dma_start(out, in_, accum_op=ALU.add)) if add else (lambda: qq.dma_start(out, in_))
        ops.append({"e": e, "f": f, "r": r, "w": w, "tok": ("dm%d" % cnt["dma"], 16), "kind": "dma",
                    "c": 1000.0 if e == "G" else 60.0, "lat": lat})
        cnt["dma"] += 1

    def send(src, land, forward):
        k = cnt["rem"]
        cnt["rem"] += 1
        dst, frm = (nxt, prv) if forward else (prv, nxt)
        rid, pid = topo.addr(dst, core)
        name, a, b = src
        ops.append({"e": "G", "kind": "rem", "r": [src], "w": [], "c": 700.0, "lat": 3500.0 if land[:2] in ("lv", "lw") else 5500.0,
                    "tok": ("ls%d" % k, len(topo.engines(core, dst))),
                    "f": lambda: g.remote_dma(T[land][:], T[name][:, a:b], T.sem["ar%d" % k], T.sem["ls%d" % k],
                                              pid, rid, topo.mask(core, dst))})
        ops.append({"e": None, "kind": "arr", "r": [], "w": [(land, 0, b - a)], "f": None, "c": 0.0, "lat": 0.0,
                    "tok": ("ar%d" % k, len(topo.engines(frm, core)))})

    def ap(x):
        return T[x[0]][:, x[1]:x[2]]

    def at(name, c, off=0):
        return (name, c[0] + off, c[1] + off)

    def full(name):
        return (name, 0, W)

    def wide(x):
        return x[2] - x[1]

    def short(*xs):
        return all(SCRATCH[x[0]][2] in (B, HF, U16) for x in xs)

    def tt(out, a, b, alu):
        op("V", lambda: V.tensor_tensor(ap(out), ap(a), ap(b), alu), [a, b], [out],
           wide(out) * (1 if a[0] in PSUM or b[0] in PSUM else 2))

    def ts(out, a, s1, o1, s2=None, o2=None):
        c = wide(out) * (0.5 if short(out, a) else 1)
        if o2 is None:
            op("V", lambda: V.tensor_scalar(ap(out), ap(a), s1, None, o1), [a], [out], c)
        else:
            op("V", lambda: V.tensor_scalar(ap(out), ap(a), s1, s2, o1, o2), [a], [out], c)

    def fill(out, value):
        op("V", lambda: V.memset(ap(out), value), [], [out], wide(out) * (0.5 if short(out) else 1))

    def offs(lst, c, off=0):
        return (lst, off + c[0] // 16, off + c[1] // 16)

    def gt(out, win, of, b, alu):
        op("V", lambda: V.tensor_tensor(ap(out), ap(win).indirect(ap(of)), ap(b), alu), [win, of, b], [out], wide(out) * GATHER + 55)

    def act(out, a, fn=ACT.Copy, scale=1.0, bias=0.0, more=0):
        op("S", lambda: S.activation(ap(out), ap(a), fn, bias=bias, scale=scale), [a], [out], wide(out) + more)

    def gact(out, win, of, fn=ACT.Copy, scale=1.0):
        op("S", lambda: S.activation(ap(out), ap(win).indirect(ap(of)), fn, scale=scale), [win, of], [out], wide(out) * GATHER)

    def select(out, a, pattern, cmp, base, cm, r, w, n):
        op("G", lambda: g.affine_select(out, a, pattern, cmp, 0.0, base, cm), r, w, 2 * n)

    def twin(e, out, a):
        if e == "S":
            act(out, a)
        else:
            select(ap(out), ap(a), [[0, wide(out)]], ALU.is_ge, 0, 0, [a], [out], wide(out))

    def pe(terms, out, first=True, last=True):
        def f():
            for n, (o_ap, l_ap, r_ap, _, _) in enumerate(terms):
                ins = P.matmul(o_ap, l_ap, r_ap, first and n == 0, last and n == len(terms) - 1)
            return ins
        bank = (out[0], out[1] // 512)
        if first:
            opened[bank] = out
        op("P", f, [x for t in terms for x in t[3]], [opened[bank] if last else out, ("sum" + bank[0], bank[1], bank[1] + 1)],
           sum(t[4] for t in terms))

    ONE, NEG, K1, M512, FAR, S16 = 0, 256, 384, 512, 640, 768

    def times(out, m, src):
        return (ap(out), T.zz[:, m:m + 128], ap(src), [src, ("zz", 0, 896)], max(64, wide(src)))

    def exact(out, src, m=0):
        return (ap(out), T.zf[:, m:m + 128], ap(src), [src, ("zf", 0, 640)], 4 * max(64, wide(src)))

    def wrap(out, src):
        return [(ap(out), T.bn[:, 15 - l:143 - l], T[src[0]][:, src[1] + l:src[2]:16], [src, ("bn", 0, 144)], 64) for l in range(16)]

    def turn(out, land, forward, z="zf", pieces=1, first=True):
        for h, s in ((0, 16 if forward else 112), (1, 64)):
            o = (out[0], out[1] + 128 * h, out[1] + 128 * h + 128)
            pe([(ap(o), T[z][:, 128 - s:256 - s], T[land][:, 256 * k + 128 * h:256 * k + 128 * h + 128],
                 [(land, 0, 256 * pieces), (z, 0, 256)], 128 * (4 if z == "zf" else 1)) for k in range(pieces)], o, first, first)

    V1, V4 = (768, 896), (896, 1024)

    def leave(out, a, b):
        tt((out, 0, 128), at(a, V1), at(b, V1), ALU.add)
        for p in (0, 64):
            op("V", lambda p=p: V.tensor_tensor(T[out][64 - p:128 - p, 128:256], T[a][p:p + 64, V4[0]:V4[1]],
                                                T[b][p:p + 64, V4[0]:V4[1]], ALU.add),
               [at(a, V4), at(b, V4)], [(out + "h", p, p + 64)], 128)

    def arrive(out, rot, land, forward, b, off):
        o = (rot[0], rot[1], rot[1] + 128)
        s = 16 if forward else 112
        pe([(ap(o), T.zf[:, 128 - s:256 - s], T[land][:, 0:128], [(land, 0, 256), ("zf", 0, 256)], 512)], o)
        tt(at(out, V4), (land, 128, 256), at(b, V4, off), ALU.add)
        tt(at(out, V1), o, at(b, V1, off), ALU.add)
        return o

    def fetch(out, off, rot, land, forward):
        o = (rot[0], rot[1], rot[1] + 128)
        s = 16 if forward else 112
        pe([(ap(o), T.zf[:, 128 - s:256 - s], T[land][:, 0:128], [(land, 0, 256), ("zf", 0, 256)], 512)], o)
        first = len(ops) - 1
        act(at(out, V1, off), o)
        for p in (0, 64):
            op("S", lambda p=p: S.activation(T[out][64 - p:128 - p, V4[0] + off:V4[1] + off], T[land][p:p + 64, 128:256], ACT.Copy),
               [(land, 0, 256)], [at(out, V4, off)], 128)
        return first

    def half6(c):
        return ("C6", c[0], c[1]) if c[0] < 512 else ("C7", c[0] - 512, c[1] - 512)

    def quarters(c):
        return [VIS, N1] if c == H1 else [Q1, Q0] if c == H0 else [c]

    dma("Y", T.ci[0:32, :], T.con[:], [], [("ci", 0, 512)], lat=3500.0)
    dma("S", T.ci[64:72, :], T.cur[:], [], [("ci", 512, 1024)], lat=3500.0)
    dma("Y", T.qb[:], T.q0[:], [], [full("qb")], lat=4000.0)
    dma("S", T.kh[:], T.kap[:], [], [full("kh")], lat=4500.0)
    dma("Y", T.qb2[:], T.q0[:], [], [full("qb2")], lat=5000.0)
    dma("S", T.vb[:], T.v0[:], [], [full("vb")], lat=5500.0)
    dma("Y", T.vb2[:], T.v0[:], [], [full("vb2")], lat=6000.0)
    dma("Y", T.ka[:, 0:NV], T.kap[:, 0:NV], [], [at("ka", NAT)], lat=6000.0)
    dma("Y", T.am[0:8, :], T.aim[:], [], [full("am")], lat=6000.0)
    in_turn(0, "Y"); in_turn(0, "S")
    fill(("bc", 0, 720), 0.0)
    fill(("cz", 0, 256), 1.0)
    fill(("bn", 0, 144), 0.0)
    fill(("big", 0, 16), 2048.0)
    for c, x in (((NEG, K1), -1.0), ((K1, M512), 1024.0), ((M512, FAR), -512.0), ((FAR, S16), -35840.0), ((S16, 896), 0.0625)):
        fill(at("cz", c), x)
    fill(("ones", 0, 2048), 1.0)
    fill(("cf", 0, 256), 1.0)
    fill(("cf", 256, 384), UNITS[0])
    fill(("cf", 384, 512), UNITS[1])
    fill(("cf", 512, 640), -1.0)
    fill(("top", 0, 64), 34816.0)
    ON = [("cz", 0, 256)]
    op("G", lambda: g.iota(T.pi[:, 0:1], [[0, 1]], 0, 1), [], [("pi", 0, 4)], 2)
    select(T.bc[:, 591:720:16], T.cz[:, 0:9], [[-1, 9]], ALU.is_equal, -64, 1, ON, [("bc", 576, 720)], 9)
    select(T.bc[:, 15:576:16], T.cz[:, 0:36], [[-4, 4], [-16, 9]], ALU.is_equal, 0, 4, ON, [("bc", 0, 576)], 36)
    select(T.bl[:], T.big[:, 0:8], [[-16, 8]], ALU.is_ge, 0, 1, [("big", 0, 16)], [("bl", 0, 8)], 8)
    select(T.bn[:, 15:143:16], T.bl[:], [[16, 8]], ALU.is_ge, 15, -1, [("bl", 0, 8)], [("bn", 0, 144)], 8)
    op("G", lambda: g.iota(T.iw0[:], [[16, 64]], 0, 1, allow_small_or_imprecise_dtypes=True), [], [("iw0", 0, 64)], 128)
    select(T.zz[:], T.cz[:], [[0, 7], [-1, 128]], ALU.is_equal, 0, 1, [("cz", 0, 896)], [("zz", 0, 896)], 896)
    select(T.wr[:], T.ones[:], [[-1, 16], [-16, 8], [0, 16]], ALU.is_equal, 0, 1, [("ones", 0, 2048)], [("wr", 0, 2048)], 2048)
    op("G", lambda: g.iota(T.ir[:], [[1, W]], 0, 0, allow_small_or_imprecise_dtypes=True), [], [full("ir")], 2 * W)
    send(at("kh", VIS), "lk", True)
    select(T.zf[:], T.cf[:], [[0, 5], [-1, 128]], ALU.is_equal, 0, 1, [("cf", 0, 640)], [("zf", 0, 640)], 640)
    select(T.wa[0:8, :], T.cz[0:8, 0:128], [[-1, 8], [0, 16]], ALU.is_equal, 0, 1, ON, [("wa", 0, 128)], 128)
    op("V", lambda: V.tensor_scalar(T.pj[:, 0:1], T.pi[:, 0:1], 112, None, ALU.bitwise_and), [("pi", 0, 4)], [("pj", 0, 4)], 1)
    op("V", lambda: V.tensor_copy(T.pf[:, 0:1], T.pj[:, 0:1]), [("pj", 0, 4)], [("pf", 0, 4)], 1)
    op("V", lambda: V.tensor_scalar(T.iw[:], T.iw0[:], T.pf[:, 0:1], None, ALU.subtract),
       [("iw0", 0, 64), ("pf", 0, 4)], [("iw", 0, 64)], 64)
    since = len(ops)
    op("V", lambda: V.tensor_copy(T.ch[0:32, :], T.ci[0:32, :]), [("ci", 0, 512)], [("ch", 0, 512)], W)
    op("V", lambda: V.tensor_copy(T.ch[64:72, :], T.ci[64:72, :]), [("ci", 512, 1024)], [("ch", 512, 1024)], W)
    rows = [("PY", 0, 64), ("PY", 512, 576), ("PB", 0, 64), ("PB", 512, 576), ("C7", 0, 64)]
    for m in (0, 1, 4, 2, 3):
        a, b, part = (64, 72, ("ch", 512, 1024)) if m == 4 else (0, 32, ("ch", 0, 512))
        pe([(ap(rows[m]), T.bc[a:b, 144 * m + 15 - l:144 * m + 143 - l], T.ch[a:b, l:W:16], [part, ("bc", 0, 720)], 64)
            for l in range(16)], rows[m])
    in_turn(since, "V"); in_turn(since, "P")
    for k, m in enumerate((1, 2, 3, 0, 1, 2, 3)):
        ts(("ee", 64 * k, 64 * k + 64), rows[4], float(m), ALU.is_equal)
    for m in range(4):
        for k in (0, 1):
            tt(("mm", 256 * k + 64 * m, 256 * k + 64 * m + 64), rows[m], ("ee", 64 * (3 - k + m), 64 * (4 - k + m)), ALU.mult)
    for k in (0, 1):
        y = ("C6", 256 + 64 * k, 320 + 64 * k)
        pe([times(y, ONE, ("mm", 256 * k + 64 * m, 256 * k + 64 * m + 64)) for m in range(4)], y)
    ts(("l1", 0, 128), ("C6", 256, 384), 1.0, ALU.mult)
    since = len(ops)
    act(full("kn"), full("kh"), ACT.Ln, more=1600)
    act(full("kn"), full("kn"), ACT.Exp, scale=-1.0, more=1800)
    for c in [H0] + ([] if (0, 1) in PE_STEPS else [H1]):
        act(at("PA", c), at("vb", c), scale=0.0625)
    act(("st1", 0, 128), ("C6", 256, 384))
    ops[-1]["r"].append(("l1", 0, 128))
    in_turn(since, "S")

    def later_rows():
        last = max(i for i, o in enumerate(ops) if o["e"] == "S")
        for m in range(4):
            act(("cc", 64 * m, 64 * m + 64), rows[m])
            ops[-1]["after"] = last

        def rest():
            last = dict((e, max(i for i, o in enumerate(ops) if o["e"] == e)) for e in "SP")
            act(("uu", 0, 512), at("PB", H0), ACT.Relu, bias=-1024.0)
            ops[-1]["after"] = last["S"]
            for k in (0, 1):
                y = ("PB", 512 + 64 * k, 576 + 64 * k)
                pe([times(y, ONE, ("uu", 256 * k + 64 * m, 256 * k + 64 * m + 64)) for m in range(4)], y)
                ops[-1]["after"] = last["P"]
            act(("st1", 128, 256), ("PB", 512, 640))
        last = len(ops) - 5
        for k in (2, 3):
            y = ("PB", 256 * (k - 2), 256 * (k - 1))
            pe([times(y, ONE, ("cc", 0, 256)), times(y, K1, ("ee", 64 * (3 - k), 64 * (3 - k) + 256))], y)
            ops[-1]["after"] = last
        return rest

    def row(t, k, n=1):
        p = 64 * ((k + 2 * (t - 1)) % 4)
        return ("st%d" % t, p, p + 64 * n)

    def advance(t, mu):
        z2, fl = ("C7", 64, 128), ("fl", 0, 64)
        pe([times(z2, FAR, ("f0", 0, 64))] + wrap(z2, full(mu)), z2)
        ops[-1]["after"] = max(i for i in range(len(ops) - 1) if ops[i]["e"] == "P")
        act(fl, z2, ACT.Sign, bias=-16384.0)
        n = 4 if t < 3 else 2
        new = row(t + 1, 0, 2) if n == 2 else ("st%d" % (t + 1), 0, 256)
        old = ("st%d" % t, new[1], new[2])
        y, z, u = ("C6", 256, 256 + 64 * n), ("C7", 128, 128 + 64 * n), ("uu", 0, 64 * n)

        def col(x, p):
            return (x[0], x[1] + 64 * p, x[1] + 64 * p + 64)
        before = [("st%d" % t, (old[1] + 64 * p - 64) % 256, (old[1] + 64 * p - 64) % 256 + 64) for p in range(n)]
        pe([times(y, NEG, old)] + [times(col(y, p), ONE, before[p]) for p in range(n)], y, True, False)
        pe([times(col(y, p), K1, fl) for p in range(n)], y, False, True)
        pe([times(z, ONE, old)] + [times(col(z, p), M512, fl) for p in range(n)], z, True, False)
        act(u, y, ACT.Relu)
        p = row(t + 1, 0)[1] - new[1]

        def relist():
            pe([times(z, ONE, u)], z, False, True)
            ts(("l%d" % (t + 1), 0, 128), ("C7", 128 + p, 256 + p), -512.0, ALU.add)
            act(new, z, ACT.Identity, bias=-512.0)
            ops[-1]["r"].append(("l%d" % (t + 1), 0, 128))
        return relist

    def decide(t):
        lst, jl = "l%d" % t, "j%d" % t
        q, q2 = ("qb", "qb2") if t == 1 else ("q", "q2")
        a, b = (H0, H1) if t == 3 or PE_SPEED else (H1, H0)

        def diff(w, c):
            gt(at("D", c, W * w), full(q), offs(lst, c, 64 * w), at(q2, c), ALU.subtract)

        def size(w, c):
            act(at("AB", c, W * w), at("D", c, W * w), ACT.Abs, scale=ABS_SCALE)

        def near(w, c, e):
            if e == "V":
                ts(at("NB", c, W * w), at("AB", c, W * w), NEAR, ALU.is_le, 0.5, ALU.subtract)
            else:
                act(at("NB", c, W * w), at("AB", c, W * w), ACT.Sign, scale=-1.0, bias=TIE)
        n0, d, zs, n1, f0, jf = ("C6", 0, 64), ("C6", 64, 128), ("C7", 64, 128), ("C7", 0, 64), ("f0", 0, 64), ("jf", 0, 64)
        pe([times(d, ONE, row(t, 1)), times(d, NEG, row(t, 0))], d)
        first = ([a] if t == 1 or not PE_SPEED else quarters(a)) + quarters(b)
        second = [a] + quarters(b) if SPLIT1 else [a, b]
        for c in first:
            diff(0, c)
        for n, c in enumerate([a] + quarters(b)):
            size(0, c); near(0, c, NEAR0[n])
        pe(wrap(n0, ("NB", 0, W)), n0)
        ts(f0, n0, 1024.0, ALU.is_lt)
        tt(d, d, f0, ALU.mult)
        tt(jf, d, row(t, 0), ALU.add)
        ts((jl, 0, 64), jf, 1.0, ALU.mult)
        for c in second:
            diff(1, c); size(1, c)
        for n, c in enumerate(second):
            near(1, c, NEAR1[n])
        pe([times(zs, ONE, ("iw", 0, 64)), times(zs, K1, f0)], zs)
        pe(wrap(n1, ("NB", W, 2 * W)) + [times(n1, ONE, ("top", 0, 64)), times(n1, FAR, f0)], n1)

    def publish(t):
        tt(("cw", 0, 64), ("C7", 0, 64), ("jf", 0, 64), ALU.min)
        ts(("j%d" % t, 64, 128), ("C7", 64, 128), 1.0, ALU.mult)
        for a, b in (H1, H0):
            for l in range(16):
                op("P", lambda a=a, b=b, l=l: P.matmul(T.PY[:, a + l:b:16], T.wr[:, 128 * l:128 * l + 128],
                                                       T.cw[:, a // 16:b // 16], True, True),
                   [("cw", 0, 64), ("wr", 0, 2048)], [("PY", a, b), ("sumPY", a // 512, a // 512 + 1)], 64)
            if a or R_COPY == "S":
                act(("R", a, b), ("PY", a, b))
            else:
                ts(("R", a, b), ("PY", a, b), 1.0, ALU.mult)

    def forward(shot, t, VP, X):
        again = shot == 1 and t == 1
        jl, kl, tp = "j%d" % t, "kl%d" % t, "tp%d" % t
        k = "kh" if t <= 2 else "ka"
        q, v, v2 = ("q", "v", "v2") if t > 1 else ("qb", "vs", "v2") if again else ("qb", "vb", "vb2")
        unit = 16.0 if v == "vb" else 1.0
        kj, mu = ("kj1", "mu1") if t == 1 else ("kj", "mu")

        def xx(c):
            return at("PY" if c in (VIS, Q1) and not again else X, c)

        def dv(c):
            gt(at("dv", c), full(v), offs(jl, c), at(v2, c), ALU.subtract)

        def pa(c, e):
            if again:
                pe([times(half6(c), ONE, at("sq1", c))], half6(c))
                tt(at("pa", c), half6(c), at("dv", c), ALU.mult)
            else:
                gt(at("pa", c), ("D", 0, 2 * W), offs(jl, c, 64), at("dv", c), ALU.mult)
            if e == "V":
                ts(at("sa", c), at("pa", c), 0.0, ALU.is_lt)
            else:
                act(at("sa", c), at("pa", c), ACT.Sign, scale=-1.0)

        def partner(c):
            gact(at(kj, c), full(k), offs(jl, c))

        def mutual(c):
            gt(at(mu, c), full("R"), offs(jl, c), at("ir", c), ALU.is_equal)

        def mask(c):
            early, late = (mu, "sa") if again else ("sa", mu)
            pe([times(xx(c), ONE, at(kj, c))], xx(c), True, False)
            pe([times(xx(c), ONE, at(early, c))], xx(c), False, False)
            pe([times(xx(c), ONE, at(late, c))], xx(c), False, True)
            act(xx(c), xx(c), ACT.Relu, scale=1.0 / unit, bias=-2.0 / unit)

        def push(parts):
            for c in parts:
                tt(xx(c), xx(c), at(k, c), ALU.mult)
            for c in parts:
                tt(at(tp, c), xx(c), at("dv", c), ALU.mult)
            on_pe = PE_SPEED and parts == [VIS, N1]
            if on_pe:
                pe([times(at(VP, H1), S16, at(v, H1)) if v == "vb" else exact(at(VP, H1), at(v, H1))], at(VP, H1), True, False)
            for c in parts:
                if on_pe:
                    pe([exact(at(VP, c), at(tp, c))], at(VP, c), False, c == N1)
                elif PE_Q1 and c == Q1 and t != 2:
                    pe([times(at(VP, c), S16, at(v, c)) if v == "vb" else exact(at(VP, c), at(v, c))], at(VP, c), True, False)
                    pe([exact(at(VP, c), at(tp, c))], at(VP, c), False, True)
                else:
                    tt(at(VP, c), at(VP, c), at(tp, c), ALU.add)
            if not on_pe:
                move(parts)

        def move(parts):
            for c in parts:
                tt(at("q", c), at(VP, c), at(q, c), ALU.add)

        def copies(c):
            for x in (quarters(c) if PE_SPEED and c == H0 else [c]) if t < 4 else []:
                twin("S", at("q2", x), at("q", x))

        def keep(parts, c):
            for x in parts:
                act(at(kl, x), xx(x), scale=unit)
                ops[-1]["r"].append(at(tp, x))
            if t < 4:
                act(at("v", c), at(VP, c))
                ops[-1]["r"].append(at("q", c))
                twin("G", at("v2", c), at("v", c))

        def both():
            push(quarters(H1))
            if not PE_SPEED:
                copies(H1)
            if t < 4 and not again:
                advance(t, mu)
            push(quarters(H0)); copies(H0)
            if PE_SPEED:
                move(quarters(H1)); copies(H1)
        a, b = H1, H0
        if again:
            def product(c):
                tt(at("ge", c), at("PY", c), at("tp1", c), ALU.mult)
            since = len(ops)
            dv(a); product(VIS); pa(VIS, "S"); pa(N1, "S"); mask(VIS); mask(N1); dv(b); product(N1)
            pa(Q1, "S"); pa(Q0, "S"); mask(Q1); mask(Q0); product(Q1); product(Q0)
            in_turn(since)
            add_g("ge", ALL)
            both(); keep([a], a); keep([b], b)
            return
        if t == 2:
            send(at("q", VIS), "lq%d" % shot, True)
        decide(t)
        publish(t); dv(a); partner(a); dv(b); pa(a, "S"); partner(b)
        if t == 1:
            later_rows()
            for c in (b,) if PE_SPEED else (a, b):
                act(at(VP, c), at("vb", c), scale=0.0625)
        mutual(VIS); mask(VIS); mutual(N1); mask(N1); pa(b, SIGN_B)
        if t == 2:
            rot = ("C6", 256, 512)
            tt(xx(VIS), xx(VIS), at(k, VIS), ALU.mult)
            tt(at(tp, VIS), xx(VIS), at("dv", VIS), ALU.mult)
            tt(("vo", 0, 256), at(VP, VIS), at(tp, VIS), ALU.add)
            send(("vo", 0, 256), "lv%d" % shot, True)
            mutual(b); mask(Q1); mask(Q0)
            advance(t, mu)
            push([N1, Q1, Q0]); copies(N1); copies(b)
            rot = at("PY", VIS)
            act(at(kl, VIS), xx(VIS))
            turn(rot, "lq%d" % shot, True)
            act(("qov", 0, 256), rot)
            turn(rot, "lv%d" % shot, True)
            tt(at("q", VIS), rot, ("qov", 0, 256), ALU.add)
            act(at("q2", VIS), at("q", VIS))
            keep([N1], N1); keep([Q1, Q0], b)
            act(at("v", VIS), rot)
            twin("G", at("v2", VIS), at("v", VIS))
            if not PE_SPEED:
                act(at(VP, VIS), at("v", VIS))
            return
        mutual(b); mask(Q1); mask(Q0)
        both(); keep([VIS, N1], a); keep([Q1, Q0], b)
        if t == 1:
            for c in (a, b):
                gact(at("sq1", c), ("D", 0, 2 * W), offs(jl, c, 64), ACT.Sign)
                ops[-1]["r"].append(xx(Q0))
            turn(at("PY", VIS), "lk", True, z="zz")
            act(at("ka", VIS), at("PY", VIS))

    def forward(shot, t, VP, X):
        again = shot == 1 and t == 1
        lst, jl, kl, tp = "l%d" % t, "j%d" % t, "kl%d" % t, "tp%d" % t
        k = "kh" if t <= 2 else "ka"
        q, q2 = ("qb", "qb2") if t == 1 else ("q", "q2")
        v, v2 = ("v", "v2") if t > 1 else ("vs", "v2") if again else ("vb", "vb2")
        unit = 16.0 if v == "vb" else 1.0
        kj, mu = ("kj1", "mu1") if t == 1 else ("kj", "mu")
        n0, d, zs, n1, f0, jf = ("C6", 0, 64), ("C6", 64, 128), ("C7", 64, 128), ("C7", 0, 64), ("f0", 0, 64), ("jf", 0, 64)
        D = "D1" if t == 1 else "D"

        def diff(w, c):
            gt(at(D, c, W * w), full(q), offs(lst, c, 64 * w), at(q2, c), ALU.subtract)
            act(at("AB", c, W * w), at(D, c, W * w), ACT.Abs, scale=ABS_SCALE)

        def near(w, c, e="V"):
            if e == "V":
                ts(at("NB", c, W * w), at("AB", c, W * w), NEAR, ALU.is_le, 0.5, ALU.subtract)
            else:
                act(at("NB", c, W * w), at("AB", c, W * w), ACT.Sign, scale=-1.0, bias=TIE)

        def publish(e):
            tt(("cw", 0, 64), n1, jf, ALU.min)
            ts((jl, 64, 128), zs, 1.0, ALU.mult)
            for c in (H1, H0):
                for x in range(c[0], c[1], 64):
                    pe([(T.PY[:, x:x + 64], T.wr[:, 2 * x:2 * x + 128], T.cw[:], [("cw", 0, 64), ("wr", 0, 2048)], 64)],
                       ("PY", x, x + 64))
                told[:] = [len(ops) - 1]
                if c == H1 or e == "S":
                    act(at("R", c), at("PY", c))

        def behind():
            rest = [i for i in range(told[0] + 1, len(ops)) if ops[i]["e"] == "P"]
            masks = [i for i in rest if ops[i].get("mask")]
            turns = [told[0], rest[0]] + [masks[n] for n in (0, 3, 6, 9, 1, 4, 2, 5, 7, 10, 8, 11)]
            if t == 2:
                turns = [told[0], rest[0]] + [masks[n] for n in (0, 3, 1, 2, 4, 5, 6, 9, 7, 8, 10, 11)]
            for a, b in zip(turns, turns[1:]):
                ops[b]["after"] = a
            for i in rest:
                if ops[i].get("after") is None:
                    ops[i]["after"] = rest[0]

        def column():
            zp, hb = ("C6", 128, 192), ("hb", 0, 64)
            pe([times(zp, K1, hb), times(zp, NEG, hb), times(zp, ONE, ("j64", 0, 64))], zp)
            return lambda: ts(("jr", 0, 64), zp, 1023.0 * 160.0, ALU.add)

        def xx(c):
            return at("PY" if c in (VIS, Q1) else X, c)

        def dv(c):
            gt(at("dv", c), full(v), offs(jl, c), at(v2, c), ALU.subtract)

        def pa(c):
            if again:
                pe([times(half6(c), ONE, at("sq1", c))], half6(c))
                ops[-1]["after"] = max(i for i in range(since) if ops[i]["e"] == "P")
                tt(at("pa", c), half6(c), at("dv", c), ALU.mult)
            else:
                gt(at("pa", c), (D, 0, 2 * W), offs(jl, c, 64), at("dv", c), ALU.mult)
            act(at("sa", c), at("pa", c), ACT.Sign, scale=-1.0)

        def partner(c):
            gact(at(kj, c), full(k), offs(jl, c))

        def mutual(c):
            gt(at(mu, c), full("R"), offs("jr", c), at("ir", c), ALU.is_equal)

        def mask(c):
            early, late = (mu, "sa") if again else ("sa", mu)
            pe([times(xx(c), ONE, at(kj, c))], xx(c), True, False)
            pe([times(xx(c), ONE, at(early, c))], xx(c), False, False)
            pe([times(xx(c), ONE, at(late, c))], xx(c), False, True)
            for o in ops[-3:]:
                o["mask"] = True
            act(xx(c), xx(c), ACT.Relu, scale=1.0 / unit, bias=-2.0 / unit)

        def kk(*parts):
            for c in parts:
                tt(xx(c), xx(c), at(k, c), ALU.mult)

        def push(*parts):
            for c in parts:
                tt(at(tp, c), xx(c), at("dv", c), ALU.mult)

        def speed(*parts):
            for c in parts:
                tt(at(VP, c), at(VP, c), at(tp, c), ALU.add)

        def speed_pe(c):
            pe([times(at(VP, c), S16, at(v, c)) if v == "vb" else exact(at(VP, c), at(v, c))], at(VP, c), True, False)
            for x in quarters(c):
                pe([exact(at(VP, x), at(tp, x))], at(VP, x), False, x == quarters(c)[-1])

        def move(*parts):
            for c in parts:
                tt(at("q" if t < 4 else VP, c), at(VP, c), at(q, c), ALU.add)

        def copies(*parts):
            for c in parts if t < 4 else []:
                twin("G" if c == Q0 and Q0_G else "S", at("q2", c), at("q", c))

        def keep(parts, c):
            for x in parts:
                act(at(kl, x), xx(x), scale=unit)
                ops[-1]["r"].append(at(tp, x))
            if t < 4:
                act(at("v", c), at(VP, c))
                ops[-1]["r"].append(at("q", c))
                twin("G", at("v2", c), at("v", c))

        def finish():
            first = len(ops)
            relist = advance(t, mu) if t < 4 and not again else None
            kk(VIS, N1); push(VIS, N1)
            if (shot, t) in PE_STEPS:
                for x in quarters(ON_PE):
                    pe([exact(at(VP, x), at(tp, x))], at(VP, x), False, x == quarters(ON_PE)[-1])
                if relist:
                    mine = [i for i in range(first, len(ops)) if ops[i]["e"] == "P"]
                    turns = [mine[0], mine[4], mine[2]] + mine[5:] + [mine[3]]
                    for a, b in zip(turns, turns[1:]):
                        ops[b]["after"] = a
                kk(Q1, Q0); push(Q1, Q0); speed(Q1, Q0); move(Q1, Q0); copies(Q1, Q0)
                if ON_PE == VIS:
                    speed(N1)
                move(VIS, N1); copies(H1)
                if relist:
                    relist()
            else:
                speed(VIS, N1); move(VIS, N1); copies(H1); kk(Q1, Q0); push(Q1, Q0)
                if relist:
                    relist()
                speed(Q1, Q0); move(Q1, Q0); copies(H0)

        def preload(c):
            pe([times(at(VP, c), S16, at(v, c)) if v == "vb" else exact(at(VP, c), at(v, c))], at(VP, c), True, False)
        since, told = len(ops), []
        if (shot, t) in PE_STEPS:
            can_wait(preload, ON_PE)
            if t == 1 and ON_PE == VIS:
                can_wait(act, at(VP, N1), at(v, N1), scale=1.0 / unit)
        if again:
            def product(c):
                tt(at("ge", c), at("PY", c), at("tp1", c), ALU.mult)
            dv(H1); product(VIS); pa(VIS); pa(N1); mask(VIS); mask(N1); dv(H0); product(Q1)
            pa(Q1); pa(Q0); mask(Q1); mask(Q0); product(Q0); product(N1)
            add_g("ge", ALL)
            finish(); keep([VIS, N1], H1); keep([Q1, Q0], H0)
            in_turn(since)
            return
        if t == 2:
            send(at("q", VIS), "lq%d" % shot, True)
        a, b1, b2 = (H0, N1, VIS) if t == 3 or (shot, t - 1) in PE_STEPS else (H1, Q1, Q0)
        a1, a2 = quarters(a)
        pe([times(d, ONE, row(t, 1)), times(d, NEG, row(t, 0))], d)
        if (shot, t - 1) in PE_STEPS:
            diff(0, Q1); diff(0, Q0)
        else:
            diff(0, a)
        diff(0, b1); diff(0, b2); diff(1, a1); near(0, a); near(0, b1); near(0, b2)
        pe(wrap(n0, ("NB", 0, W)), n0)
        if (shot, t) in PE_STEPS:
            ops[-1]["after"] = since
        if t == 1:
            rest = later_rows()
        diff(1, a2); diff(1, b1); diff(1, b2)
        ts(f0, n0, 1024.0, ALU.is_lt)
        pe([times(zs, ONE, ("iw", 0, 64)), times(zs, K1, f0)], zs)
        near(1, a)
        tt(d, d, f0, ALU.mult)
        near(1, b1)
        tt(jf, d, row(t, 0), ALU.add)
        near(1, b2)
        ts((jl, 0, 64), jf, 1.0, ALU.mult)
        ts(("hb", 0, 64), jf, -1.0 / 16.0, ALU.mult, 15.0 / 32.0 - 160.0, ALU.add)
        ts(("j64", 0, 64), jf, 64.0, ALU.mult)
        pe([times(n1, ONE, ("top", 0, 64)), times(n1, FAR, f0)], n1, True, False)
        pe(wrap(n1, ("NB", W, 2 * W)), n1, False, True)
        if t == 1:
            rest()
        if t == 2:
            rot = at("PY", VIS)
            dv(VIS); partner(H1); publish("V"); jr = column(); dv(N1); pa(VIS)
            ts(at("R", H0), at("PY", H0), 1.0, ALU.mult)
            pa(N1); jr(); can_wait(partner, H0)
            mutual(VIS); mask(VIS); mutual(N1); mask(N1); dv(H0); kk(VIS); kk(N1); push(VIS); push(N1)
            leave("vo", VP, tp)
            send(("vo", 0, 256), "lv%d" % shot, True)
            ops[-2]["r"].append(("voh", 0, 128))
            pa(H0); mutual(Q1); mask(Q1); mutual(Q0); mask(Q0)
            masked = len(ops) + 3
            relist = advance(t, mu)
            speed(N1); move(N1); kk(Q1, Q0); push(Q1, Q0); speed(Q1, Q0); move(Q1, Q0); relist()
            copies(N1, Q1, Q0)
            act(at(kl, VIS), xx(VIS))
            ops[fetch("qov", -NV, rot, "lq%d" % shot, True)]["after"] = masked
            turned = arrive("q", rot, "lv%d" % shot, True, "qov", -NV)
            came = len(ops) - 3
            act(at("q2", VIS), at("q", VIS))
            keep([N1], N1); keep([Q1, Q0], H0)
            act(at("v", V1), turned)
            act(at("v", V4), ("lv%d" % shot, 128, 256))
            twin("G", at("v2", VIS), at("v", VIS))
            if (shot, 3) not in PE_STEPS:
                act(at(VP, VIS), at("v", VIS))
            in_turn(since); behind()
            for c in (H0, H1) if shot == 0 else ():
                pe([(ap(at(X, c)), T.wa[0:8, :], T.am[0:8, c[0]:c[1]], [("wa", 0, 128), full("am")], 512)], at(X, c))
                ops[-1]["after"] = came
                act(at("amr", c), at(X, c))
            return
        dv(H1); partner(H1); publish("S"); jr = column(); dv(H0); pa(H1); can_wait(partner, H0)
        if not EARLY_MU:
            jr(); pa(H0)
        mutual(VIS); mask(VIS); mutual(N1); mask(N1)
        if EARLY_MU:
            pa(H0)
        if MU_Q:
            mutual(Q1); mask(Q1); mutual(Q0); mask(Q0)
        else:
            mutual(H0); mask(Q1); mask(Q0)
        finish(); keep([VIS, N1], H1); keep([Q1, Q0], H0)
        in_turn(since); behind()
        if t == 1:
            turn(at("PY", VIS), "lk", True, z="zz")
            act(at("ka", VIS), at("PY", VIS))

    def add_g(src, c, off=0):
        dma("G", ap(at("G", c)), ap(at(src, c, off)), [at(src, c, off), at("G", c)], [at("G", c)], add=True, lat=3500.0)

    def backward(shot, VP, X):
        rot = ("C7", 256, 512)
        for c in (H1, H0):
            for x in quarters(c):
                tt(at("A", x), at(VP, x), at("amr", x), ALU.subtract)
        send(at("A", VIS), "la%d" % shot, False)
        wins = {4: "A", 3: "av1", 2: "av2", 1: "av1"}
        unit = UNITS[shot]

        def da(t):
            return X if t % 2 == 0 else "PY"

        def av(t, c):
            return ("C7" if t % 2 else "C6", 0, 256) if c == Q1 and t in Q1_PE else at(VP, c)

        def pull(t, c, fine=False):
            kept = c == H0 and t > 1 and t + 1 in Q1_PE
            act(at(VP, Q0 if kept else c), at(wins[t], Q0 if kept else c), scale=unit if t == 1 else 1.0)
            for x in (quarters(c) if fine or FINE else [c]):
                gact(at("ag", x), full(wins[t]), offs("j%d" % t, x), scale=unit if t == 1 else 1.0)
            for x in quarters(c):
                tt(at(da(t), x), at("ag", x), av(t + 1, x) if kept else at(VP, x), ALU.subtract)
            for x in quarters(c):
                tt(at("tb", x), at(da(t), x), at("kl%d" % t, x), ALU.mult)

        def add(t, c):
            for x in quarters(c):
                if x == Q1 and t in Q1_PE:
                    pe([exact(av(t, x), at(wins[t], x), 256 + 128 * shot if t == 1 else 0)], av(t, x), True, False)
                    pe([exact(av(t, x), at("tb", x))], av(t, x), False, t == 1)
                else:
                    tt(at(VP, x), at(VP, x), at("tb", x), ALU.add)

        def drift(t, c):
            for x in quarters(c):
                if x == Q1 and t in Q1_PE:
                    pe([exact(av(t, x), at("A", x))], av(t, x), False, True)
                    act(at(wins[t - 1], x), av(t, x))
                else:
                    tt(at(wins[t - 1], x), av(t, x), at("A", x), ALU.add)

        def gain(t, c):
            out = {4: at("gg", c), 3: at("gg", c, 256 if c == VIS else 1280), 2: at("gb", c), 1: at("ge", c)}[t]
            tt(out, at(da(t), c), at("tp%d" % t, c), ALU.mult)
        def aside(out, src, fn=ACT.Copy, scale=1.0):
            last = max(i for i, o in enumerate(ops) if o["w"] and o["w"][0][0] == "ag")
            for x in (VIS, N1, Q1, Q0):
                act(at(out, x), at(src, x), fn, scale=scale)
                ops[-1]["after"] = last
        def step(t, order, late):
            scale, since = unit if t == 1 else 1.0, len(ops)

            def load(x):
                if not (x == Q1 and t > 1 and t + 1 in Q1_PE):
                    act(at(VP, x), at(wins[t], x), scale=scale)
            for x in order:
                if x not in late:
                    load(x)
            since = len(ops)
            for x in order:
                if x in late:
                    load(x)
                if x == order[0] and (t, shot) in V_GATHERS:
                    o, w, of = at("ag", x), full(wins[t]), offs("j%d" % t, x)
                    op("V", lambda o=o, w=w, of=of: V.tensor_scalar(ap(o), ap(w).indirect(ap(of)), scale, None, ALU.mult),
                       [w, of], [o], 256 * GATHER + 55)
                else:
                    gact(at("ag", x), full(wins[t]), offs("j%d" % t, x), scale=scale)
            in_turn(since, "S")
            for pair in (order[:2], order[2:]):
                for x in pair:
                    tt(at(da(t), x), at("ag", x), av(t + 1, x) if t > 1 else at(VP, x), ALU.subtract)
                for x in pair:
                    tt(at("tb", x), at(da(t), x), at("kl%d" % t, x), ALU.mult)
                for x in pair:
                    if (t, x) == (3, VIS):
                        leave("ao", VP, "tb")
                        send(("ao", 0, 256), "lw%d" % shot, False)
                        ops[-2]["r"].append(("aoh", 0, 128))
                        fetch("A", 0, rot, "la%d" % shot, False)
                    else:
                        add(t, x)
                for x in pair:
                    if t > 1 and (t, x) != (3, VIS):
                        drift(t, x)
            if CHAIN:
                in_turn(since)
        step(4, (VIS, N1, Q1, Q0), (Q1, Q0))
        if shot == 0:
            can_wait(newton)
            aside("G", "kh", ACT.Square)
            aside("G", "G", scale=-1.0)
        else:
            turn(rot, "lg0", False, pieces=2)
            act(("gr", 0, 256), rot)
            add_g("gr", VIS, -NV)
            aside("rk", "kn", scale=-2.0)
            dma("G", T.rk[:], T.ou[:], [full("ou"), full("rk")], [full("rk")], add=True, lat=3500.0)
            aside("ov", "vs", scale=16.0)
        step(3, (VIS, N1, Q1, Q0), (Q1, Q0))
        last = max(i for i, o in enumerate(ops) if o["w"] and o["w"][0][0] == "ag")
        for c in (VIS, N1, Q1, Q0) if shot == 0 else ():
            gact(at("sq1", c), ("D1", 0, 2 * W), offs("j1", c, 64), ACT.Sign)
            ops[-1]["after"] = last
        arrive("av2", rot, "lw%d" % shot, False, "A", 0)
        gain(4, VIS); gain(3, VIS)
        send(("gg", NV, NV + 512), "lg%d" % shot, False)
        for c in (N1, Q1, Q0):
            gain(4, c)
        for c in (N1, Q1, Q0):
            gain(3, c)
        add_g("gg", NAT, 1280)
        add_g("gg", NAT)
        step(2, (Q1, Q0, N1, VIS), (VIS,))
        for c in (VIS, N1, Q1, Q0):
            gain(2, c)
        if shot == 0:
            add_g("gb", ALL)
        else:
            if TAIL_PE:
                pe([exact(half6(H0), at("G", H0))], half6(H0), True, False)
                pe([exact(half6(H0), at("gb", H0))], half6(H0), False, False)
            else:
                add_g("gb", H0)
            turn(rot, "lg1", False, pieces=2)
            tt(at("gb", VIS), rot, at("gb", VIS), ALU.add)
            add_g("gb", H1)
        aside("tp1", "tp1", scale=1.0 / unit)
        if shot == 0:
            aside("vs", "vb", scale=0.0625)
        v0 = "ov" if shot else "vs"

        def settle(c, on_pe):
            if on_pe:
                pe([exact(at(VP, c), at(v0, c))], at(VP, c), True, False)
            for x in quarters(c):
                ts(at("cl", x) if on_pe else av(1, x), av(1, x), CLIP * unit, ALU.min, -CLIP * unit, ALU.max)
            for x in quarters(c):
                if on_pe:
                    pe([exact(at(VP, x), at("cl", x), 512)], at(VP, x), False, x == quarters(c)[-1])
                else:
                    tt(at(v0, x), at(v0, x), av(1, x), ALU.subtract)
            if on_pe:
                act(at(v0, c), at(VP, c))
            if shot == 0:
                act(at("v2", c), at(VP if on_pe else "vs", c))
            else:
                dma("Y", T.yv[:, c[0]:c[1]], ap(at("ov", c)), [at("ov", c)], [])

        def result(c, e):
            for src, alu in (("tp1", ALU.mult), ("G", ALU.add)):
                for x in quarters(c):
                    tt(at("PY", x), at("PY", x), at(src, x), alu)
            for x in quarters(c):
                tt(at("ou", x), at("PY", x), at("rk", x), ALU.mult)
            dma(e, T.yg[:, c[0]:c[1]], ap(at("ou", c)), [at("ou", c)], [])
        if shot == 0:
            step(1, (Q1, Q0, N1, VIS), (N1, VIS)); settle(H0, False); settle(H1, False)
            for c in [H0] + ([] if (1, 1) in PE_STEPS else [H1]):
                act(at(VP, c), at("vs", c))
        else:
            step(1, (Q1, Q0, N1, VIS), (N1, VIS))
            if TAIL_PE:
                for x in (Q1, Q0):
                    gain(1, x)
                pe([exact(half6(H0), at("ge", H0))], half6(H0), False, True)
            settle(H0, False); settle(H1, False)
            result(H1, "S")
            if TAIL_PE:
                for x in (Q1, Q0):
                    tt(at("ou", x), half6(x), at("rk", x), ALU.mult)
                dma("Y", T.yg[:, 0:512], ap(at("ou", H0)), [at("ou", H0)], [])
            else:
                result(H0, "Y")

    def newton():
        for c in (H1, H0):
            act(at("PY", c), at("kn", c), ACT.Square)
            for x in quarters(c):
                tt(at("ou", x), at("PY", x), at("kh", x), ALU.mult)

    for shot in (0, 1):
        for t in (1, 2, 3, 4):
            forward(shot, t, "PA", "PB")
        backward(shot, "PA", "PB")
    for o in ops:
        name = o["w"][0][0].rstrip("01234") if o["w"] else ""
        if (o["e"] == "S" and name in ("kl", "v", "sq", "ka", "st", "cc", "qov", "G", "vs", "ov", "rk", "tp", "gr", "A")
                or o["e"] == "V" and name in ("gg", "gb") or o["e"] == "G" and name in ("v", "G", "rk")):
            o["lazy"] = True
    if not ORDER:
        ORDER.extend(arrange(ops))
    emit([ops[i] for i in ORDER], g, T)
